import numpy as np
import ml_dtypes


def mxq(x, axis, fmt="e4m3"):
    dtype, down = {"e4m3": (ml_dtypes.float8_e4m3fn, 7), "e5m2": (ml_dtypes.float8_e5m2, 14)}[fmt]
    v = np.moveaxis(np.asarray(x, np.float32).astype(ml_dtypes.bfloat16).astype(np.float64), axis, -1)
    blocks = v.reshape(v.shape[:-1] + (-1, 32))
    amax = np.abs(blocks).max(-1, keepdims=True)
    byte = np.maximum(np.where(amax > 0, np.frexp(amax)[1] - 1 + 127, 0) - down, 1)
    scale = np.exp2(byte - 127.0)
    codes = (blocks / scale).astype(np.float32).astype(dtype).astype(np.float64)
    return np.moveaxis((codes * scale).reshape(v.shape), -1, axis)


WIDE = False


def mx_kscale(k):
    if not WIDE:
        return np.ones(k)
    levels = np.array([10, -10, 5, -5, 0])
    if k % 512:
        return np.exp2(np.random.permutation(np.resize(levels, k // 32))).repeat(32)
    a = np.empty((k // 512, 16))
    for p in range(k // 512):
        a[p, :8] = np.random.permutation(np.resize(levels, 8))
        for g in range(8):
            far = levels[np.abs(levels - a[p, g]) >= 10]
            a[p, g + 8] = far[np.random.randint(len(far))]
    return np.exp2(a.ravel()).repeat(32)


def f64(x):
    return np.asarray(x).astype(np.float64)


def striped(idx):
    return np.tile(idx.reshape(-1, 16).T, (8, 1)).astype(np.uint16)


def unstriped(offs):
    return offs[:16].T.reshape(-1).astype(np.int64)


E2M1 = np.array([0.0, 0.5, 1.0, 1.5, 2.0, 3.0, 4.0, 6.0, -0.0, -0.5, -1.0, -1.5, -2.0, -3.0, -4.0, -6.0])


def pack_weight(w, fmt):
    k, n = w.shape
    w = f64(np.asarray(w, np.float32).astype(ml_dtypes.bfloat16)).reshape(k // 32, 32, n)
    amax = np.abs(w).max(1)
    if fmt == "e4m3":
        byte = np.frexp(amax)[1] - 1 + 127 - 7
    else:
        mant, ex = np.frexp(amax / 6.0)
        byte = np.where(mant > 0.5, ex, ex - 1) + 127
    byte = np.clip(np.where(amax > 0, byte, 1), 1, 254)
    scaled = (w * np.exp2(127.0 - byte)[:, None, :]).reshape(k, n).astype(np.float32)
    by_word = np.ascontiguousarray(scaled.reshape(k // 512, 128, 4, n).transpose(0, 1, 3, 2))
    if fmt == "e4m3":
        words = by_word.astype(ml_dtypes.float8_e4m3fn).view(np.uint8)
    else:
        c = by_word.astype(ml_dtypes.float4_e2m1fn).view(np.uint8) & 0xF
        words = (c[..., 0::2] | (c[..., 1::2] << 4)).reshape(k // 512, 128, 2 * n)
    return np.ascontiguousarray(words), np.ascontiguousarray(byte.astype(np.uint8).reshape(k // 512, 16, n))


def unpack_weight(words, scales, fmt):
    g, _, n = scales.shape
    words = np.ascontiguousarray(words).reshape(g, 128, n, -1)
    if fmt == "e4m3":
        vals = words.view(ml_dtypes.float8_e4m3fn).astype(np.float64)
    else:
        nib = np.empty((g, 128, n, 4), np.uint8)
        nib[..., 0::2] = words & 0xF
        nib[..., 1::2] = words >> 4
        vals = E2M1[nib]
    vals = vals * np.repeat(np.exp2(scales.astype(np.float64) - 127.0), 8, axis=1)[..., None]
    return vals.transpose(0, 1, 3, 2).reshape(g * 512, n)


def gelu(v):
    return 0.5 * v * (1.0 + np.tanh(np.sqrt(2.0 / np.pi) * (v + 0.044715 * v**3)))


K, H, N, T, S = 1024, 1024, 512, 2048, 1024

def setup_inputs():
    n = np.random.standard_normal
    s = mx_kscale(K)[:, None]
    u = mx_kscale(H)[:, None]
    tab_words, tab_scales = pack_weight(n((K, T)) * s, "e4m3")
    wh = (n((K, H)) / np.sqrt(K) / s).astype(np.float32)
    wa_words, wa_scales = pack_weight(n((K, H)) / np.sqrt(K) / s, "e2m1")
    wo_words, wo_scales = pack_weight(n((H, N)) / np.sqrt(H) / u, "e4m3")
    return {
        "tab_words": tab_words, "tab_scales": tab_scales,
        "offs": striped(np.random.permutation(T)[:S]),
        "gT": n((N, T)).astype(np.float32),
        "wh": wh,
        "wa_words": wa_words, "wa_scales": wa_scales,
        "lead": (0.5 * n(H)).astype(np.float32),
        "gain": (np.exp(0.3 * n(H)) * u[:, 0]).astype(np.float32),
        "wo_words": wo_words, "wo_scales": wo_scales,
        "bo": (1.0 + 0.3 * n(N)).astype(np.float32),
    }

def reference(tab_words, tab_scales, offs, gT, wh, wa_words, wa_scales, lead, gain, wo_words, wo_scales, bo):
    v = unpack_weight(tab_words, tab_scales, "e4m3")[:, unstriped(offs)]
    home = mxq(f64(wh), 0, "e4m3").T @ v
    away = unpack_weight(wa_words, wa_scales, "e2m1").T @ v
    d = away - home + f64(lead)[:, None]
    h = f64(gain)[:, None] * (1.0 / (1.0 + np.exp(-d)))
    y = unpack_weight(wo_words, wo_scales, "e4m3").T @ mxq(h, 0, "e4m3")
    g = f64(gT)[:, unstriped(offs)]
    new = g * (y + f64(bo)[:, None])
    out = f64(gT).copy()
    out[:, unstriped(offs)] = new
    return out

@@ -1,0 +1,268 @@
+from contextlib import ExitStack
+
+import concourse.mybir as mybir
+
+K, H, N, T, S = 1024, 1024, 512, 2048, 1024
+FLOPS = 2 * S * (2 * K * H + H * N)
+
+F32 = mybir.dt.float32
+BF16 = mybir.dt.bfloat16
+I32 = mybir.dt.int32
+U32 = mybir.dt.uint32
+U16 = mybir.dt.uint16
+U8 = mybir.dt.uint8
+FP8X4 = mybir.dt.float8_e4m3fn_x4
+FP4X4 = mybir.dt.float4_e2m1fn_x4
+ACT = mybir.ActivationFunctionType
+MULT = mybir.AluOpType.mult
+
+P = 128
+PACK = 4
+PASS = P * PACK
+PASSES = 2
+LIST_ROWS = 16
+HALF = 512
+CHUNK = 256
+CHUNKS = S // CHUNK
+TILES = N // P
+FP4_NARROW = 128
+
+
+def tile_list_pitch_control_rescale_kernel(
+    tc, tab_words, tab_scales, offs, gT, wh, wa_words, wa_scales, lead, gain, wo_words, wo_scales, bo, out
+):
+    nc = tc.nc
+    with ExitStack() as ctx:
+        keep = ctx.enter_context(tc.tile_pool(name="keep", bufs=1))
+        shared = ctx.enter_context(tc.tile_pool(name="shared", bufs=1))
+        ring = ctx.enter_context(tc.tile_pool(name="ring", bufs=2))
+        psum_d = ctx.enter_context(tc.psum_pool(name="psum_d", bufs=5))
+        psum_y = ctx.enter_context(tc.psum_pool(name="psum_y", bufs=3))
+
+        def held(shape, dtype, name):
+            return keep.tile(shape, dtype, name=name, align_bytes=64)
+
+        offsets = keep.tile([P, S // LIST_ROWS], U16, name="offsets")
+        nc.sync.dma_start(offsets[:], offs)
+
+        def entries(first, count):
+            return offsets[:, first // LIST_ROWS : (first + count) // LIST_ROWS]
+
+        def load_planes(scales, width, name, queue):
+            planes = held([P, PASSES * width], U8, name)
+            nc.vector.memset(planes[:].bitcast(I32), 0)
+            for q in range(4):
+                queue.dma_start(
+                    planes[32 * q : 32 * q + 4, :].bitcast(I32).rearrange("r (a w) -> r a w", a=PASSES),
+                    scales[:, 4 * q : 4 * q + 4, :].bitcast(I32).rearrange("a r w -> r a w"),
+                )
+            return planes
+
+        warm = held([P, 2], F32, "warm")
+        nc.vector.memset(warm[:, 0:1], 0.0)
+        nc.scalar.activation(warm[:, 1:2], warm[:, 0:1], ACT.Sigmoid)
+
+        tab_planes = load_planes(tab_scales, T, "tab_planes", nc.scalar)
+        wa_planes_raw = load_planes(wa_scales, H, "wa_planes_raw", nc.scalar)
+        lead_sb = held([P, PASSES, PACK], F32, "lead_sb")
+        gain_sb = held([P, PASSES, PACK], F32, "gain_sb")
+        bo_sb = held([P, TILES], F32, "bo_sb")
+
+        nc.sync.dma_start(lead_sb[:], lead.rearrange("(b p t) -> p b t", b=PASSES, t=PACK))
+        nc.sync.dma_start(gain_sb[:], gain.rearrange("(b p t) -> p b t", b=PASSES, t=PACK))
+        with nc.allow_non_contiguous_dma("one bias value for each partition"):
+            nc.sync.dma_start(bo_sb[:], bo.rearrange("(u p) -> p u", p=P))
+        wa_raw = held([P, PASSES * 2 * H], U8, "wa_raw")
+        nc.sync.dma_start(
+            wa_raw[:].bitcast(I32).rearrange("p (a w) -> p a w", a=PASSES),
+            wa_words.bitcast(I32).rearrange("a p w -> p a w"),
+        )
+        tab_sb = [held([P, T], U32, f"tab_sb{a}") for a in range(PASSES)]
+        wh_raw = {(b, a): held([P, PACK, PASS], F32, f"wh_raw{b}{a}") for b in range(PASSES) for a in range(PASSES)}
+
+        def load_tab(a):
+            nc.sync.dma_start(tab_sb[a][:].bitcast(I32), tab_words[a].rearrange("p t i -> p (t i)").bitcast(I32))
+
+        def load_wh(b, a):
+            rows = wh[a * PASS : (a + 1) * PASS, b * PASS : (b + 1) * PASS]
+            nc.sync.dma_start(wh_raw[b, a][:], rows.rearrange("(p j) c -> p j c", j=PACK))
+
+        load_tab(0)
+        load_wh(0, 0)
+        load_wh(0, 1)
+        load_tab(1)
+        load_wh(1, 0)
+        load_wh(1, 1)
+        wo_planes = load_planes(wo_scales, N, "wo_planes", nc.sync)
+        wo_sb = held([P, PASSES * N], U32, "wo_sb")
+        nc.sync.dma_start(
+            wo_sb[:].bitcast(I32).rearrange("p (b c) -> p b c", b=PASSES),
+            wo_words.rearrange("b p c i -> p b (c i)").bitcast(I32),
+        )
+        map_sb = [held([P, T], F32, f"map_sb{u}") for u in range(TILES)]
+        for u in range(TILES):
+            nc.sync.dma_start(map_sb[u][:], gT[u * P : (u + 1) * P, :])
+
+        wa_codes = held([P, PASSES * 2 * H], U8, "wa_codes")
+        nc.vector.tensor_copy(
+            wa_codes[:].bitcast(U16).rearrange("p (g t m) -> p g t m", t=PACK, m=P),
+            wa_raw[:].bitcast(U16).rearrange("p (g m t) -> p g t m", t=PACK, m=P),
+        )
+
+        v_codes = {}
+        v_planes = {}
+
+        def gather_words(a, half):
+            v_codes[a, half] = held([P, HALF], U32, f"v_codes{a}{half}")
+            nc.vector.tensor_copy(v_codes[a, half][:], tab_sb[a][:].indirect(entries(half * HALF, HALF)))
+
+        def gather_planes(a, half):
+            v_planes[a, half] = held([P, HALF], U8, f"v_planes{a}{half}")
+            nc.vector.tensor_copy(
+                v_planes[a, half][:], tab_planes[:, a * T : (a + 1) * T].indirect(entries(half * HALF, HALF))
+            )
+
+        wh_codes = {}
+        wh_planes = {}
+
+        def quantize_wh(b, a):
+            grouped = ring.tile([P, PACK * PASS], BF16, name="wh_grouped", align_bytes=64)
+            dst = grouped[:].rearrange("p (t m j) -> p m j t", t=PACK, j=PACK)
+            src = wh_raw[b, a][:].rearrange("p j (m t) -> p m j t", t=PACK)
+            for t in range(0, PACK, 2):
+                nc.scalar.activation(dst[:, :, :, t : t + 2], src[:, :, :, t : t + 2], ACT.Copy, scale=-1.0)
+            wh_codes[b, a] = held([P, PASS], U32, f"wh_codes{b}{a}")
+            wh_planes[b, a] = held([P, PASS], U8, f"wh_planes{b}{a}")
+            nc.vector.quantize_mx(wh_codes[b, a][:].bitcast(FP8X4), wh_planes[b, a][:], grouped[:])
+
+        gather_words(0, 0)
+        gather_planes(0, 0)
+        gather_planes(1, 0)
+        wa_planes = held([P, PASSES * H], U8, "wa_planes")
+        nc.vector.tensor_copy(
+            wa_planes[:].rearrange("p (g t m) -> p g t m", t=PACK, m=P),
+            wa_planes_raw[:].rearrange("p (g m t) -> p g t m", t=PACK, m=P),
+        )
+        quantize_wh(0, 0)
+        quantize_wh(0, 1)
+        gather_words(1, 0)
+        quantize_wh(1, 0)
+        quantize_wh(1, 1)
+        gather_words(0, 1)
+        gather_planes(0, 1)
+        gather_planes(1, 1)
+        gather_words(1, 1)
+
+        h_codes = {}
+        h_planes = {}
+
+        def control(b, first, width, fused, grouped):
+            half, start = divmod(first, HALF)
+            sig = ring.tile([P, PACK, width], F32, name=f"sig{b}")
+            for t in range(PACK):
+                d = psum_d.tile([P, width], F32, name="d")
+                cols = slice(t * P, (t + 1) * P)
+                for a in range(PASSES):
+                    nc.tensor.matmul_mx(
+                        d[:],
+                        lhsT=wh_codes[b, a][:, cols].bitcast(FP8X4),
+                        lhsT_scale=wh_planes[b, a][:, cols],
+                        rhs=v_codes[a, half][:, start : start + width].bitcast(FP8X4),
+                        rhs_scale=v_planes[a, half][:, start : start + width],
+                        start=(a == 0),
+                        stop=False,
+                    )
+                step = width if width == HALF else FP4_NARROW
+                for a in range(PASSES):
+                    col = a * H + b * PASS + t * P
+                    for n0 in range(0, width, step):
+                        nc.tensor.matmul_mx(
+                            d[:, n0 : n0 + step],
+                            lhsT=wa_codes[:, 2 * col : 2 * (col + P)].bitcast(FP4X4),
+                            lhsT_scale=wa_planes[:, col : col + P],
+                            rhs=v_codes[a, half][:, start + n0 : start + n0 + step].bitcast(FP8X4),
+                            rhs_scale=v_planes[a, half][:, start + n0 : start + n0 + step],
+                            start=False,
+                            stop=(a == PASSES - 1 and n0 + step == width),
+                        )
+                nc.scalar.activation(sig[:, t, :], d[:], ACT.Sigmoid, bias=lead_sb[:, b, t : t + 1])
+            if fused:
+                factor = gain_sb[:, b, :].unsqueeze(1).unsqueeze(3).broadcast_to([P, width // 2, PACK, 2])
+                nc.vector.tensor_tensor(
+                    grouped[:].rearrange("p (c i t) -> p c t i", i=2, t=PACK),
+                    sig[:].rearrange("p t (c i) -> p c t i", i=2),
+                    factor,
+                    MULT,
+                )
+            else:
+                scaled = ring.tile([P, PACK, width], BF16, name=f"scaled{b}")
+                for t in range(PACK):
+                    nc.scalar.activation(scaled[:, t, :], sig[:, t, :], ACT.Copy, scale=gain_sb[:, b, t : t + 1])
+                nc.scalar.copy(
+                    grouped[:].rearrange("p (c i t) -> p c t i", i=4, t=PACK),
+                    scaled[:].rearrange("p t (c i) -> p c t i", i=4),
+                )
+            codes = held([P, width], U32, f"h_codes{b}_{first}")
+            planes = held([P, width], U8, f"h_planes{b}_{first}")
+            nc.vector.quantize_mx(codes[:].bitcast(FP8X4), planes[:], grouped[:])
+            for c0 in range(0, width, CHUNK):
+                h_codes[b, (first + c0) // CHUNK] = codes[:, c0 : c0 + CHUNK]
+                h_planes[b, (first + c0) // CHUNK] = planes[:, c0 : c0 + CHUNK]
+
+        def factors(c, u, dst):
+            y = psum_y.tile([P, CHUNK], F32, name="y")
+            for b in range(PASSES):
+                cols = slice(b * N + u * P, b * N + (u + 1) * P)
+                nc.tensor.matmul_mx(
+                    y[:],
+                    lhsT=wo_sb[:, cols].bitcast(FP8X4),
+                    lhsT_scale=wo_planes[:, cols],
+                    rhs=h_codes[b, c].bitcast(FP8X4),
+                    rhs_scale=h_planes[b, c],
+                    start=(b == 0),
+                    stop=(b == PASSES - 1),
+                )
+            nc.scalar.activation(dst, y[:], ACT.Identity, bias=bo_sb[:, u : u + 1])
+
+        def pick(u, first, picked):
+            nc.vector.tensor_copy(picked, map_sb[u][:].indirect(entries(first, picked.shape[1])))
+
+        def rescale(u, first, picked, factor):
+            nc.vector.tensor_tensor(map_sb[u][:].indirect(entries(first, picked.shape[1])), picked, factor, MULT)
+
+        LAG, WIDE = 2, 3
+        picked = {u: held([P, S], F32, f"picked{u}") for u in range(TILES) if u != LAG}
+        factor = [held([P, S], F32, f"factor{u}") for u in range(TILES)]
+
+        def span(c, n=1):
+            return slice(c * CHUNK, (c + n) * CHUNK)
+
+        def lagged(c, offset):
+            late = shared.tile([P, CHUNK], F32, name=f"late{c}", align_bytes=64, offset=offset)
+            pick(LAG, c * CHUNK, late[:])
+            rescale(LAG, c * CHUNK, late[:], factor[LAG][:, span(c)])
+
+        for c in range(CHUNKS):
+            if c % 2 == 0:
+                grouped0 = ring.tile([P, PACK * HALF], BF16, name="h_grouped0", align_bytes=64)
+                control(0, c * CHUNK, HALF, c == 0, grouped0)
+            offset = c * PACK * CHUNK * 2
+            grouped1 = shared.tile([P, PACK * CHUNK], BF16, name=f"h_grouped1_{c}", align_bytes=64, offset=offset)
+            control(1, c * CHUNK, CHUNK, c == 0, grouped1)
+            if c == 0:
+                for u in picked:
+                    for first in range(0, S, HALF):
+                        pick(u, first, picked[u][:, first : first + HALF])
+            else:
+                lagged(c - 1, offset)
+            for u in range(TILES):
+                factors(c, u, factor[u][:, span(c)])
+            for u in range(LAG):
+                rescale(u, c * CHUNK, picked[u][:, span(c)], factor[u][:, span(c)])
+            if c == CHUNKS - 1:
+                lagged(c, CHUNKS * PACK * CHUNK * 2)
+            if c % 2 == 1:
+                rescale(WIDE, (c - 1) * CHUNK, picked[WIDE][:, span(c - 1, 2)], factor[WIDE][:, span(c - 1, 2)])
+
+        for u in range(TILES):
+            nc.sync.dma_start(out[u * P : (u + 1) * P, :], map_sb[u][:])

@@ -34,7 +34,6 @@ def tile_list_pitch_control_rescale_kernel(
     nc = tc.nc
     with ExitStack() as ctx:
         keep = ctx.enter_context(tc.tile_pool(name="keep", bufs=1))
-        shared = ctx.enter_context(tc.tile_pool(name="shared", bufs=1))
         ring = ctx.enter_context(tc.tile_pool(name="ring", bufs=2))
         psum_d = ctx.enter_context(tc.psum_pool(name="psum_d", bufs=5))
         psum_y = ctx.enter_context(tc.psum_pool(name="psum_y", bufs=3))
@@ -48,37 +47,34 @@ def tile_list_pitch_control_rescale_kernel(
         def entries(first, count):
             return offsets[:, first // LIST_ROWS : (first + count) // LIST_ROWS]
 
-        def load_planes(scales, width, name, queue):
+        def zeroed_planes(width, name, engine):
             planes = held([P, PASSES * width], U8, name)
-            nc.vector.memset(planes[:].bitcast(I32), 0)
+            engine.memset(planes[:].bitcast(I32), 0)
+            return planes
+
+        def load_planes(planes, scales):
             for q in range(4):
-                queue.dma_start(
+                nc.sync.dma_start(
                     planes[32 * q : 32 * q + 4, :].bitcast(I32).rearrange("r (a w) -> r a w", a=PASSES),
                     scales[:, 4 * q : 4 * q + 4, :].bitcast(I32).rearrange("a r w -> r a w"),
                 )
-            return planes
+
+        tab_planes = zeroed_planes(T, "tab_planes", nc.vector)
+        wa_planes_raw = zeroed_planes(H, "wa_planes_raw", nc.gpsimd)
+        wo_planes = zeroed_planes(N, "wo_planes", nc.gpsimd)
 
         warm = held([P, 2], F32, "warm")
         nc.vector.memset(warm[:, 0:1], 0.0)
         nc.scalar.activation(warm[:, 1:2], warm[:, 0:1], ACT.Sigmoid)
 
-        tab_planes = load_planes(tab_scales, T, "tab_planes", nc.scalar)
-        wa_planes_raw = load_planes(wa_scales, H, "wa_planes_raw", nc.scalar)
+        wa_raw = held([P, PASSES * 2 * H], U8, "wa_raw")
+        tab_sb = [held([P, T], U32, f"tab_sb{a}") for a in range(PASSES)]
+        wh_raw = {(b, a): held([P, PACK, PASS], F32, f"wh_raw{b}{a}") for b in range(PASSES) for a in range(PASSES)}
+        map_sb = [held([P, T], F32, f"map_sb{u}") for u in range(TILES)]
         lead_sb = held([P, PASSES, PACK], F32, "lead_sb")
         gain_sb = held([P, PASSES, PACK], F32, "gain_sb")
         bo_sb = held([P, TILES], F32, "bo_sb")
-
-        nc.sync.dma_start(lead_sb[:], lead.rearrange("(b p t) -> p b t", b=PASSES, t=PACK))
-        nc.sync.dma_start(gain_sb[:], gain.rearrange("(b p t) -> p b t", b=PASSES, t=PACK))
-        with nc.allow_non_contiguous_dma("one bias value for each partition"):
-            nc.sync.dma_start(bo_sb[:], bo.rearrange("(u p) -> p u", p=P))
-        wa_raw = held([P, PASSES * 2 * H], U8, "wa_raw")
-        nc.sync.dma_start(
-            wa_raw[:].bitcast(I32).rearrange("p (a w) -> p a w", a=PASSES),
-            wa_words.bitcast(I32).rearrange("a p w -> p a w"),
-        )
-        tab_sb = [held([P, T], U32, f"tab_sb{a}") for a in range(PASSES)]
-        wh_raw = {(b, a): held([P, PACK, PASS], F32, f"wh_raw{b}{a}") for b in range(PASSES) for a in range(PASSES)}
+        wo_sb = held([P, PASSES * N], U32, "wo_sb")
 
         def load_tab(a):
             nc.sync.dma_start(tab_sb[a][:].bitcast(I32), tab_words[a].rearrange("p t i -> p (t i)").bitcast(I32))
@@ -87,21 +83,34 @@ def tile_list_pitch_control_rescale_kernel(
             rows = wh[a * PASS : (a + 1) * PASS, b * PASS : (b + 1) * PASS]
             nc.sync.dma_start(wh_raw[b, a][:], rows.rearrange("(p j) c -> p j c", j=PACK))
 
+        def load_map(u):
+            nc.sync.dma_start(map_sb[u][:], gT[u * P : (u + 1) * P, :])
+
+        nc.sync.dma_start(
+            wa_raw[:].bitcast(I32).rearrange("p (a w) -> p a w", a=PASSES),
+            wa_words.bitcast(I32).rearrange("a p w -> p a w"),
+        )
+        load_planes(tab_planes, tab_scales)
         load_tab(0)
         load_wh(0, 0)
+        load_planes(wa_planes_raw, wa_scales)
         load_wh(0, 1)
+        nc.sync.dma_start(lead_sb[:], lead.rearrange("(b p t) -> p b t", b=PASSES, t=PACK))
         load_tab(1)
+        nc.sync.dma_start(gain_sb[:], gain.rearrange("(b p t) -> p b t", b=PASSES, t=PACK))
         load_wh(1, 0)
+        load_map(0)
         load_wh(1, 1)
-        wo_planes = load_planes(wo_scales, N, "wo_planes", nc.sync)
-        wo_sb = held([P, PASSES * N], U32, "wo_sb")
+        load_map(1)
+        load_planes(wo_planes, wo_scales)
         nc.sync.dma_start(
             wo_sb[:].bitcast(I32).rearrange("p (b c) -> p b c", b=PASSES),
             wo_words.rearrange("b p c i -> p b (c i)").bitcast(I32),
         )
-        map_sb = [held([P, T], F32, f"map_sb{u}") for u in range(TILES)]
-        for u in range(TILES):
-            nc.sync.dma_start(map_sb[u][:], gT[u * P : (u + 1) * P, :])
+        load_map(2)
+        load_map(3)
+        with nc.allow_non_contiguous_dma("one bias value for each partition"):
+            nc.sync.dma_start(bo_sb[:], bo.rearrange("(u p) -> p u", p=P))
 
         wa_codes = held([P, PASSES * 2 * H], U8, "wa_codes")
         nc.vector.tensor_copy(
@@ -135,9 +144,9 @@ def tile_list_pitch_control_rescale_kernel(
             wh_planes[b, a] = held([P, PASS], U8, f"wh_planes{b}{a}")
             nc.vector.quantize_mx(wh_codes[b, a][:].bitcast(FP8X4), wh_planes[b, a][:], grouped[:])
 
-        gather_words(0, 0)
         gather_planes(0, 0)
         gather_planes(1, 0)
+        gather_words(0, 0)
         wa_planes = held([P, PASSES * H], U8, "wa_planes")
         nc.vector.tensor_copy(
             wa_planes[:].rearrange("p (g t m) -> p g t m", t=PACK, m=P),
@@ -148,9 +157,9 @@ def tile_list_pitch_control_rescale_kernel(
         gather_words(1, 0)
         quantize_wh(1, 0)
         quantize_wh(1, 1)
-        gather_words(0, 1)
         gather_planes(0, 1)
         gather_planes(1, 1)
+        gather_words(0, 1)
         gather_words(1, 1)
 
         h_codes = {}
@@ -230,39 +239,36 @@ def tile_list_pitch_control_rescale_kernel(
         def rescale(u, first, picked, factor):
             nc.vector.tensor_tensor(map_sb[u][:].indirect(entries(first, picked.shape[1])), picked, factor, MULT)
 
-        LAG, WIDE = 2, 3
-        picked = {u: held([P, S], F32, f"picked{u}") for u in range(TILES) if u != LAG}
+        picked = [held([P, S], F32, f"picked{u}") for u in range(TILES)]
         factor = [held([P, S], F32, f"factor{u}") for u in range(TILES)]
 
         def span(c, n=1):
             return slice(c * CHUNK, (c + n) * CHUNK)
 
-        def lagged(c, offset):
-            late = shared.tile([P, CHUNK], F32, name=f"late{c}", align_bytes=64, offset=offset)
-            pick(LAG, c * CHUNK, late[:])
-            rescale(LAG, c * CHUNK, late[:], factor[LAG][:, span(c)])
-
-        for c in range(CHUNKS):
+        def controls(c):
             if c % 2 == 0:
                 grouped0 = ring.tile([P, PACK * HALF], BF16, name="h_grouped0", align_bytes=64)
                 control(0, c * CHUNK, HALF, c == 0, grouped0)
-            offset = c * PACK * CHUNK * 2
-            grouped1 = shared.tile([P, PACK * CHUNK], BF16, name=f"h_grouped1_{c}", align_bytes=64, offset=offset)
+            grouped1 = ring.tile([P, PACK * CHUNK], BF16, name="h_grouped1", align_bytes=64)
             control(1, c * CHUNK, CHUNK, c == 0, grouped1)
-            if c == 0:
-                for u in picked:
-                    for first in range(0, S, HALF):
-                        pick(u, first, picked[u][:, first : first + HALF])
-            else:
-                lagged(c - 1, offset)
+
+        def update(c):
             for u in range(TILES):
                 factors(c, u, factor[u][:, span(c)])
-            for u in range(LAG):
-                rescale(u, c * CHUNK, picked[u][:, span(c)], factor[u][:, span(c)])
-            if c == CHUNKS - 1:
-                lagged(c, CHUNKS * PACK * CHUNK * 2)
-            if c % 2 == 1:
-                rescale(WIDE, (c - 1) * CHUNK, picked[WIDE][:, span(c - 1, 2)], factor[WIDE][:, span(c - 1, 2)])
+            for u in range(TILES):
+                if u < TILES - 1 or c < CHUNKS - 2:
+                    rescale(u, c * CHUNK, picked[u][:, span(c)], factor[u][:, span(c)])
+                elif c == CHUNKS - 1:
+                    rescale(u, (c - 1) * CHUNK, picked[u][:, span(c - 1, 2)], factor[u][:, span(c - 1, 2)])
+
+        controls(0)
+        for u in range(TILES):
+            for first in range(0, S, HALF):
+                pick(u, first, picked[u][:, first : first + HALF])
+        for c in range(CHUNKS):
+            if c + 1 < CHUNKS:
+                controls(c + 1)
+            update(c)
 
         for u in range(TILES):
             nc.sync.dma_start(out[u * P : (u + 1) * P, :], map_sb[u][:])

@@ -53,10 +53,10 @@ def tile_list_pitch_control_rescale_kernel(
             return planes
 
         def load_planes(planes, scales):
-            for q in range(4):
+            for r in range(4):
                 nc.sync.dma_start(
-                    planes[32 * q : 32 * q + 4, :].bitcast(I32).rearrange("r (a w) -> r a w", a=PASSES),
-                    scales[:, 4 * q : 4 * q + 4, :].bitcast(I32).rearrange("a r w -> r a w"),
+                    planes[r:P:32, :].bitcast(I32).rearrange("q (a w) -> q a w", a=PASSES),
+                    scales[:, r:16:4, :].bitcast(I32).rearrange("a q w -> q a w"),
                 )
 
         tab_planes = zeroed_planes(T, "tab_planes", nc.vector)
@@ -95,12 +95,12 @@ def tile_list_pitch_control_rescale_kernel(
         load_wh(0, 0)
         load_planes(wa_planes_raw, wa_scales)
         load_wh(0, 1)
-        nc.sync.dma_start(lead_sb[:], lead.rearrange("(b p t) -> p b t", b=PASSES, t=PACK))
         load_tab(1)
-        nc.sync.dma_start(gain_sb[:], gain.rearrange("(b p t) -> p b t", b=PASSES, t=PACK))
+        nc.sync.dma_start(lead_sb[:], lead.rearrange("(b p t) -> p b t", b=PASSES, t=PACK))
         load_wh(1, 0)
-        load_map(0)
         load_wh(1, 1)
+        nc.sync.dma_start(gain_sb[:], gain.rearrange("(b p t) -> p b t", b=PASSES, t=PACK))
+        load_map(0)
         load_map(1)
         load_planes(wo_planes, wo_scales)
         nc.sync.dma_start(
@@ -139,7 +139,10 @@ def tile_list_pitch_control_rescale_kernel(
             dst = grouped[:].rearrange("p (t m j) -> p m j t", t=PACK, j=PACK)
             src = wh_raw[b, a][:].rearrange("p j (m t) -> p m j t", t=PACK)
             for t in range(0, PACK, 2):
-                nc.scalar.activation(dst[:, :, :, t : t + 2], src[:, :, :, t : t + 2], ACT.Copy, scale=-1.0)
+                if b == 0:
+                    nc.scalar.activation(dst[:, :, :, t : t + 2], src[:, :, :, t : t + 2], ACT.Copy, scale=-1.0)
+                else:
+                    nc.vector.tensor_scalar_mul(dst[:, :, :, t : t + 2], src[:, :, :, t : t + 2], -1.0)
             wh_codes[b, a] = held([P, PASS], U32, f"wh_codes{b}{a}")
             wh_planes[b, a] = held([P, PASS], U8, f"wh_planes{b}{a}")
             nc.vector.quantize_mx(wh_codes[b, a][:].bitcast(FP8X4), wh_planes[b, a][:], grouped[:])
@@ -250,7 +253,7 @@ def tile_list_pitch_control_rescale_kernel(
                 grouped0 = ring.tile([P, PACK * HALF], BF16, name="h_grouped0", align_bytes=64)
                 control(0, c * CHUNK, HALF, c == 0, grouped0)
             grouped1 = ring.tile([P, PACK * CHUNK], BF16, name="h_grouped1", align_bytes=64)
-            control(1, c * CHUNK, CHUNK, c == 0, grouped1)
+            control(1, c * CHUNK, CHUNK, False, grouped1)
 
         def update(c):
             for u in range(TILES):

@@ -19,13 +19,16 @@ MULT = mybir.AluOpType.mult
 P = 128
 PACK = 4
 PASS = P * PACK
-PASSES = 2
-LIST_ROWS = 16
+PASSES = K // PASS
+QUADRANT = 32
+PLANE_ROWS = PASS // 32
+PER_COLUMN = 16
 HALF = 512
 CHUNK = 256
 CHUNKS = S // CHUNK
 TILES = N // P
 FP4_NARROW = 128
+D_BANKS, Y_BANKS = 5, 3
 
 
 def tile_list_pitch_control_rescale_kernel(
@@ -35,17 +38,17 @@ def tile_list_pitch_control_rescale_kernel(
     with ExitStack() as ctx:
         keep = ctx.enter_context(tc.tile_pool(name="keep", bufs=1))
         ring = ctx.enter_context(tc.tile_pool(name="ring", bufs=2))
-        psum_d = ctx.enter_context(tc.psum_pool(name="psum_d", bufs=5))
-        psum_y = ctx.enter_context(tc.psum_pool(name="psum_y", bufs=3))
+        psum_d = ctx.enter_context(tc.psum_pool(name="psum_d", bufs=D_BANKS))
+        psum_y = ctx.enter_context(tc.psum_pool(name="psum_y", bufs=Y_BANKS))
 
         def held(shape, dtype, name):
             return keep.tile(shape, dtype, name=name, align_bytes=64)
 
-        offsets = keep.tile([P, S // LIST_ROWS], U16, name="offsets")
+        offsets = keep.tile([P, S // PER_COLUMN], U16, name="offsets")
         nc.sync.dma_start(offsets[:], offs)
 
         def entries(first, count):
-            return offsets[:, first // LIST_ROWS : (first + count) // LIST_ROWS]
+            return offsets[:, first // PER_COLUMN : (first + count) // PER_COLUMN]
 
         def zeroed_planes(width, name, engine):
             planes = held([P, PASSES * width], U8, name)
@@ -53,19 +56,15 @@ def tile_list_pitch_control_rescale_kernel(
             return planes
 
         def load_planes(planes, scales):
-            for r in range(4):
+            for r in range(PACK):
                 nc.sync.dma_start(
-                    planes[r:P:32, :].bitcast(I32).rearrange("q (a w) -> q a w", a=PASSES),
-                    scales[:, r:16:4, :].bitcast(I32).rearrange("a q w -> q a w"),
+                    planes[r:P:QUADRANT, :].bitcast(I32).rearrange("q (a w) -> q a w", a=PASSES),
+                    scales[:, r:PLANE_ROWS:PACK, :].bitcast(I32).rearrange("a q w -> q a w"),
                 )
 
         tab_planes = zeroed_planes(T, "tab_planes", nc.vector)
         wa_planes_raw = zeroed_planes(H, "wa_planes_raw", nc.gpsimd)
         wo_planes = zeroed_planes(N, "wo_planes", nc.gpsimd)
-
-        warm = held([P, 2], F32, "warm")
-        nc.vector.memset(warm[:, 0:1], 0.0)
-        nc.scalar.activation(warm[:, 1:2], warm[:, 0:1], ACT.Sigmoid)
 
         wa_raw = held([P, PASSES * 2 * H], U8, "wa_raw")
         tab_sb = [held([P, T], U32, f"tab_sb{a}") for a in range(PASSES)]
@@ -112,24 +111,26 @@ def tile_list_pitch_control_rescale_kernel(
         with nc.allow_non_contiguous_dma("one bias value for each partition"):
             nc.sync.dma_start(bo_sb[:], bo.rearrange("(u p) -> p u", p=P))
 
-        wa_codes = held([P, PASSES * 2 * H], U8, "wa_codes")
-        nc.vector.tensor_copy(
-            wa_codes[:].bitcast(U16).rearrange("p (g t m) -> p g t m", t=PACK, m=P),
-            wa_raw[:].bitcast(U16).rearrange("p (g m t) -> p g t m", t=PACK, m=P),
-        )
+        def reorder_columns(dst, src):
+            nc.vector.tensor_copy(
+                dst.rearrange("p (g t m) -> p g t m", t=PACK, m=P),
+                src.rearrange("p (g m t) -> p g t m", t=PACK, m=P),
+            )
 
         v_codes = {}
         v_planes = {}
 
-        def gather_words(a, half):
-            v_codes[a, half] = held([P, HALF], U32, f"v_codes{a}{half}")
-            nc.vector.tensor_copy(v_codes[a, half][:], tab_sb[a][:].indirect(entries(half * HALF, HALF)))
+        def gather_words(a, first, count):
+            listed_words = held([P, count], U32, f"v_codes{a}_{first}")
+            nc.vector.tensor_copy(listed_words[:], tab_sb[a][:].indirect(entries(first, count)))
+            for start in range(0, count, HALF):
+                v_codes[a, (first + start) // HALF] = listed_words[:, start : start + HALF]
 
-        def gather_planes(a, half):
-            v_planes[a, half] = held([P, HALF], U8, f"v_planes{a}{half}")
-            nc.vector.tensor_copy(
-                v_planes[a, half][:], tab_planes[:, a * T : (a + 1) * T].indirect(entries(half * HALF, HALF))
-            )
+        def gather_plane(a):
+            listed_scales = held([P, S], U8, f"v_planes{a}")
+            nc.vector.tensor_copy(listed_scales[:], tab_planes[:, a * T : (a + 1) * T].indirect(offsets[:]))
+            for half in range(S // HALF):
+                v_planes[a, half] = listed_scales[:, half * HALF : (half + 1) * HALF]
 
         wh_codes = {}
         wh_planes = {}
@@ -147,30 +148,23 @@ def tile_list_pitch_control_rescale_kernel(
             wh_planes[b, a] = held([P, PASS], U8, f"wh_planes{b}{a}")
             nc.vector.quantize_mx(wh_codes[b, a][:].bitcast(FP8X4), wh_planes[b, a][:], grouped[:])
 
-        gather_planes(0, 0)
-        gather_planes(1, 0)
-        gather_words(0, 0)
+        wa_codes = held([P, PASSES * 2 * H], U8, "wa_codes")
+        reorder_columns(wa_codes[:].bitcast(U16), wa_raw[:].bitcast(U16))
+        gather_plane(0)
+        gather_plane(1)
+        gather_words(0, 0, S)
         wa_planes = held([P, PASSES * H], U8, "wa_planes")
-        nc.vector.tensor_copy(
-            wa_planes[:].rearrange("p (g t m) -> p g t m", t=PACK, m=P),
-            wa_planes_raw[:].rearrange("p (g m t) -> p g t m", t=PACK, m=P),
-        )
+        reorder_columns(wa_planes[:], wa_planes_raw[:])
         quantize_wh(0, 0)
         quantize_wh(0, 1)
-        gather_words(1, 0)
+        gather_words(1, 0, HALF)
         quantize_wh(1, 0)
         quantize_wh(1, 1)
-        gather_planes(0, 1)
-        gather_planes(1, 1)
-        gather_words(0, 1)
-        gather_words(1, 1)
+        gather_words(1, HALF, HALF)
 
-        h_codes = {}
-        h_planes = {}
-
-        def control(b, first, width, fused, grouped):
+        def control(b, first, width):
             half, start = divmod(first, HALF)
-            sig = ring.tile([P, PACK, width], F32, name=f"sig{b}")
+            sig = ring.tile([P, PACK, width], F32, name=f"sig{width}")
             for t in range(PACK):
                 d = psum_d.tile([P, width], F32, name="d")
                 cols = slice(t * P, (t + 1) * P)
@@ -198,30 +192,28 @@ def tile_list_pitch_control_rescale_kernel(
                             stop=(a == PASSES - 1 and n0 + step == width),
                         )
                 nc.scalar.activation(sig[:, t, :], d[:], ACT.Sigmoid, bias=lead_sb[:, b, t : t + 1])
-            if fused:
-                factor = gain_sb[:, b, :].unsqueeze(1).unsqueeze(3).broadcast_to([P, width // 2, PACK, 2])
-                nc.vector.tensor_tensor(
-                    grouped[:].rearrange("p (c i t) -> p c t i", i=2, t=PACK),
-                    sig[:].rearrange("p t (c i) -> p c t i", i=2),
-                    factor,
-                    MULT,
-                )
-            else:
-                scaled = ring.tile([P, PACK, width], BF16, name=f"scaled{b}")
-                for t in range(PACK):
-                    nc.scalar.activation(scaled[:, t, :], sig[:, t, :], ACT.Copy, scale=gain_sb[:, b, t : t + 1])
-                nc.scalar.copy(
-                    grouped[:].rearrange("p (c i t) -> p c t i", i=4, t=PACK),
-                    scaled[:].rearrange("p t (c i) -> p c t i", i=4),
-                )
-            codes = held([P, width], U32, f"h_codes{b}_{first}")
-            planes = held([P, width], U8, f"h_planes{b}_{first}")
-            nc.vector.quantize_mx(codes[:].bitcast(FP8X4), planes[:], grouped[:])
-            for c0 in range(0, width, CHUNK):
-                h_codes[b, (first + c0) // CHUNK] = codes[:, c0 : c0 + CHUNK]
-                h_planes[b, (first + c0) // CHUNK] = planes[:, c0 : c0 + CHUNK]
+            scaled = ring.tile([P, PACK, width], BF16, name=f"scaled{width}")
+            for t in range(PACK):
+                nc.scalar.activation(scaled[:, t, :], sig[:, t, :], ACT.Copy, scale=gain_sb[:, b, t : t + 1])
+            return scaled
 
-        def factors(c, u, dst):
+        h_codes = {}
+        h_planes = {}
+
+        def quantize_h(b, c, scaled):
+            grouped = ring.tile([P, PACK * CHUNK], BF16, name="h_grouped", align_bytes=64, bufs=3)
+            nc.scalar.copy(
+                grouped[:].rearrange("p (e i t) -> p e t i", i=4, t=PACK),
+                scaled.rearrange("p t (e i) -> p e t i", i=4),
+            )
+            h_codes[b, c] = held([P, CHUNK], U32, f"h_codes{b}{c}")
+            h_planes[b, c] = held([P, CHUNK], U8, f"h_planes{b}{c}")
+            nc.vector.quantize_mx(h_codes[b, c][:].bitcast(FP8X4), h_planes[b, c][:], grouped[:])
+
+        picked = [held([P, S], F32, f"picked{u}") for u in range(TILES)]
+        factor = [held([P, S], F32, f"factor{u}") for u in range(TILES)]
+
+        def factors(c, u):
             y = psum_y.tile([P, CHUNK], F32, name="y")
             for b in range(PASSES):
                 cols = slice(b * N + u * P, b * N + (u + 1) * P)
@@ -229,49 +221,40 @@ def tile_list_pitch_control_rescale_kernel(
                     y[:],
                     lhsT=wo_sb[:, cols].bitcast(FP8X4),
                     lhsT_scale=wo_planes[:, cols],
-                    rhs=h_codes[b, c].bitcast(FP8X4),
-                    rhs_scale=h_planes[b, c],
+                    rhs=h_codes[b, c][:].bitcast(FP8X4),
+                    rhs_scale=h_planes[b, c][:],
                     start=(b == 0),
                     stop=(b == PASSES - 1),
                 )
-            nc.scalar.activation(dst, y[:], ACT.Identity, bias=bo_sb[:, u : u + 1])
+            span = slice(c * CHUNK, (c + 1) * CHUNK)
+            nc.scalar.activation(factor[u][:, span], y[:], ACT.Identity, bias=bo_sb[:, u : u + 1])
 
-        def pick(u, first, picked):
-            nc.vector.tensor_copy(picked, map_sb[u][:].indirect(entries(first, picked.shape[1])))
-
-        def rescale(u, first, picked, factor):
-            nc.vector.tensor_tensor(map_sb[u][:].indirect(entries(first, picked.shape[1])), picked, factor, MULT)
-
-        picked = [held([P, S], F32, f"picked{u}") for u in range(TILES)]
-        factor = [held([P, S], F32, f"factor{u}") for u in range(TILES)]
-
-        def span(c, n=1):
-            return slice(c * CHUNK, (c + n) * CHUNK)
-
-        def controls(c):
-            if c % 2 == 0:
-                grouped0 = ring.tile([P, PACK * HALF], BF16, name="h_grouped0", align_bytes=64)
-                control(0, c * CHUNK, HALF, c == 0, grouped0)
-            grouped1 = ring.tile([P, PACK * CHUNK], BF16, name="h_grouped1", align_bytes=64)
-            control(1, c * CHUNK, CHUNK, False, grouped1)
+        def rescale(u, first, count):
+            span = slice(first, first + count)
+            window = map_sb[u][:].indirect(entries(first, count))
+            nc.vector.tensor_tensor(window, picked[u][:, span], factor[u][:, span], MULT)
 
         def update(c):
             for u in range(TILES):
-                factors(c, u, factor[u][:, span(c)])
+                factors(c, u)
             for u in range(TILES):
                 if u < TILES - 1 or c < CHUNKS - 2:
-                    rescale(u, c * CHUNK, picked[u][:, span(c)], factor[u][:, span(c)])
+                    rescale(u, c * CHUNK, CHUNK)
                 elif c == CHUNKS - 1:
-                    rescale(u, (c - 1) * CHUNK, picked[u][:, span(c - 1, 2)], factor[u][:, span(c - 1, 2)])
+                    rescale(u, (c - 1) * CHUNK, 2 * CHUNK)
 
-        controls(0)
-        for u in range(TILES):
-            for first in range(0, S, HALF):
-                pick(u, first, picked[u][:, first : first + HALF])
         for c in range(CHUNKS):
-            if c + 1 < CHUNKS:
-                controls(c + 1)
-            update(c)
+            first = c * CHUNK
+            if first % HALF == 0:
+                scaled_wide = control(0, first, HALF)
+            quantize_h(0, c, scaled_wide[:, :, first % HALF : first % HALF + CHUNK])
+            quantize_h(1, c, control(1, first, CHUNK)[:])
+            if c == 0:
+                for u in range(TILES):
+                    nc.vector.tensor_copy(picked[u][:], map_sb[u][:].indirect(offsets[:]))
+            else:
+                update(c - 1)
+        update(CHUNKS - 1)
 
         for u in range(TILES):
             nc.sync.dma_start(out[u * P : (u + 1) * P, :], map_sb[u][:])

@@ -41,8 +41,8 @@ def tile_list_pitch_control_rescale_kernel(
         psum_d = ctx.enter_context(tc.psum_pool(name="psum_d", bufs=D_BANKS))
         psum_y = ctx.enter_context(tc.psum_pool(name="psum_y", bufs=Y_BANKS))
 
-        def held(shape, dtype, name):
-            return keep.tile(shape, dtype, name=name, align_bytes=64)
+        def held(shape, dtype, name, pool=keep):
+            return pool.tile(shape, dtype, name=name, align_bytes=64)
 
         offsets = keep.tile([P, S // PER_COLUMN], U16, name="offsets")
         nc.sync.dma_start(offsets[:], offs)
@@ -50,9 +50,9 @@ def tile_list_pitch_control_rescale_kernel(
         def entries(first, count):
             return offsets[:, first // PER_COLUMN : (first + count) // PER_COLUMN]
 
-        def zeroed_planes(width, name, engine):
-            planes = held([P, PASSES * width], U8, name)
-            engine.memset(planes[:].bitcast(I32), 0)
+        def zeroed(width, name, pool=keep):
+            planes = held([P, width], U8, name, pool)
+            nc.vector.memset(planes[:].bitcast(I32), 0)
             return planes
 
         def load_planes(planes, scales):
@@ -62,54 +62,22 @@ def tile_list_pitch_control_rescale_kernel(
                     scales[:, r:PLANE_ROWS:PACK, :].bitcast(I32).rearrange("a q w -> q a w"),
                 )
 
-        tab_planes = zeroed_planes(T, "tab_planes", nc.vector)
-        wa_planes_raw = zeroed_planes(H, "wa_planes_raw", nc.gpsimd)
-        wo_planes = zeroed_planes(N, "wo_planes", nc.gpsimd)
+        tab_sb = {}
+        wh_raw = {}
+        map_sb = {}
 
-        wa_raw = held([P, PASSES * 2 * H], U8, "wa_raw")
-        tab_sb = [held([P, T], U32, f"tab_sb{a}") for a in range(PASSES)]
-        wh_raw = {(b, a): held([P, PACK, PASS], F32, f"wh_raw{b}{a}") for b in range(PASSES) for a in range(PASSES)}
-        map_sb = [held([P, T], F32, f"map_sb{u}") for u in range(TILES)]
-        lead_sb = held([P, PASSES, PACK], F32, "lead_sb")
-        gain_sb = held([P, PASSES, PACK], F32, "gain_sb")
-        bo_sb = held([P, TILES], F32, "bo_sb")
-        wo_sb = held([P, PASSES * N], U32, "wo_sb")
-
-        def load_tab(a):
+        def load_tab(a, pool):
+            tab_sb[a] = held([P, T], U32, f"tab_sb{a}", pool)
             nc.sync.dma_start(tab_sb[a][:].bitcast(I32), tab_words[a].rearrange("p t i -> p (t i)").bitcast(I32))
 
-        def load_wh(b, a):
+        def load_wh(b, a, pool):
+            wh_raw[b, a] = held([P, PACK, PASS], F32, f"wh_raw{b}{a}", pool)
             rows = wh[a * PASS : (a + 1) * PASS, b * PASS : (b + 1) * PASS]
             nc.sync.dma_start(wh_raw[b, a][:], rows.rearrange("(p j) c -> p j c", j=PACK))
 
-        def load_map(u):
+        def load_map(u, pool):
+            map_sb[u] = held([P, T], F32, f"map_sb{u}", pool)
             nc.sync.dma_start(map_sb[u][:], gT[u * P : (u + 1) * P, :])
-
-        nc.sync.dma_start(
-            wa_raw[:].bitcast(I32).rearrange("p (a w) -> p a w", a=PASSES),
-            wa_words.bitcast(I32).rearrange("a p w -> p a w"),
-        )
-        load_planes(tab_planes, tab_scales)
-        load_tab(0)
-        load_wh(0, 0)
-        load_planes(wa_planes_raw, wa_scales)
-        load_wh(0, 1)
-        load_tab(1)
-        nc.sync.dma_start(lead_sb[:], lead.rearrange("(b p t) -> p b t", b=PASSES, t=PACK))
-        load_wh(1, 0)
-        load_wh(1, 1)
-        nc.sync.dma_start(gain_sb[:], gain.rearrange("(b p t) -> p b t", b=PASSES, t=PACK))
-        load_map(0)
-        load_map(1)
-        load_planes(wo_planes, wo_scales)
-        nc.sync.dma_start(
-            wo_sb[:].bitcast(I32).rearrange("p (b c) -> p b c", b=PASSES),
-            wo_words.rearrange("b p c i -> p b (c i)").bitcast(I32),
-        )
-        load_map(2)
-        load_map(3)
-        with nc.allow_non_contiguous_dma("one bias value for each partition"):
-            nc.sync.dma_start(bo_sb[:], bo.rearrange("(u p) -> p u", p=P))
 
         def reorder_columns(dst, src):
             nc.vector.tensor_copy(
@@ -117,20 +85,61 @@ def tile_list_pitch_control_rescale_kernel(
                 src.rearrange("p (g m t) -> p g t m", t=PACK, m=P),
             )
 
-        v_codes = {}
-        v_planes = {}
+        wa_raw = held([P, PASSES * 2 * H], U8, "wa_raw")
+        wa_codes = held([P, PASSES * 2 * H], U8, "wa_codes")
+        v_plane = [held([P, S], U8, "v_plane0")]
+        with tc.tile_pool(name="early", bufs=1) as early:
+            tab_rows = zeroed(T, "tab_rows", early)
+            wa_planes_raw = zeroed(PASSES * H, "wa_planes_raw")
+            v_plane.append(zeroed(S, "v_plane1"))
+            nc.sync.dma_start(
+                wa_raw[:].bitcast(I32).rearrange("p (a w) -> p a w", a=PASSES),
+                wa_words.bitcast(I32).rearrange("a p w -> p a w"),
+            )
+            for r in range(PACK):
+                nc.sync.dma_start(
+                    tab_rows[r:P:QUADRANT, :].bitcast(I32), tab_scales[0, r:PLANE_ROWS:PACK, :].bitcast(I32)
+                )
+            nc.sync.dma_start(tab_rows[PACK : PACK + PLANE_ROWS, :].bitcast(I32), tab_scales[1].bitcast(I32))
+            load_tab(0, keep)
+            load_wh(0, 0, keep)
+            load_planes(wa_planes_raw, wa_scales)
+            load_wh(0, 1, keep)
+            reorder_columns(wa_codes[:].bitcast(U16), wa_raw[:].bitcast(U16))
+            nc.vector.tensor_copy(v_plane[0][:], tab_rows[:].indirect(offsets[:]))
+        for q in range(P // QUADRANT):
+            nc.sync.dma_start(
+                v_plane[1][q * QUADRANT : q * QUADRANT + PACK, :].bitcast(I32),
+                v_plane[0][PACK * (q + 1) : PACK * (q + 2), :].bitcast(I32),
+            )
+
+        late = ctx.enter_context(tc.tile_pool(name="late", bufs=1))
+        lead_sb = held([P, PASSES, PACK], F32, "lead_sb", late)
+        gain_sb = held([P, PASSES, PACK], F32, "gain_sb", late)
+        bo_sb = held([P, TILES], F32, "bo_sb", late)
+        wo_sb = held([P, PASSES * N], U32, "wo_sb", late)
+        load_tab(1, late)
+        nc.sync.dma_start(lead_sb[:], lead.rearrange("(b p t) -> p b t", b=PASSES, t=PACK))
+        load_wh(1, 0, late)
+        nc.sync.dma_start(gain_sb[:], gain.rearrange("(b p t) -> p b t", b=PASSES, t=PACK))
+        load_wh(1, 1, late)
+        load_map(0, late)
+        load_map(1, late)
+        load_map(2, late)
+        wo_planes = zeroed(PASSES * N, "wo_planes", late)
+        load_planes(wo_planes, wo_scales)
+        nc.sync.dma_start(
+            wo_sb[:].bitcast(I32).rearrange("p (b c) -> p b c", b=PASSES),
+            wo_words.rearrange("b p c i -> p b (c i)").bitcast(I32),
+        )
+        with nc.allow_non_contiguous_dma("one bias value for each partition"):
+            nc.sync.dma_start(bo_sb[:], bo.rearrange("(u p) -> p u", p=P))
+        load_map(3, late)
+
+        v_codes = [held([P, S], U32, f"v_codes{a}") for a in range(PASSES)]
 
         def gather_words(a, first, count):
-            listed_words = held([P, count], U32, f"v_codes{a}_{first}")
-            nc.vector.tensor_copy(listed_words[:], tab_sb[a][:].indirect(entries(first, count)))
-            for start in range(0, count, HALF):
-                v_codes[a, (first + start) // HALF] = listed_words[:, start : start + HALF]
-
-        def gather_plane(a):
-            listed_scales = held([P, S], U8, f"v_planes{a}")
-            nc.vector.tensor_copy(listed_scales[:], tab_planes[:, a * T : (a + 1) * T].indirect(offsets[:]))
-            for half in range(S // HALF):
-                v_planes[a, half] = listed_scales[:, half * HALF : (half + 1) * HALF]
+            nc.vector.tensor_copy(v_codes[a][:, first : first + count], tab_sb[a][:].indirect(entries(first, count)))
 
         wh_codes = {}
         wh_planes = {}
@@ -140,31 +149,38 @@ def tile_list_pitch_control_rescale_kernel(
             dst = grouped[:].rearrange("p (t m j) -> p m j t", t=PACK, j=PACK)
             src = wh_raw[b, a][:].rearrange("p j (m t) -> p m j t", t=PACK)
             for t in range(0, PACK, 2):
-                if b == 0:
+                if (b, a) == (0, 0) or (b, a, t) == (0, 1, 0):
                     nc.scalar.activation(dst[:, :, :, t : t + 2], src[:, :, :, t : t + 2], ACT.Copy, scale=-1.0)
                 else:
                     nc.vector.tensor_scalar_mul(dst[:, :, :, t : t + 2], src[:, :, :, t : t + 2], -1.0)
             wh_codes[b, a] = held([P, PASS], U32, f"wh_codes{b}{a}")
             wh_planes[b, a] = held([P, PASS], U8, f"wh_planes{b}{a}")
-            nc.vector.quantize_mx(wh_codes[b, a][:].bitcast(FP8X4), wh_planes[b, a][:], grouped[:])
+            for t in range(0, PACK, 2):
+                cols = slice(t * P, (t + 2) * P)
+                nc.vector.quantize_mx(
+                    wh_codes[b, a][:, cols].bitcast(FP8X4),
+                    wh_planes[b, a][:, cols],
+                    grouped[:, t * PASS : (t + 2) * PASS],
+                )
 
-        wa_codes = held([P, PASSES * 2 * H], U8, "wa_codes")
-        reorder_columns(wa_codes[:].bitcast(U16), wa_raw[:].bitcast(U16))
-        gather_plane(0)
-        gather_plane(1)
+        picked = [held([P, S], F32, f"picked{u}") for u in range(TILES)]
+
+        def pick(u):
+            nc.vector.tensor_copy(picked[u][:], map_sb[u][:].indirect(offsets[:]))
+
         gather_words(0, 0, S)
         wa_planes = held([P, PASSES * H], U8, "wa_planes")
         reorder_columns(wa_planes[:], wa_planes_raw[:])
         quantize_wh(0, 0)
         quantize_wh(0, 1)
         gather_words(1, 0, HALF)
+        gather_words(1, HALF, HALF)
         quantize_wh(1, 0)
         quantize_wh(1, 1)
-        gather_words(1, HALF, HALF)
 
-        def control(b, first, width):
-            half, start = divmod(first, HALF)
+        def sigmoids(b, first, width):
             sig = ring.tile([P, PACK, width], F32, name=f"sig{width}")
+            step = width if width == HALF else FP4_NARROW
             for t in range(PACK):
                 d = psum_d.tile([P, width], F32, name="d")
                 cols = slice(t * P, (t + 1) * P)
@@ -173,88 +189,106 @@ def tile_list_pitch_control_rescale_kernel(
                         d[:],
                         lhsT=wh_codes[b, a][:, cols].bitcast(FP8X4),
                         lhsT_scale=wh_planes[b, a][:, cols],
-                        rhs=v_codes[a, half][:, start : start + width].bitcast(FP8X4),
-                        rhs_scale=v_planes[a, half][:, start : start + width],
+                        rhs=v_codes[a][:, first : first + width].bitcast(FP8X4),
+                        rhs_scale=v_plane[a][:, first : first + width],
                         start=(a == 0),
                         stop=False,
                     )
-                step = width if width == HALF else FP4_NARROW
-                for a in range(PASSES):
                     col = a * H + b * PASS + t * P
                     for n0 in range(0, width, step):
                         nc.tensor.matmul_mx(
                             d[:, n0 : n0 + step],
                             lhsT=wa_codes[:, 2 * col : 2 * (col + P)].bitcast(FP4X4),
                             lhsT_scale=wa_planes[:, col : col + P],
-                            rhs=v_codes[a, half][:, start + n0 : start + n0 + step].bitcast(FP8X4),
-                            rhs_scale=v_planes[a, half][:, start + n0 : start + n0 + step],
+                            rhs=v_codes[a][:, first + n0 : first + n0 + step].bitcast(FP8X4),
+                            rhs_scale=v_plane[a][:, first + n0 : first + n0 + step],
                             start=False,
                             stop=(a == PASSES - 1 and n0 + step == width),
                         )
                 nc.scalar.activation(sig[:, t, :], d[:], ACT.Sigmoid, bias=lead_sb[:, b, t : t + 1])
-            scaled = ring.tile([P, PACK, width], BF16, name=f"scaled{width}")
+            return sig
+
+        def gains(b, sig, space):
+            width = sig.shape[2]
+            scaled = space.bitcast(BF16)[:, : PACK * width].rearrange("p (t e) -> p t e", t=PACK)
             for t in range(PACK):
                 nc.scalar.activation(scaled[:, t, :], sig[:, t, :], ACT.Copy, scale=gain_sb[:, b, t : t + 1])
             return scaled
 
-        h_codes = {}
-        h_planes = {}
+        h_codes = [held([P, S], U32, f"h_codes{b}") for b in range(PASSES)]
+        h_planes = [held([P, S], U8, f"h_planes{b}") for b in range(PASSES)]
 
-        def quantize_h(b, c, scaled):
-            grouped = ring.tile([P, PACK * CHUNK], BF16, name="h_grouped", align_bytes=64, bufs=3)
+        def quantize_h(b, first, scaled, space=None):
+            width = scaled.shape[2]
+            if space is None:
+                space = ring.tile([P, PACK * width // 2], F32, name="h_grouped", align_bytes=64, bufs=3)[:]
+            grouped = space.bitcast(BF16)[:, : PACK * width]
             nc.scalar.copy(
-                grouped[:].rearrange("p (e i t) -> p e t i", i=4, t=PACK),
+                grouped.rearrange("p (e i t) -> p e t i", i=4, t=PACK),
                 scaled.rearrange("p t (e i) -> p e t i", i=4),
             )
-            h_codes[b, c] = held([P, CHUNK], U32, f"h_codes{b}{c}")
-            h_planes[b, c] = held([P, CHUNK], U8, f"h_planes{b}{c}")
-            nc.vector.quantize_mx(h_codes[b, c][:].bitcast(FP8X4), h_planes[b, c][:], grouped[:])
+            span = slice(first, first + width)
+            nc.vector.quantize_mx(h_codes[b][:, span].bitcast(FP8X4), h_planes[b][:, span], grouped)
 
-        picked = [held([P, S], F32, f"picked{u}") for u in range(TILES)]
-        factor = [held([P, S], F32, f"factor{u}") for u in range(TILES)]
-
-        def factors(c, u):
-            y = psum_y.tile([P, CHUNK], F32, name="y")
+        def factors(u, first, width, factor):
+            y = psum_y.tile([P, width], F32, name="y")
+            span = slice(first, first + width)
             for b in range(PASSES):
                 cols = slice(b * N + u * P, b * N + (u + 1) * P)
                 nc.tensor.matmul_mx(
                     y[:],
                     lhsT=wo_sb[:, cols].bitcast(FP8X4),
                     lhsT_scale=wo_planes[:, cols],
-                    rhs=h_codes[b, c][:].bitcast(FP8X4),
-                    rhs_scale=h_planes[b, c][:],
+                    rhs=h_codes[b][:, span].bitcast(FP8X4),
+                    rhs_scale=h_planes[b][:, span],
                     start=(b == 0),
                     stop=(b == PASSES - 1),
                 )
-            span = slice(c * CHUNK, (c + 1) * CHUNK)
-            nc.scalar.activation(factor[u][:, span], y[:], ACT.Identity, bias=bo_sb[:, u : u + 1])
+            nc.scalar.activation(factor, y[:], ACT.Identity, bias=bo_sb[:, u : u + 1])
 
-        def rescale(u, first, count):
+        def rescale(u, first, count, factor):
             span = slice(first, first + count)
             window = map_sb[u][:].indirect(entries(first, count))
-            nc.vector.tensor_tensor(window, picked[u][:, span], factor[u][:, span], MULT)
+            nc.vector.tensor_tensor(window, picked[u][:, span], factor, MULT)
 
-        def update(c):
-            for u in range(TILES):
-                factors(c, u)
-            for u in range(TILES):
-                if u < TILES - 1 or c < CHUNKS - 2:
-                    rescale(u, c * CHUNK, CHUNK)
-                elif c == CHUNKS - 1:
-                    rescale(u, (c - 1) * CHUNK, 2 * CHUNK)
+        def update(u, c, factor):
+            factors(u, c * CHUNK, CHUNK, factor)
+            rescale(u, c * CHUNK, CHUNK, factor)
 
-        for c in range(CHUNKS):
-            first = c * CHUNK
-            if first % HALF == 0:
-                scaled_wide = control(0, first, HALF)
-            quantize_h(0, c, scaled_wide[:, :, first % HALF : first % HALF + CHUNK])
-            quantize_h(1, c, control(1, first, CHUNK)[:])
-            if c == 0:
-                for u in range(TILES):
-                    nc.vector.tensor_copy(picked[u][:], map_sb[u][:].indirect(offsets[:]))
-            else:
-                update(c - 1)
-        update(CHUNKS - 1)
+        last = CHUNKS - 1
+        room = {(b, c): held([P, 3 * CHUNK], F32, f"room{b}{c}") for b in range(PASSES) for c in range(1, CHUNKS)}
+        room[0, 1] = held([P, 2 * HALF], F32, "room_wide")
+        room[1, 0] = held([P, 2 * CHUNK], F32, "room10")
+        final = held([P, (TILES - 1) * CHUNK], F32, "final")
+
+        def part(space, i, count=1):
+            return space[:, i * CHUNK : (i + count) * CHUNK]
+
+        def unit(b, c):
+            return gains(b, sigmoids(b, c * CHUNK, CHUNK), room[b, c][:])
+
+        pick(0)
+        wide = gains(0, sigmoids(0, 0, HALF), room[0, 1][:])
+        quantize_h(0, 0, wide[:, :, :CHUNK])
+        pick(1)
+        pick(2)
+        quantize_h(1, 0, unit(1, 0), picked[3][:])
+        pick(3)
+        quantize_h(0, CHUNK, wide[:, :, CHUNK:], room[1, 0][:])
+        for c in range(1, CHUNKS):
+            if c > 1:
+                quantize_h(0, c * CHUNK, unit(0, c))
+            update(0, c - 1, part(room[0, c], 0))
+            update(1, c - 1, part(room[0, c], 1))
+            quantize_h(1, c * CHUNK, unit(1, c))
+            update(2, c - 1, part(room[1, c], 0))
+            if c < last:
+                update(3, c - 1, part(room[1, c], 1))
+        factors(3, (last - 1) * CHUNK, CHUNK, part(room[1, last], 1))
+        for u in range(TILES - 1):
+            update(u, last, part(final, u))
+        factors(3, last * CHUNK, CHUNK, part(room[1, last], 2))
+        rescale(3, (last - 1) * CHUNK, 2 * CHUNK, part(room[1, last], 1, 2))
 
         for u in range(TILES):
             nc.sync.dma_start(out[u * P : (u + 1) * P, :], map_sb[u][:])

@@ -28,7 +28,7 @@ CHUNK = 256
 CHUNKS = S // CHUNK
 TILES = N // P
 FP4_NARROW = 128
-D_BANKS, Y_BANKS = 5, 3
+BANKS = 5
 
 
 def tile_list_pitch_control_rescale_kernel(
@@ -38,8 +38,12 @@ def tile_list_pitch_control_rescale_kernel(
     with ExitStack() as ctx:
         keep = ctx.enter_context(tc.tile_pool(name="keep", bufs=1))
         ring = ctx.enter_context(tc.tile_pool(name="ring", bufs=2))
-        psum_d = ctx.enter_context(tc.psum_pool(name="psum_d", bufs=D_BANKS))
-        psum_y = ctx.enter_context(tc.psum_pool(name="psum_y", bufs=Y_BANKS))
+        psum = ctx.enter_context(tc.psum_pool(name="psum", bufs=1))
+        banks = [psum.tile([P, HALF], F32, name=f"bank{i}") for i in range(BANKS)]
+
+        def next_bank():
+            banks.append(banks.pop(0))
+            return banks[-1]
 
         def held(shape, dtype, name, pool=keep):
             return pool.tile(shape, dtype, name=name, align_bytes=64)
@@ -52,7 +56,7 @@ def tile_list_pitch_control_rescale_kernel(
 
         def zeroed(width, name, pool=keep):
             planes = held([P, width], U8, name, pool)
-            nc.vector.memset(planes[:].bitcast(I32), 0)
+            nc.gpsimd.memset(planes[:].bitcast(I32), 0)
             return planes
 
         def load_planes(planes, scales):
@@ -85,27 +89,46 @@ def tile_list_pitch_control_rescale_kernel(
                 src.rearrange("p (g m t) -> p g t m", t=PACK, m=P),
             )
 
-        wa_raw = held([P, PASSES * 2 * H], U8, "wa_raw")
-        wa_codes = held([P, PASSES * 2 * H], U8, "wa_codes")
+        wa_raw = {}
+        wa_codes = {}
+        wa_planes = {}
+
+        def load_wa_words(b, pool):
+            wa_raw[b] = held([P, PASSES * 2 * PASS], U8, f"wa_raw{b}", pool)
+            nc.sync.dma_start(
+                wa_raw[b][:].bitcast(I32).rearrange("p (a w) -> p a w", a=PASSES),
+                wa_words[:, :, 2 * PASS * b : 2 * PASS * (b + 1)].bitcast(I32).rearrange("a p w -> p a w"),
+            )
+
+        def reorder_wa_words(b):
+            wa_codes[b] = held([P, PASSES * 2 * PASS], U8, f"wa_codes{b}")
+            reorder_columns(wa_codes[b][:].bitcast(U16), wa_raw[b][:].bitcast(U16))
+
+        def reorder_wa_planes(b):
+            wa_planes[b] = held([P, PASSES * PASS], U8, f"wa_planes{b}")
+            nc.vector.tensor_copy(
+                wa_planes[b][:].rearrange("p (a t m) -> p a t m", t=PACK, m=P),
+                wa_planes_raw[:].rearrange("p (a b m t) -> p b a t m", a=PASSES, b=PASSES, t=PACK)[:, b],
+            )
+
         v_plane = [held([P, S], U8, "v_plane0")]
         with tc.tile_pool(name="early", bufs=1) as early:
             tab_rows = zeroed(T, "tab_rows", early)
+            wo_planes = zeroed(PASSES * N, "wo_planes")
             wa_planes_raw = zeroed(PASSES * H, "wa_planes_raw")
             v_plane.append(zeroed(S, "v_plane1"))
-            nc.sync.dma_start(
-                wa_raw[:].bitcast(I32).rearrange("p (a w) -> p a w", a=PASSES),
-                wa_words.bitcast(I32).rearrange("a p w -> p a w"),
-            )
             for r in range(PACK):
                 nc.sync.dma_start(
                     tab_rows[r:P:QUADRANT, :].bitcast(I32), tab_scales[0, r:PLANE_ROWS:PACK, :].bitcast(I32)
                 )
             nc.sync.dma_start(tab_rows[PACK : PACK + PLANE_ROWS, :].bitcast(I32), tab_scales[1].bitcast(I32))
+            load_wa_words(0, keep)
             load_tab(0, keep)
+            load_planes(wo_planes, wo_scales)
             load_wh(0, 0, keep)
             load_planes(wa_planes_raw, wa_scales)
             load_wh(0, 1, keep)
-            reorder_columns(wa_codes[:].bitcast(U16), wa_raw[:].bitcast(U16))
+            load_tab(1, keep)
             nc.vector.tensor_copy(v_plane[0][:], tab_rows[:].indirect(offsets[:]))
         for q in range(P // QUADRANT):
             nc.sync.dma_start(
@@ -118,22 +141,20 @@ def tile_list_pitch_control_rescale_kernel(
         gain_sb = held([P, PASSES, PACK], F32, "gain_sb", late)
         bo_sb = held([P, TILES], F32, "bo_sb", late)
         wo_sb = held([P, PASSES * N], U32, "wo_sb", late)
-        load_tab(1, late)
         nc.sync.dma_start(lead_sb[:], lead.rearrange("(b p t) -> p b t", b=PASSES, t=PACK))
         load_wh(1, 0, late)
         nc.sync.dma_start(gain_sb[:], gain.rearrange("(b p t) -> p b t", b=PASSES, t=PACK))
+        load_wa_words(1, late)
         load_wh(1, 1, late)
         load_map(0, late)
         load_map(1, late)
-        load_map(2, late)
-        wo_planes = zeroed(PASSES * N, "wo_planes", late)
-        load_planes(wo_planes, wo_scales)
         nc.sync.dma_start(
             wo_sb[:].bitcast(I32).rearrange("p (b c) -> p b c", b=PASSES),
             wo_words.rearrange("b p c i -> p b (c i)").bitcast(I32),
         )
         with nc.allow_non_contiguous_dma("one bias value for each partition"):
             nc.sync.dma_start(bo_sb[:], bo.rearrange("(u p) -> p u", p=P))
+        load_map(2, late)
         load_map(3, late)
 
         v_codes = [held([P, S], U32, f"v_codes{a}") for a in range(PASSES)]
@@ -168,25 +189,26 @@ def tile_list_pitch_control_rescale_kernel(
         def pick(u):
             nc.vector.tensor_copy(picked[u][:], map_sb[u][:].indirect(offsets[:]))
 
+        reorder_wa_words(0)
         gather_words(0, 0, S)
-        wa_planes = held([P, PASSES * H], U8, "wa_planes")
-        reorder_columns(wa_planes[:], wa_planes_raw[:])
+        reorder_wa_planes(0)
         quantize_wh(0, 0)
         quantize_wh(0, 1)
         gather_words(1, 0, HALF)
         gather_words(1, HALF, HALF)
         quantize_wh(1, 0)
+        reorder_wa_words(1)
+        reorder_wa_planes(1)
         quantize_wh(1, 1)
 
-        def sigmoids(b, first, width):
-            sig = ring.tile([P, PACK, width], F32, name=f"sig{width}")
+        def sigmoids(b, first, width, sig):
             step = width if width == HALF else FP4_NARROW
             for t in range(PACK):
-                d = psum_d.tile([P, width], F32, name="d")
+                d = next_bank()[:, :width]
                 cols = slice(t * P, (t + 1) * P)
                 for a in range(PASSES):
                     nc.tensor.matmul_mx(
-                        d[:],
+                        d,
                         lhsT=wh_codes[b, a][:, cols].bitcast(FP8X4),
                         lhsT_scale=wh_planes[b, a][:, cols],
                         rhs=v_codes[a][:, first : first + width].bitcast(FP8X4),
@@ -194,57 +216,64 @@ def tile_list_pitch_control_rescale_kernel(
                         start=(a == 0),
                         stop=False,
                     )
-                    col = a * H + b * PASS + t * P
+                    col = a * PASS + t * P
                     for n0 in range(0, width, step):
                         nc.tensor.matmul_mx(
                             d[:, n0 : n0 + step],
-                            lhsT=wa_codes[:, 2 * col : 2 * (col + P)].bitcast(FP4X4),
-                            lhsT_scale=wa_planes[:, col : col + P],
+                            lhsT=wa_codes[b][:, 2 * col : 2 * (col + P)].bitcast(FP4X4),
+                            lhsT_scale=wa_planes[b][:, col : col + P],
                             rhs=v_codes[a][:, first + n0 : first + n0 + step].bitcast(FP8X4),
                             rhs_scale=v_plane[a][:, first + n0 : first + n0 + step],
                             start=False,
                             stop=(a == PASSES - 1 and n0 + step == width),
                         )
-                nc.scalar.activation(sig[:, t, :], d[:], ACT.Sigmoid, bias=lead_sb[:, b, t : t + 1])
-            return sig
+                nc.scalar.activation(sig[:, t, :], d, ACT.Sigmoid, bias=lead_sb[:, b, t : t + 1])
 
-        def gains(b, sig, space):
+        def gains(b, sig, room):
             width = sig.shape[2]
-            scaled = space.bitcast(BF16)[:, : PACK * width].rearrange("p (t e) -> p t e", t=PACK)
+            scaled = room[:, : PACK * width].rearrange("p (t e) -> p t e", t=PACK)
             for t in range(PACK):
                 nc.scalar.activation(scaled[:, t, :], sig[:, t, :], ACT.Copy, scale=gain_sb[:, b, t : t + 1])
             return scaled
 
-        h_codes = [held([P, S], U32, f"h_codes{b}") for b in range(PASSES)]
-        h_planes = [held([P, S], U8, f"h_planes{b}") for b in range(PASSES)]
+        grouped = [held([P, PASSES, PACK * CHUNK], BF16, f"grouped{c}") for c in range(CHUNKS)]
+        h_codes = [held([P, PASSES * CHUNK], U32, f"h_codes{c}")[:] for c in range(CHUNKS)]
+        h_planes = [held([P, PASSES * CHUNK], U8, f"h_planes{c}") for c in range(CHUNKS)]
 
-        def quantize_h(b, first, scaled, space=None):
-            width = scaled.shape[2]
-            if space is None:
-                space = ring.tile([P, PACK * width // 2], F32, name="h_grouped", align_bytes=64, bufs=3)[:]
-            grouped = space.bitcast(BF16)[:, : PACK * width]
+        def interleave(b, c, scaled):
             nc.scalar.copy(
-                grouped.rearrange("p (e i t) -> p e t i", i=4, t=PACK),
+                grouped[c][:, b, :].rearrange("p (e i t) -> p e t i", i=4, t=PACK),
                 scaled.rearrange("p t (e i) -> p e t i", i=4),
             )
-            span = slice(first, first + width)
-            nc.vector.quantize_mx(h_codes[b][:, span].bitcast(FP8X4), h_planes[b][:, span], grouped)
 
-        def factors(u, first, width, factor):
-            y = psum_y.tile([P, width], F32, name="y")
-            span = slice(first, first + width)
+        def scale_and_interleave(b, c, sig):
+            nc.vector.tensor_tensor(
+                grouped[c][:, b, :].rearrange("p (e i t) -> p e t i", i=4, t=PACK),
+                sig.rearrange("p t (e i) -> p e t i", i=4),
+                gain_sb[:, b, :].unsqueeze(1).unsqueeze(3).to_broadcast([P, CHUNK // 4, PACK, 4]),
+                MULT,
+            )
+
+        def quantize_h(c):
+            nc.vector.quantize_mx(
+                h_codes[c].bitcast(FP8X4), h_planes[c][:], grouped[c][:].rearrange("p b w -> p (b w)")
+            )
+
+        def factors(u, c, factor):
+            y = next_bank()[:, :CHUNK]
             for b in range(PASSES):
                 cols = slice(b * N + u * P, b * N + (u + 1) * P)
+                span = slice(b * CHUNK, (b + 1) * CHUNK)
                 nc.tensor.matmul_mx(
-                    y[:],
+                    y,
                     lhsT=wo_sb[:, cols].bitcast(FP8X4),
                     lhsT_scale=wo_planes[:, cols],
-                    rhs=h_codes[b][:, span].bitcast(FP8X4),
-                    rhs_scale=h_planes[b][:, span],
+                    rhs=h_codes[c][:, span].bitcast(FP8X4),
+                    rhs_scale=h_planes[c][:, span],
                     start=(b == 0),
                     stop=(b == PASSES - 1),
                 )
-            nc.scalar.activation(factor, y[:], ACT.Identity, bias=bo_sb[:, u : u + 1])
+            nc.scalar.activation(factor, y, ACT.Identity, bias=bo_sb[:, u : u + 1])
 
         def rescale(u, first, count, factor):
             span = slice(first, first + count)
@@ -252,43 +281,63 @@ def tile_list_pitch_control_rescale_kernel(
             nc.vector.tensor_tensor(window, picked[u][:, span], factor, MULT)
 
         def update(u, c, factor):
-            factors(u, c * CHUNK, CHUNK, factor)
+            factors(u, c, factor)
             rescale(u, c * CHUNK, CHUNK, factor)
 
-        last = CHUNKS - 1
-        room = {(b, c): held([P, 3 * CHUNK], F32, f"room{b}{c}") for b in range(PASSES) for c in range(1, CHUNKS)}
-        room[0, 1] = held([P, 2 * HALF], F32, "room_wide")
-        room[1, 0] = held([P, 2 * CHUNK], F32, "room10")
+        def part(room, i, count=1):
+            return room[:, i * CHUNK : (i + count) * CHUNK]
+
+        sig_wide = held([P, PACK, HALF], F32, "sig_wide")
+        sig = [held([P, PACK, CHUNK], F32, f"sig{i}") for i in range(2)]
+        first_factors = held([P, TILES * CHUNK], F32, "first_factors")[:]
         final = held([P, (TILES - 1) * CHUNK], F32, "final")
 
-        def part(space, i, count=1):
-            return space[:, i * CHUNK : (i + count) * CHUNK]
+        def begin(b, c):
+            sig.reverse()
+            sigmoids(b, c * CHUNK, CHUNK, sig[0])
 
-        def unit(b, c):
-            return gains(b, sigmoids(b, c * CHUNK, CHUNK), room[b, c][:])
+        def finish(b, c, room):
+            interleave(b, c, gains(b, sig[0], room))
+
+        def unit(b, c, room):
+            begin(b, c)
+            finish(b, c, room)
 
         pick(0)
-        wide = gains(0, sigmoids(0, 0, HALF), room[0, 1][:])
-        quantize_h(0, 0, wide[:, :, :CHUNK])
         pick(1)
+        sigmoids(0, 0, HALF, sig_wide)
+        wide = gains(0, sig_wide, first_factors.bitcast(BF16))
+        interleave(0, 0, wide[:, :, :CHUNK])
+        unit(1, 0, grouped[1][:, 0, :])
+        quantize_h(0)
         pick(2)
-        quantize_h(1, 0, unit(1, 0), picked[3][:])
         pick(3)
-        quantize_h(0, CHUNK, wide[:, :, CHUNK:], room[1, 0][:])
-        for c in range(1, CHUNKS):
-            if c > 1:
-                quantize_h(0, c * CHUNK, unit(0, c))
-            update(0, c - 1, part(room[0, c], 0))
-            update(1, c - 1, part(room[0, c], 1))
-            quantize_h(1, c * CHUNK, unit(1, c))
-            update(2, c - 1, part(room[1, c], 0))
-            if c < last:
-                update(3, c - 1, part(room[1, c], 1))
-        factors(3, (last - 1) * CHUNK, CHUNK, part(room[1, last], 1))
+        interleave(0, 1, wide[:, :, CHUNK:])
+        begin(1, 1)
+        update(2, 0, part(first_factors, 0))
+        update(3, 0, part(first_factors, 1))
+        room = held([P, 2 * CHUNK], F32, "room11")[:]
+        finish(1, 1, room.bitcast(BF16))
+        quantize_h(1)
+        update(0, 0, part(room, 0))
+        update(1, 0, part(room, 1))
+        for c in range(2, CHUNKS):
+            room = held([P, 2 * CHUNK], F32, f"room0{c}")[:]
+            unit(0, c, room.bitcast(BF16))
+            begin(1, c)
+            update(0, c - 1, part(room, 0))
+            update(1, c - 1, part(room, 1))
+            room = held([P, 3 * CHUNK], F32, f"room1{c}")[:]
+            finish(1, c, room.bitcast(BF16))
+            quantize_h(c)
+            update(2, c - 1, part(room, 0))
+            if c < CHUNKS - 1:
+                update(3, c - 1, part(room, 1))
+        factors(3, c - 1, part(room, 1))
         for u in range(TILES - 1):
-            update(u, last, part(final, u))
-        factors(3, last * CHUNK, CHUNK, part(room[1, last], 2))
-        rescale(3, (last - 1) * CHUNK, 2 * CHUNK, part(room[1, last], 1, 2))
+            update(u, c, part(final, u))
+        factors(3, c, part(room, 2))
+        rescale(3, (c - 1) * CHUNK, 2 * CHUNK, part(room, 1, 2))
 
         for u in range(TILES):
             nc.sync.dma_start(out[u * P : (u + 1) * P, :], map_sb[u][:])

@@ -59,10 +59,10 @@ def tile_list_pitch_control_rescale_kernel(
             nc.gpsimd.memset(planes[:].bitcast(I32), 0)
             return planes
 
-        def load_planes(planes, scales):
+        def load_planes(planes, scales, row0=0):
             for r in range(PACK):
                 nc.sync.dma_start(
-                    planes[r:P:QUADRANT, :].bitcast(I32).rearrange("q (a w) -> q a w", a=PASSES),
+                    planes[row0 + r : P : QUADRANT, :].bitcast(I32).rearrange("q (a w) -> q a w", a=PASSES),
                     scales[:, r:PLANE_ROWS:PACK, :].bitcast(I32).rearrange("a q w -> q a w"),
                 )
 
@@ -79,8 +79,8 @@ def tile_list_pitch_control_rescale_kernel(
             rows = wh[a * PASS : (a + 1) * PASS, b * PASS : (b + 1) * PASS]
             nc.sync.dma_start(wh_raw[b, a][:], rows.rearrange("(p j) c -> p j c", j=PACK))
 
-        def load_map(u, pool):
-            map_sb[u] = held([P, T], F32, f"map_sb{u}", pool)
+        def load_map(u, pool, name):
+            map_sb[u] = held([P, T], F32, name, pool)
             nc.sync.dma_start(map_sb[u][:], gT[u * P : (u + 1) * P, :])
 
         def reorder_columns(dst, src):
@@ -114,7 +114,6 @@ def tile_list_pitch_control_rescale_kernel(
         v_plane = [held([P, S], U8, "v_plane0")]
         with tc.tile_pool(name="early", bufs=1) as early:
             tab_rows = zeroed(T, "tab_rows", early)
-            wo_planes = zeroed(PASSES * N, "wo_planes")
             wa_planes_raw = zeroed(PASSES * H, "wa_planes_raw")
             v_plane.append(zeroed(S, "v_plane1"))
             for r in range(PACK):
@@ -124,7 +123,6 @@ def tile_list_pitch_control_rescale_kernel(
             nc.sync.dma_start(tab_rows[PACK : PACK + PLANE_ROWS, :].bitcast(I32), tab_scales[1].bitcast(I32))
             load_wa_words(0, keep)
             load_tab(0, keep)
-            load_planes(wo_planes, wo_scales)
             load_wh(0, 0, keep)
             load_planes(wa_planes_raw, wa_scales)
             load_wh(0, 1, keep)
@@ -140,22 +138,15 @@ def tile_list_pitch_control_rescale_kernel(
         lead_sb = held([P, PASSES, PACK], F32, "lead_sb", late)
         gain_sb = held([P, PASSES, PACK], F32, "gain_sb", late)
         bo_sb = held([P, TILES], F32, "bo_sb", late)
-        wo_sb = held([P, PASSES * N], U32, "wo_sb", late)
         nc.sync.dma_start(lead_sb[:], lead.rearrange("(b p t) -> p b t", b=PASSES, t=PACK))
         load_wh(1, 0, late)
         nc.sync.dma_start(gain_sb[:], gain.rearrange("(b p t) -> p b t", b=PASSES, t=PACK))
         load_wa_words(1, late)
         load_wh(1, 1, late)
-        load_map(0, late)
-        load_map(1, late)
-        nc.sync.dma_start(
-            wo_sb[:].bitcast(I32).rearrange("p (b c) -> p b c", b=PASSES),
-            wo_words.rearrange("b p c i -> p b (c i)").bitcast(I32),
-        )
         with nc.allow_non_contiguous_dma("one bias value for each partition"):
             nc.sync.dma_start(bo_sb[:], bo.rearrange("(u p) -> p u", p=P))
-        load_map(2, late)
-        load_map(3, late)
+        for u in range(TILES - 1):
+            load_map(u, late, f"map_sb{u}")
 
         v_codes = [held([P, S], U32, f"v_codes{a}") for a in range(PASSES)]
 
@@ -201,6 +192,16 @@ def tile_list_pitch_control_rescale_kernel(
         reorder_wa_planes(1)
         quantize_wh(1, 1)
 
+        shared_planes = wa_planes_raw[:, : PASSES * N]
+        load_planes(shared_planes, wo_scales, PACK)
+        wo_planes = shared_planes[PACK:P, :]
+        load_map(TILES - 1, keep, "wh_raw00")
+        wo_sb = held([P, PASSES * N], U32, "wh_raw01")
+        nc.sync.dma_start(
+            wo_sb[:].bitcast(I32).rearrange("p (b c) -> p b c", b=PASSES),
+            wo_words.rearrange("b p c i -> p b (c i)").bitcast(I32),
+        )
+
         def sigmoids(b, first, width, sig):
             step = width if width == HALF else FP4_NARROW
             for t in range(PACK):
@@ -238,7 +239,8 @@ def tile_list_pitch_control_rescale_kernel(
 
         grouped = [held([P, PASSES, PACK * CHUNK], BF16, f"grouped{c}") for c in range(CHUNKS)]
         h_codes = [held([P, PASSES * CHUNK], U32, f"h_codes{c}")[:] for c in range(CHUNKS)]
-        h_planes = [held([P, PASSES * CHUNK], U8, f"h_planes{c}") for c in range(CHUNKS)]
+        h_planes = [shared_planes[:, c * PASSES * CHUNK : (c + 1) * PASSES * CHUNK] for c in range(2)]
+        h_planes += [held([P, PASSES * CHUNK], U8, f"h_planes{c}")[:] for c in range(2, CHUNKS)]
 
         def interleave(b, c, scaled):
             nc.scalar.copy(
@@ -256,7 +258,7 @@ def tile_list_pitch_control_rescale_kernel(
 
         def quantize_h(c):
             nc.vector.quantize_mx(
-                h_codes[c].bitcast(FP8X4), h_planes[c][:], grouped[c][:].rearrange("p b w -> p (b w)")
+                h_codes[c].bitcast(FP8X4), h_planes[c], grouped[c][:].rearrange("p b w -> p (b w)")
             )
 
         def factors(u, c, factor):
@@ -309,18 +311,18 @@ def tile_list_pitch_control_rescale_kernel(
         wide = gains(0, sig_wide, first_factors.bitcast(BF16))
         interleave(0, 0, wide[:, :, :CHUNK])
         unit(1, 0, grouped[1][:, 0, :])
-        quantize_h(0)
         pick(2)
+        quantize_h(0)
         pick(3)
         interleave(0, 1, wide[:, :, CHUNK:])
         begin(1, 1)
-        update(2, 0, part(first_factors, 0))
-        update(3, 0, part(first_factors, 1))
+        update(0, 0, part(first_factors, 0))
+        update(1, 0, part(first_factors, 1))
         room = held([P, 2 * CHUNK], F32, "room11")[:]
         finish(1, 1, room.bitcast(BF16))
         quantize_h(1)
-        update(0, 0, part(room, 0))
-        update(1, 0, part(room, 1))
+        update(2, 0, part(room, 0))
+        update(3, 0, part(room, 1))
         for c in range(2, CHUNKS):
             room = held([P, 2 * CHUNK], F32, f"room0{c}")[:]
             unit(0, c, room.bitcast(BF16))

@@ -56,7 +56,7 @@ def tile_list_pitch_control_rescale_kernel(
 
         def zeroed(width, name, pool=keep):
             planes = held([P, width], U8, name, pool)
-            nc.gpsimd.memset(planes[:].bitcast(I32), 0)
+            nc.vector.memset(planes[:].bitcast(I32), 0)
             return planes
 
         def load_planes(planes, scales, row0=0):
@@ -237,7 +237,7 @@ def tile_list_pitch_control_rescale_kernel(
                 nc.scalar.activation(scaled[:, t, :], sig[:, t, :], ACT.Copy, scale=gain_sb[:, b, t : t + 1])
             return scaled
 
-        grouped = [held([P, PASSES, PACK * CHUNK], BF16, f"grouped{c}") for c in range(CHUNKS)]
+        grouped = [held([P, PASSES + 1, PACK * CHUNK], BF16, f"grouped{c}") for c in range(CHUNKS)]
         h_codes = [held([P, PASSES * CHUNK], U32, f"h_codes{c}")[:] for c in range(CHUNKS)]
         h_planes = [shared_planes[:, c * PASSES * CHUNK : (c + 1) * PASSES * CHUNK] for c in range(2)]
         h_planes += [held([P, PASSES * CHUNK], U8, f"h_planes{c}")[:] for c in range(2, CHUNKS)]
@@ -258,7 +258,7 @@ def tile_list_pitch_control_rescale_kernel(
 
         def quantize_h(c):
             nc.vector.quantize_mx(
-                h_codes[c].bitcast(FP8X4), h_planes[c], grouped[c][:].rearrange("p b w -> p (b w)")
+                h_codes[c].bitcast(FP8X4), h_planes[c], grouped[c][:, :PASSES, :].rearrange("p b w -> p (b w)")
             )
 
         def factors(u, c, factor):
@@ -310,16 +310,24 @@ def tile_list_pitch_control_rescale_kernel(
         sigmoids(0, 0, HALF, sig_wide)
         wide = gains(0, sig_wide, first_factors.bitcast(BF16))
         interleave(0, 0, wide[:, :, :CHUNK])
-        unit(1, 0, grouped[1][:, 0, :])
+        sigmoids(1, 0, HALF, sig_wide)
+        halves = grouped[1][:, 0 : PASSES + 1 : PASSES, :]
+        for t in range(PACK):
+            nc.scalar.activation(
+                halves[:, :, t * CHUNK : (t + 1) * CHUNK],
+                sig_wide[:, t, :].rearrange("p (c e) -> p c e", c=2),
+                ACT.Copy,
+                scale=gain_sb[:, 1, t : t + 1],
+            )
+        interleave(1, 0, halves[:, 0, :].rearrange("p (t e) -> p t e", t=PACK))
         pick(2)
         quantize_h(0)
         pick(3)
         interleave(0, 1, wide[:, :, CHUNK:])
-        begin(1, 1)
         update(0, 0, part(first_factors, 0))
         update(1, 0, part(first_factors, 1))
-        room = held([P, 2 * CHUNK], F32, "room11")[:]
-        finish(1, 1, room.bitcast(BF16))
+        interleave(1, 1, halves[:, 1, :].rearrange("p (t e) -> p t e", t=PACK))
+        room = halves[:, 1, :].bitcast(F32)
         quantize_h(1)
         update(2, 0, part(room, 0))
         update(3, 0, part(room, 1))

@@ -54,9 +54,9 @@ def tile_list_pitch_control_rescale_kernel(
         def entries(first, count):
             return offsets[:, first // PER_COLUMN : (first + count) // PER_COLUMN]
 
-        def zeroed(width, name, pool=keep):
+        def zeroed(engine, width, name, pool=keep):
             planes = held([P, width], U8, name, pool)
-            nc.vector.memset(planes[:].bitcast(I32), 0)
+            engine.memset(planes[:].bitcast(I32), 0)
             return planes
 
         def load_planes(planes, scales, row0=0):
@@ -91,7 +91,6 @@ def tile_list_pitch_control_rescale_kernel(
 
         wa_raw = {}
         wa_codes = {}
-        wa_planes = {}
 
         def load_wa_words(b, pool):
             wa_raw[b] = held([P, PASSES * 2 * PASS], U8, f"wa_raw{b}", pool)
@@ -104,18 +103,16 @@ def tile_list_pitch_control_rescale_kernel(
             wa_codes[b] = held([P, PASSES * 2 * PASS], U8, f"wa_codes{b}")
             reorder_columns(wa_codes[b][:].bitcast(U16), wa_raw[b][:].bitcast(U16))
 
-        def reorder_wa_planes(b):
-            wa_planes[b] = held([P, PASSES * PASS], U8, f"wa_planes{b}")
-            nc.vector.tensor_copy(
-                wa_planes[b][:].rearrange("p (a t m) -> p a t m", t=PACK, m=P),
-                wa_planes_raw[:].rearrange("p (a b m t) -> p b a t m", a=PASSES, b=PASSES, t=PACK)[:, b],
-            )
+        def reorder_wa_planes():
+            ordered = held([P, PASSES * H], U8, "wa_planes")
+            reorder_columns(ordered[:], wa_planes_raw[:])
+            return ordered
 
         v_plane = [held([P, S], U8, "v_plane0")]
         with tc.tile_pool(name="early", bufs=1) as early:
-            tab_rows = zeroed(T, "tab_rows", early)
-            wa_planes_raw = zeroed(PASSES * H, "wa_planes_raw")
-            v_plane.append(zeroed(S, "v_plane1"))
+            tab_rows = zeroed(nc.gpsimd, T, "tab_rows", early)
+            wa_planes_raw = zeroed(nc.vector, PASSES * H, "wa_planes_raw")
+            v_plane.append(zeroed(nc.gpsimd, S, "v_plane1"))
             for r in range(PACK):
                 nc.sync.dma_start(
                     tab_rows[r:P:QUADRANT, :].bitcast(I32), tab_scales[0, r:PLANE_ROWS:PACK, :].bitcast(I32)
@@ -123,10 +120,9 @@ def tile_list_pitch_control_rescale_kernel(
             nc.sync.dma_start(tab_rows[PACK : PACK + PLANE_ROWS, :].bitcast(I32), tab_scales[1].bitcast(I32))
             load_wa_words(0, keep)
             load_tab(0, keep)
-            load_wh(0, 0, keep)
             load_planes(wa_planes_raw, wa_scales)
+            load_wh(0, 0, keep)
             load_wh(0, 1, keep)
-            load_tab(1, keep)
             nc.vector.tensor_copy(v_plane[0][:], tab_rows[:].indirect(offsets[:]))
         for q in range(P // QUADRANT):
             nc.sync.dma_start(
@@ -138,15 +134,16 @@ def tile_list_pitch_control_rescale_kernel(
         lead_sb = held([P, PASSES, PACK], F32, "lead_sb", late)
         gain_sb = held([P, PASSES, PACK], F32, "gain_sb", late)
         bo_sb = held([P, TILES], F32, "bo_sb", late)
+        load_tab(1, late)
         nc.sync.dma_start(lead_sb[:], lead.rearrange("(b p t) -> p b t", b=PASSES, t=PACK))
         load_wh(1, 0, late)
         nc.sync.dma_start(gain_sb[:], gain.rearrange("(b p t) -> p b t", b=PASSES, t=PACK))
         load_wa_words(1, late)
         load_wh(1, 1, late)
-        with nc.allow_non_contiguous_dma("one bias value for each partition"):
-            nc.sync.dma_start(bo_sb[:], bo.rearrange("(u p) -> p u", p=P))
         for u in range(TILES - 1):
             load_map(u, late, f"map_sb{u}")
+        with nc.allow_non_contiguous_dma("one bias value for each partition"):
+            nc.sync.dma_start(bo_sb[:], bo.rearrange("(u p) -> p u", p=P))
 
         v_codes = [held([P, S], U32, f"v_codes{a}") for a in range(PASSES)]
 
@@ -157,14 +154,15 @@ def tile_list_pitch_control_rescale_kernel(
         wh_planes = {}
 
         def quantize_wh(b, a):
-            grouped = ring.tile([P, PACK * PASS], BF16, name="wh_grouped", align_bytes=64)
-            dst = grouped[:].rearrange("p (t m j) -> p m j t", t=PACK, j=PACK)
+            grouped = {}
             src = wh_raw[b, a][:].rearrange("p j (m t) -> p m j t", t=PACK)
             for t in range(0, PACK, 2):
-                if (b, a) == (0, 0) or (b, a, t) == (0, 1, 0):
-                    nc.scalar.activation(dst[:, :, :, t : t + 2], src[:, :, :, t : t + 2], ACT.Copy, scale=-1.0)
+                grouped[t] = ring.tile([P, 2 * PASS], BF16, name=f"wh_grouped{t}", align_bytes=64)
+                dst = grouped[t][:].rearrange("p (t m j) -> p m j t", t=2, j=PACK)
+                if b == 0:
+                    nc.scalar.activation(dst, src[:, :, :, t : t + 2], ACT.Copy, scale=-1.0)
                 else:
-                    nc.vector.tensor_scalar_mul(dst[:, :, :, t : t + 2], src[:, :, :, t : t + 2], -1.0)
+                    nc.vector.tensor_scalar_mul(dst, src[:, :, :, t : t + 2], -1.0)
             wh_codes[b, a] = held([P, PASS], U32, f"wh_codes{b}{a}")
             wh_planes[b, a] = held([P, PASS], U8, f"wh_planes{b}{a}")
             for t in range(0, PACK, 2):
@@ -172,7 +170,7 @@ def tile_list_pitch_control_rescale_kernel(
                 nc.vector.quantize_mx(
                     wh_codes[b, a][:, cols].bitcast(FP8X4),
                     wh_planes[b, a][:, cols],
-                    grouped[:, t * PASS : (t + 2) * PASS],
+                    grouped[t][:],
                 )
 
         picked = [held([P, S], F32, f"picked{u}") for u in range(TILES)]
@@ -182,14 +180,13 @@ def tile_list_pitch_control_rescale_kernel(
 
         reorder_wa_words(0)
         gather_words(0, 0, S)
-        reorder_wa_planes(0)
+        wa_planes = reorder_wa_planes()
         quantize_wh(0, 0)
         quantize_wh(0, 1)
         gather_words(1, 0, HALF)
         gather_words(1, HALF, HALF)
         quantize_wh(1, 0)
         reorder_wa_words(1)
-        reorder_wa_planes(1)
         quantize_wh(1, 1)
 
         shared_planes = wa_planes_raw[:, : PASSES * N]
@@ -207,7 +204,8 @@ def tile_list_pitch_control_rescale_kernel(
             for t in range(PACK):
                 d = next_bank()[:, :width]
                 cols = slice(t * P, (t + 1) * P)
-                for a in range(PASSES):
+
+                def home(a):
                     nc.tensor.matmul_mx(
                         d,
                         lhsT=wh_codes[b, a][:, cols].bitcast(FP8X4),
@@ -215,19 +213,23 @@ def tile_list_pitch_control_rescale_kernel(
                         rhs=v_codes[a][:, first : first + width].bitcast(FP8X4),
                         rhs_scale=v_plane[a][:, first : first + width],
                         start=(a == 0),
-                        stop=False,
+                        stop=(a == PASSES - 1),
                     )
+
+                home(0)
+                for a in range(PASSES):
                     col = a * PASS + t * P
                     for n0 in range(0, width, step):
                         nc.tensor.matmul_mx(
                             d[:, n0 : n0 + step],
                             lhsT=wa_codes[b][:, 2 * col : 2 * (col + P)].bitcast(FP4X4),
-                            lhsT_scale=wa_planes[b][:, col : col + P],
+                            lhsT_scale=wa_planes[:, a * H + b * PASS + t * P : a * H + b * PASS + (t + 1) * P],
                             rhs=v_codes[a][:, first + n0 : first + n0 + step].bitcast(FP8X4),
                             rhs_scale=v_plane[a][:, first + n0 : first + n0 + step],
                             start=False,
-                            stop=(a == PASSES - 1 and n0 + step == width),
+                            stop=False,
                         )
+                home(1)
                 nc.scalar.activation(sig[:, t, :], d, ACT.Sigmoid, bias=lead_sb[:, b, t : t + 1])
 
         def gains(b, sig, room):

@@ -28,7 +28,7 @@ CHUNK = 256
 CHUNKS = S // CHUNK
 TILES = N // P
 FP4_NARROW = 128
-BANKS = 5
+BANKS = 8
 
 
 def tile_list_pitch_control_rescale_kernel(
@@ -38,12 +38,9 @@ def tile_list_pitch_control_rescale_kernel(
     with ExitStack() as ctx:
         keep = ctx.enter_context(tc.tile_pool(name="keep", bufs=1))
         ring = ctx.enter_context(tc.tile_pool(name="ring", bufs=2))
+        laid = ctx.enter_context(tc.tile_pool(name="laid", bufs=1))
         psum = ctx.enter_context(tc.psum_pool(name="psum", bufs=1))
         banks = [psum.tile([P, HALF], F32, name=f"bank{i}") for i in range(BANKS)]
-
-        def next_bank():
-            banks.append(banks.pop(0))
-            return banks[-1]
 
         def held(shape, dtype, name, pool=keep):
             return pool.tile(shape, dtype, name=name, align_bytes=64)
@@ -121,6 +118,8 @@ def tile_list_pitch_control_rescale_kernel(
             load_wa_words(0, keep)
             load_tab(0, keep)
             load_planes(wa_planes_raw, wa_scales)
+            lead_sb = held([P, PASSES, PACK], F32, "lead_sb")
+            nc.sync.dma_start(lead_sb[:], lead.rearrange("(b p t) -> p b t", b=PASSES, t=PACK))
             load_wh(0, 0, keep)
             load_wh(0, 1, keep)
             nc.vector.tensor_copy(v_plane[0][:], tab_rows[:].indirect(offsets[:]))
@@ -131,11 +130,9 @@ def tile_list_pitch_control_rescale_kernel(
             )
 
         late = ctx.enter_context(tc.tile_pool(name="late", bufs=1))
-        lead_sb = held([P, PASSES, PACK], F32, "lead_sb", late)
         gain_sb = held([P, PASSES, PACK], F32, "gain_sb", late)
         bo_sb = held([P, TILES], F32, "bo_sb", late)
         load_tab(1, late)
-        nc.sync.dma_start(lead_sb[:], lead.rearrange("(b p t) -> p b t", b=PASSES, t=PACK))
         load_wh(1, 0, late)
         nc.sync.dma_start(gain_sb[:], gain.rearrange("(b p t) -> p b t", b=PASSES, t=PACK))
         load_wa_words(1, late)
@@ -145,10 +142,13 @@ def tile_list_pitch_control_rescale_kernel(
         with nc.allow_non_contiguous_dma("one bias value for each partition"):
             nc.sync.dma_start(bo_sb[:], bo.rearrange("(u p) -> p u", p=P))
 
-        v_codes = [held([P, S], U32, f"v_codes{a}") for a in range(PASSES)]
+        v_codes = {}
 
         def gather_words(a, first, count):
-            nc.vector.tensor_copy(v_codes[a][:, first : first + count], tab_sb[a][:].indirect(entries(first, count)))
+            words = held([P, count], U32, f"v_codes{a}{first}")
+            nc.vector.tensor_copy(words[:], tab_sb[a][:].indirect(entries(first, count)))
+            for e in range(0, count, FP4_NARROW):
+                v_codes[a, first + e] = words[:, e:]
 
         wh_codes = {}
         wh_planes = {}
@@ -157,9 +157,12 @@ def tile_list_pitch_control_rescale_kernel(
             grouped = {}
             src = wh_raw[b, a][:].rearrange("p j (m t) -> p m j t", t=PACK)
             for t in range(0, PACK, 2):
-                grouped[t] = ring.tile([P, 2 * PASS], BF16, name=f"wh_grouped{t}", align_bytes=64)
+                if (b, a, t) == (1, 1, 2):
+                    grouped[t] = laid.tile([P, 2 * PASS], BF16, name="last_grouped", align_bytes=64, offset=3072)
+                else:
+                    grouped[t] = ring.tile([P, 2 * PASS], BF16, name=f"wh_grouped{t}", align_bytes=64)
                 dst = grouped[t][:].rearrange("p (t m j) -> p m j t", t=2, j=PACK)
-                if b == 0:
+                if (b, a) == (0, 0) or (b, a, t) == (0, 1, 0):
                     nc.scalar.activation(dst, src[:, :, :, t : t + 2], ACT.Copy, scale=-1.0)
                 else:
                     nc.vector.tensor_scalar_mul(dst, src[:, :, :, t : t + 2], -1.0)
@@ -199,10 +202,11 @@ def tile_list_pitch_control_rescale_kernel(
             wo_words.rearrange("b p c i -> p b (c i)").bitcast(I32),
         )
 
-        def sigmoids(b, first, width, sig):
+        def sums(b, first, width, bank0):
             step = width if width == HALF else FP4_NARROW
+            span = slice(first, first + width)
             for t in range(PACK):
-                d = next_bank()[:, :width]
+                d = banks[bank0 + t][:, :width]
                 cols = slice(t * P, (t + 1) * P)
 
                 def home(a):
@@ -210,61 +214,79 @@ def tile_list_pitch_control_rescale_kernel(
                         d,
                         lhsT=wh_codes[b, a][:, cols].bitcast(FP8X4),
                         lhsT_scale=wh_planes[b, a][:, cols],
-                        rhs=v_codes[a][:, first : first + width].bitcast(FP8X4),
-                        rhs_scale=v_plane[a][:, first : first + width],
-                        start=(a == 0),
+                        rhs=v_codes[a, first][:, :width].bitcast(FP8X4),
+                        rhs_scale=v_plane[a][:, span],
+                        start=(a == 0 and width != HALF),
                         stop=(a == PASSES - 1),
                     )
 
-                home(0)
-                for a in range(PASSES):
+                def away(a):
                     col = a * PASS + t * P
                     for n0 in range(0, width, step):
                         nc.tensor.matmul_mx(
                             d[:, n0 : n0 + step],
                             lhsT=wa_codes[b][:, 2 * col : 2 * (col + P)].bitcast(FP4X4),
                             lhsT_scale=wa_planes[:, a * H + b * PASS + t * P : a * H + b * PASS + (t + 1) * P],
-                            rhs=v_codes[a][:, first + n0 : first + n0 + step].bitcast(FP8X4),
+                            rhs=v_codes[a, first + n0][:, :step].bitcast(FP8X4),
                             rhs_scale=v_plane[a][:, first + n0 : first + n0 + step],
-                            start=False,
+                            start=(a == 0 and width == HALF),
                             stop=False,
                         )
+
+                for product in (away, home) if width == HALF else (home, away):
+                    product(0)
+                away(1)
                 home(1)
-                nc.scalar.activation(sig[:, t, :], d, ACT.Sigmoid, bias=lead_sb[:, b, t : t + 1])
 
-        def gains(b, sig, room):
-            width = sig.shape[2]
-            scaled = room[:, : PACK * width].rearrange("p (t e) -> p t e", t=PACK)
+        def sigmoids(b, width, bank0, name, first=0):
+            sig = held([P, PACK, width], F32, name)
             for t in range(PACK):
-                nc.scalar.activation(scaled[:, t, :], sig[:, t, :], ACT.Copy, scale=gain_sb[:, b, t : t + 1])
-            return scaled
+                nc.scalar.activation(
+                    sig[:, t, :], banks[bank0 + t][:, first : first + width], ACT.Sigmoid, bias=lead_sb[:, b, t : t + 1]
+                )
+            return [sig[:, :, e : e + CHUNK] for e in range(0, width, CHUNK)]
 
-        grouped = [held([P, PASSES + 1, PACK * CHUNK], BF16, f"grouped{c}") for c in range(CHUNKS)]
+        grouped = [
+            laid.tile([P, PASSES * PACK * CHUNK], BF16, name=f"grouped{c}", align_bytes=64, offset=4096 * c)[:]
+            for c in range(2)
+        ]
         h_codes = [held([P, PASSES * CHUNK], U32, f"h_codes{c}")[:] for c in range(CHUNKS)]
         h_planes = [shared_planes[:, c * PASSES * CHUNK : (c + 1) * PASSES * CHUNK] for c in range(2)]
         h_planes += [held([P, PASSES * CHUNK], U8, f"h_planes{c}")[:] for c in range(2, CHUNKS)]
 
+        def operand(b, c):
+            return grouped[c][:, b * PACK * CHUNK : (b + 1) * PACK * CHUNK]
+
+        def gains(b, sig, room):
+            scaled = room.bitcast(BF16)[:, : PACK * CHUNK].rearrange("p (t e) -> p t e", t=PACK)
+            for t in range(PACK):
+                nc.scalar.activation(
+                    scaled[:, t, :], sig[:, t, :], ACT.Copy, scale=gain_sb[:, b, t : t + 1]
+                )
+            return scaled
+
         def interleave(b, c, scaled):
             nc.scalar.copy(
-                grouped[c][:, b, :].rearrange("p (e i t) -> p e t i", i=4, t=PACK),
+                operand(b, c).rearrange("p (e i t) -> p e t i", i=4, t=PACK),
                 scaled.rearrange("p t (e i) -> p e t i", i=4),
             )
 
-        def scale_and_interleave(b, c, sig):
-            nc.vector.tensor_tensor(
-                grouped[c][:, b, :].rearrange("p (e i t) -> p e t i", i=4, t=PACK),
-                sig.rearrange("p t (e i) -> p e t i", i=4),
-                gain_sb[:, b, :].unsqueeze(1).unsqueeze(3).to_broadcast([P, CHUNK // 4, PACK, 4]),
+        def scale_on_scalar(b, c, sig, room):
+            interleave(b, c, gains(b, sig, room))
+
+        def scale_on_gpsimd(b, c, sig):
+            nc.gpsimd.tensor_tensor(
+                operand(b, c).rearrange("p (e t) -> p e t", t=PACK),
+                sig.rearrange("p t e -> p e t"),
+                gain_sb[:, b, :].unsqueeze(1).to_broadcast([P, CHUNK, PACK]),
                 MULT,
             )
 
         def quantize_h(c):
-            nc.vector.quantize_mx(
-                h_codes[c].bitcast(FP8X4), h_planes[c], grouped[c][:, :PASSES, :].rearrange("p b w -> p (b w)")
-            )
+            nc.vector.quantize_mx(h_codes[c].bitcast(FP8X4), h_planes[c], grouped[c])
 
-        def factors(u, c, factor):
-            y = next_bank()[:, :CHUNK]
+        def factors(u, c, factor, bank):
+            y = banks[bank][:, :CHUNK]
             for b in range(PASSES):
                 cols = slice(b * N + u * P, b * N + (u + 1) * P)
                 span = slice(b * CHUNK, (b + 1) * CHUNK)
@@ -279,77 +301,72 @@ def tile_list_pitch_control_rescale_kernel(
                 )
             nc.scalar.activation(factor, y, ACT.Identity, bias=bo_sb[:, u : u + 1])
 
-        def rescale(u, first, count, factor):
-            span = slice(first, first + count)
-            window = map_sb[u][:].indirect(entries(first, count))
-            nc.vector.tensor_tensor(window, picked[u][:, span], factor, MULT)
-
-        def update(u, c, factor):
-            factors(u, c, factor)
-            rescale(u, c * CHUNK, CHUNK, factor)
+        def rescale(u, c, factor):
+            count = factor.shape[1]
+            window = map_sb[u][:].indirect(entries(c * CHUNK, count))
+            nc.vector.tensor_tensor(window, picked[u][:, c * CHUNK : c * CHUNK + count], factor, MULT)
 
         def part(room, i, count=1):
             return room[:, i * CHUNK : (i + count) * CHUNK]
 
-        sig_wide = held([P, PACK, HALF], F32, "sig_wide")
-        sig = [held([P, PACK, CHUNK], F32, f"sig{i}") for i in range(2)]
-        first_factors = held([P, TILES * CHUNK], F32, "first_factors")[:]
-        final = held([P, (TILES - 1) * CHUNK], F32, "final")
+        def room(name):
+            return held([P, 2 * CHUNK], F32, name)[:]
 
-        def begin(b, c):
-            sig.reverse()
-            sigmoids(b, c * CHUNK, CHUNK, sig[0])
+        early = held([P, (TILES + 2) * CHUNK], F32, "early_factors")[:]
+        tail = held([P, 2 * TILES * CHUNK], F32, "tail_factors")[:]
+        low, high = 0, PACK
 
-        def finish(b, c, room):
-            interleave(b, c, gains(b, sig[0], room))
-
-        def unit(b, c, room):
-            begin(b, c)
-            finish(b, c, room)
+        def update(u, c, factor, bank):
+            factors(u, c, factor, bank)
+            rescale(u, c, factor)
 
         pick(0)
         pick(1)
-        sigmoids(0, 0, HALF, sig_wide)
-        wide = gains(0, sig_wide, first_factors.bitcast(BF16))
-        interleave(0, 0, wide[:, :, :CHUNK])
-        sigmoids(1, 0, HALF, sig_wide)
-        halves = grouped[1][:, 0 : PASSES + 1 : PASSES, :]
-        for t in range(PACK):
-            nc.scalar.activation(
-                halves[:, :, t * CHUNK : (t + 1) * CHUNK],
-                sig_wide[:, t, :].rearrange("p (c e) -> p c e", c=2),
-                ACT.Copy,
-                scale=gain_sb[:, 1, t : t + 1],
-            )
-        interleave(1, 0, halves[:, 0, :].rearrange("p (t e) -> p t e", t=PACK))
+        sums(0, 0, HALF, low)
+        sig = sigmoids(0, HALF, low, "sig00")
+        scale_on_gpsimd(0, 0, sig[0])
+        scale_on_gpsimd(0, 1, sig[1])
+        sums(0, 2 * CHUNK, CHUNK, low)
+        scaled = gains(0, sigmoids(0, CHUNK, low, "sig02")[0], room("room02"))
+        sums(1, 0, HALF, high)
+        scale_on_scalar(1, 0, sigmoids(1, CHUNK, high, "sig10")[0], room("room10"))
         pick(2)
         quantize_h(0)
         pick(3)
-        interleave(0, 1, wide[:, :, CHUNK:])
-        update(0, 0, part(first_factors, 0))
-        update(1, 0, part(first_factors, 1))
-        interleave(1, 1, halves[:, 1, :].rearrange("p (t e) -> p t e", t=PACK))
-        room = halves[:, 1, :].bitcast(F32)
-        quantize_h(1)
-        update(2, 0, part(room, 0))
-        update(3, 0, part(room, 1))
-        for c in range(2, CHUNKS):
-            room = held([P, 2 * CHUNK], F32, f"room0{c}")[:]
-            unit(0, c, room.bitcast(BF16))
-            begin(1, c)
-            update(0, c - 1, part(room, 0))
-            update(1, c - 1, part(room, 1))
-            room = held([P, 3 * CHUNK], F32, f"room1{c}")[:]
-            finish(1, c, room.bitcast(BF16))
-            quantize_h(c)
-            update(2, c - 1, part(room, 0))
-            if c < CHUNKS - 1:
-                update(3, c - 1, part(room, 1))
-        factors(3, c - 1, part(room, 1))
-        for u in range(TILES - 1):
-            update(u, c, part(final, u))
-        factors(3, c, part(room, 2))
-        rescale(3, (c - 1) * CHUNK, 2 * CHUNK, part(room, 1, 2))
+        scale_on_scalar(1, 1, sigmoids(1, CHUNK, high, "sig11", CHUNK)[0], room("room11"))
+        for u in range(TILES):
+            factors(u, 0, part(early, u), low + u)
+        sums(1, HALF, HALF, high)
+        for u in range(TILES):
+            if u == 2:
+                quantize_h(1)
+            rescale(u, 0, part(early, u))
+        sums(0, 3 * CHUNK, CHUNK, low)
+        grouped.append(held([P, PASSES * PACK * CHUNK], BF16, "h_codes0")[:])
+        grouped.append(held([P, PASSES * PACK * CHUNK], BF16, "grouped3")[:])
+        interleave(0, 2, scaled)
+        sig = sigmoids(1, HALF, high, "room02")
+        last = sigmoids(0, CHUNK, low, "sig02")[0]
+        for u in range(2):
+            update(u, 1, part(early, TILES + u), low + u)
+        staged = room("room12")
+        scale_on_scalar(1, 2, sig[0], staged)
+        quantize_h(2)
+        for u in range(2, TILES):
+            update(u, 1, part(staged, u - 2), low + u)
+        staged = room("room03")
+        scale_on_scalar(0, 3, last, staged)
+        update(0, 2, part(staged, 0), low)
+        staged = room("room13")
+        scale_on_scalar(1, 3, sig[1], staged)
+        quantize_h(3)
+        update(1, 2, part(staged, 0), low + 1)
+        update(0, 3, part(tail, 1), low + 2)
+        update(1, 3, part(tail, 2), low + 3)
+        for u in range(2, TILES):
+            for c in range(2, CHUNKS):
+                factors(u, c, part(tail, 2 * u + c - 2), low + c)
+            rescale(u, 2, part(tail, 2 * u, 2))
 
         for u in range(TILES):
             nc.sync.dma_start(out[u * P : (u + 1) * P, :], map_sb[u][:])

@@ -162,7 +162,7 @@ def tile_list_pitch_control_rescale_kernel(
                 else:
                     grouped[t] = ring.tile([P, 2 * PASS], BF16, name=f"wh_grouped{t}", align_bytes=64)
                 dst = grouped[t][:].rearrange("p (t m j) -> p m j t", t=2, j=PACK)
-                if (b, a) == (0, 0) or (b, a, t) == (0, 1, 0):
+                if (b, a) == (0, 0) or (a, t) == (1, 2):
                     nc.scalar.activation(dst, src[:, :, :, t : t + 2], ACT.Copy, scale=-1.0)
                 else:
                     nc.vector.tensor_scalar_mul(dst, src[:, :, :, t : t + 2], -1.0)
@@ -202,7 +202,7 @@ def tile_list_pitch_control_rescale_kernel(
             wo_words.rearrange("b p c i -> p b (c i)").bitcast(I32),
         )
 
-        def sums(b, first, width, bank0):
+        def sums(b, first, width, bank0, order):
             step = width if width == HALF else FP4_NARROW
             span = slice(first, first + width)
             for t in range(PACK):
@@ -216,8 +216,8 @@ def tile_list_pitch_control_rescale_kernel(
                         lhsT_scale=wh_planes[b, a][:, cols],
                         rhs=v_codes[a, first][:, :width].bitcast(FP8X4),
                         rhs_scale=v_plane[a][:, span],
-                        start=(a == 0 and width != HALF),
-                        stop=(a == PASSES - 1),
+                        start=(("home", a) == order[0]),
+                        stop=(("home", a) == order[-1]),
                     )
 
                 def away(a):
@@ -229,17 +229,15 @@ def tile_list_pitch_control_rescale_kernel(
                             lhsT_scale=wa_planes[:, a * H + b * PASS + t * P : a * H + b * PASS + (t + 1) * P],
                             rhs=v_codes[a, first + n0][:, :step].bitcast(FP8X4),
                             rhs_scale=v_plane[a][:, first + n0 : first + n0 + step],
-                            start=(a == 0 and width == HALF),
-                            stop=False,
+                            start=(("away", a) == order[0]),
+                            stop=(("away", a) == order[-1] and n0 + step == width),
                         )
 
-                for product in (away, home) if width == HALF else (home, away):
-                    product(0)
-                away(1)
-                home(1)
+                for side, a in order:
+                    (home if side == "home" else away)(a)
 
-        def sigmoids(b, width, bank0, name, first=0):
-            sig = held([P, PACK, width], F32, name)
+        def sigmoids(b, width, bank0, name, first=0, pool=keep):
+            sig = held([P, PACK, width], F32, name, pool)
             for t in range(PACK):
                 nc.scalar.activation(
                     sig[:, t, :], banks[bank0 + t][:, first : first + width], ACT.Sigmoid, bias=lead_sb[:, b, t : t + 1]
@@ -315,6 +313,9 @@ def tile_list_pitch_control_rescale_kernel(
         early = held([P, (TILES + 2) * CHUNK], F32, "early_factors")[:]
         tail = held([P, 2 * TILES * CHUNK], F32, "tail_factors")[:]
         low, high = 0, PACK
+        as_loaded = (("away", 0), ("home", 0), ("away", 1), ("home", 1))
+        widest_first = (("home", 0), ("away", 0), ("away", 1), ("home", 1))
+        last_first = as_loaded[::-1]
 
         def update(u, c, factor, bank):
             factors(u, c, factor, bank)
@@ -322,31 +323,31 @@ def tile_list_pitch_control_rescale_kernel(
 
         pick(0)
         pick(1)
-        sums(0, 0, HALF, low)
+        sums(0, 0, HALF, low, as_loaded)
         sig = sigmoids(0, HALF, low, "sig00")
         scale_on_gpsimd(0, 0, sig[0])
         scale_on_gpsimd(0, 1, sig[1])
-        sums(0, 2 * CHUNK, CHUNK, low)
-        scaled = gains(0, sigmoids(0, CHUNK, low, "sig02")[0], room("room02"))
-        sums(1, 0, HALF, high)
+        sums(0, 2 * CHUNK, CHUNK, low, widest_first)
+        scaled = gains(0, sigmoids(0, CHUNK, low, "wh_raw11", pool=late)[0], room("room02"))
+        sums(1, 0, HALF, high, as_loaded)
+        sums(1, HALF, HALF, low, last_first)
         scale_on_scalar(1, 0, sigmoids(1, CHUNK, high, "sig10")[0], room("room10"))
         pick(2)
         quantize_h(0)
         pick(3)
         scale_on_scalar(1, 1, sigmoids(1, CHUNK, high, "sig11", CHUNK)[0], room("room11"))
         for u in range(TILES):
-            factors(u, 0, part(early, u), low + u)
-        sums(1, HALF, HALF, high)
+            factors(u, 0, part(early, u), high + u)
         for u in range(TILES):
             if u == 2:
                 quantize_h(1)
             rescale(u, 0, part(early, u))
-        sums(0, 3 * CHUNK, CHUNK, low)
+        sums(0, 3 * CHUNK, CHUNK, high, widest_first)
         grouped.append(held([P, PASSES * PACK * CHUNK], BF16, "h_codes0")[:])
         grouped.append(held([P, PASSES * PACK * CHUNK], BF16, "grouped3")[:])
         interleave(0, 2, scaled)
-        sig = sigmoids(1, HALF, high, "room02")
-        last = sigmoids(0, CHUNK, low, "sig02")[0]
+        sig = sigmoids(1, HALF, low, "room02")
+        last = sigmoids(0, CHUNK, high, "sig02")[0]
         for u in range(2):
             update(u, 1, part(early, TILES + u), low + u)
         staged = room("room12")
@@ -356,16 +357,16 @@ def tile_list_pitch_control_rescale_kernel(
             update(u, 1, part(staged, u - 2), low + u)
         staged = room("room03")
         scale_on_scalar(0, 3, last, staged)
-        update(0, 2, part(staged, 0), low)
+        update(0, 2, part(staged, 0), high)
         staged = room("room13")
         scale_on_scalar(1, 3, sig[1], staged)
         quantize_h(3)
-        update(1, 2, part(staged, 0), low + 1)
-        update(0, 3, part(tail, 1), low + 2)
-        update(1, 3, part(tail, 2), low + 3)
+        update(1, 2, part(staged, 0), high + 1)
+        update(0, 3, part(tail, 1), high + 2)
+        update(1, 3, part(tail, 2), high + 3)
         for u in range(2, TILES):
             for c in range(2, CHUNKS):
-                factors(u, c, part(tail, 2 * u + c - 2), low + c)
+                factors(u, c, part(tail, 2 * u + c - 2), high + c)
             rescale(u, 2, part(tail, 2 * u, 2))
 
         for u in range(TILES):

@@ -38,7 +38,6 @@ def tile_list_pitch_control_rescale_kernel(
     with ExitStack() as ctx:
         keep = ctx.enter_context(tc.tile_pool(name="keep", bufs=1))
         ring = ctx.enter_context(tc.tile_pool(name="ring", bufs=2))
-        laid = ctx.enter_context(tc.tile_pool(name="laid", bufs=1))
         psum = ctx.enter_context(tc.psum_pool(name="psum", bufs=1))
         banks = [psum.tile([P, HALF], F32, name=f"bank{i}") for i in range(BANKS)]
 
@@ -72,7 +71,10 @@ def tile_list_pitch_control_rescale_kernel(
             nc.sync.dma_start(tab_sb[a][:].bitcast(I32), tab_words[a].rearrange("p t i -> p (t i)").bitcast(I32))
 
         def load_wh(b, a, pool):
-            wh_raw[b, a] = held([P, PACK, PASS], F32, f"wh_raw{b}{a}", pool)
+            if (b, a) == (1, 1):
+                wh_raw[b, a] = pool.tile([P, PACK, PASS], F32, name="wh_last", align_bytes=64, offset=0)
+            else:
+                wh_raw[b, a] = held([P, PACK, PASS], F32, f"wh_raw{b}{a}", pool)
             rows = wh[a * PASS : (a + 1) * PASS, b * PASS : (b + 1) * PASS]
             nc.sync.dma_start(wh_raw[b, a][:], rows.rearrange("(p j) c -> p j c", j=PACK))
 
@@ -130,14 +132,16 @@ def tile_list_pitch_control_rescale_kernel(
             )
 
         late = ctx.enter_context(tc.tile_pool(name="late", bufs=1))
+        laid = ctx.enter_context(tc.tile_pool(name="laid", bufs=1))
         gain_sb = held([P, PASSES, PACK], F32, "gain_sb", late)
         bo_sb = held([P, TILES], F32, "bo_sb", late)
         load_tab(1, late)
         load_wh(1, 0, late)
         nc.sync.dma_start(gain_sb[:], gain.rearrange("(b p t) -> p b t", b=PASSES, t=PACK))
         load_wa_words(1, late)
-        load_wh(1, 1, late)
-        for u in range(TILES - 1):
+        load_map(0, late, "map_sb0")
+        load_wh(1, 1, laid)
+        for u in range(1, TILES - 1):
             load_map(u, late, f"map_sb{u}")
         with nc.allow_non_contiguous_dma("one bias value for each partition"):
             nc.sync.dma_start(bo_sb[:], bo.rearrange("(u p) -> p u", p=P))
@@ -157,10 +161,7 @@ def tile_list_pitch_control_rescale_kernel(
             grouped = {}
             src = wh_raw[b, a][:].rearrange("p j (m t) -> p m j t", t=PACK)
             for t in range(0, PACK, 2):
-                if (b, a, t) == (1, 1, 2):
-                    grouped[t] = laid.tile([P, 2 * PASS], BF16, name="last_grouped", align_bytes=64, offset=3072)
-                else:
-                    grouped[t] = ring.tile([P, 2 * PASS], BF16, name=f"wh_grouped{t}", align_bytes=64)
+                grouped[t] = ring.tile([P, 2 * PASS], BF16, name=f"wh_grouped{t}", align_bytes=64)
                 dst = grouped[t][:].rearrange("p (t m j) -> p m j t", t=2, j=PACK)
                 if (b, a) == (0, 0) or (a, t) == (1, 2):
                     nc.scalar.activation(dst, src[:, :, :, t : t + 2], ACT.Copy, scale=-1.0)
@@ -190,6 +191,7 @@ def tile_list_pitch_control_rescale_kernel(
         gather_words(1, HALF, HALF)
         quantize_wh(1, 0)
         reorder_wa_words(1)
+        pick(0)
         quantize_wh(1, 1)
 
         shared_planes = wa_planes_raw[:, : PASSES * N]
@@ -236,24 +238,30 @@ def tile_list_pitch_control_rescale_kernel(
                 for side, a in order:
                     (home if side == "home" else away)(a)
 
-        def sigmoids(b, width, bank0, name, first=0, pool=keep):
-            sig = held([P, PACK, width], F32, name, pool)
+        def sigmoids(b, width, bank0, sig, first=0):
             for t in range(PACK):
                 nc.scalar.activation(
                     sig[:, t, :], banks[bank0 + t][:, first : first + width], ACT.Sigmoid, bias=lead_sb[:, b, t : t + 1]
                 )
             return [sig[:, :, e : e + CHUNK] for e in range(0, width, CHUNK)]
 
-        grouped = [
-            laid.tile([P, PASSES * PACK * CHUNK], BF16, name=f"grouped{c}", align_bytes=64, offset=4096 * c)[:]
-            for c in range(2)
-        ]
-        h_codes = [held([P, PASSES * CHUNK], U32, f"h_codes{c}")[:] for c in range(CHUNKS)]
-        h_planes = [shared_planes[:, c * PASSES * CHUNK : (c + 1) * PASSES * CHUNK] for c in range(2)]
-        h_planes += [held([P, PASSES * CHUNK], U8, f"h_planes{c}")[:] for c in range(2, CHUNKS)]
+        grouped = {}
+        h_codes = {}
+        h_planes = {}
 
-        def operand(b, c):
-            return grouped[c][:, b * PACK * CHUNK : (b + 1) * PACK * CHUNK]
+        def spread(table, whole, keys):
+            width = whole.shape[1] // len(keys)
+            for i, key in enumerate(keys):
+                table[key] = whole[:, i * width : (i + 1) * width]
+            return whole
+
+        def new_grouped(keys, name, pool=keep):
+            return spread(grouped, held([P, len(keys) * PACK * CHUNK], BF16, name, pool)[:], keys)
+
+        def quantize_h(keys, values, codes, planes):
+            spread(h_codes, codes, keys)
+            spread(h_planes, planes, keys)
+            nc.vector.quantize_mx(codes.bitcast(FP8X4), planes, values)
 
         def gains(b, sig, room):
             scaled = room.bitcast(BF16)[:, : PACK * CHUNK].rearrange("p (t e) -> p t e", t=PACK)
@@ -265,7 +273,7 @@ def tile_list_pitch_control_rescale_kernel(
 
         def interleave(b, c, scaled):
             nc.scalar.copy(
-                operand(b, c).rearrange("p (e i t) -> p e t i", i=4, t=PACK),
+                grouped[b, c].rearrange("p (e i t) -> p e t i", i=4, t=PACK),
                 scaled.rearrange("p t (e i) -> p e t i", i=4),
             )
 
@@ -274,26 +282,22 @@ def tile_list_pitch_control_rescale_kernel(
 
         def scale_on_gpsimd(b, c, sig):
             nc.gpsimd.tensor_tensor(
-                operand(b, c).rearrange("p (e t) -> p e t", t=PACK),
+                grouped[b, c].rearrange("p (e t) -> p e t", t=PACK),
                 sig.rearrange("p t e -> p e t"),
                 gain_sb[:, b, :].unsqueeze(1).to_broadcast([P, CHUNK, PACK]),
                 MULT,
             )
 
-        def quantize_h(c):
-            nc.vector.quantize_mx(h_codes[c].bitcast(FP8X4), h_planes[c], grouped[c])
-
         def factors(u, c, factor, bank):
             y = banks[bank][:, :CHUNK]
             for b in range(PASSES):
                 cols = slice(b * N + u * P, b * N + (u + 1) * P)
-                span = slice(b * CHUNK, (b + 1) * CHUNK)
                 nc.tensor.matmul_mx(
                     y,
                     lhsT=wo_sb[:, cols].bitcast(FP8X4),
                     lhsT_scale=wo_planes[:, cols],
-                    rhs=h_codes[c][:, span].bitcast(FP8X4),
-                    rhs_scale=h_planes[c][:, span],
+                    rhs=h_codes[b, c].bitcast(FP8X4),
+                    rhs_scale=h_planes[b, c],
                     start=(b == 0),
                     stop=(b == PASSES - 1),
                 )
@@ -321,38 +325,52 @@ def tile_list_pitch_control_rescale_kernel(
             factors(u, c, factor, bank)
             rescale(u, c, factor)
 
-        pick(0)
-        pick(1)
+        def buffer(width, name):
+            return held([P, PACK, width], F32, name)
+
+        def words(count, name):
+            return held([P, count * CHUNK], U32, name)[:]
+
+        def plane(count, name):
+            return held([P, count * CHUNK], U8, name)[:]
+
         sums(0, 0, HALF, low, as_loaded)
-        sig = sigmoids(0, HALF, low, "sig00")
-        scale_on_gpsimd(0, 0, sig[0])
+        sig = sigmoids(0, HALF, low, buffer(HALF, "sig00"))
+        keys = ((0, 0), (0, 1))
+        values = new_grouped(keys, "wa_raw1", late)
+        scale_on_scalar(0, 0, sig[0], room("room00"))
         scale_on_gpsimd(0, 1, sig[1])
+        codes = laid.tile([P, 2 * CHUNK], U32, name="h_codes_first", align_bytes=64, offset=0)
+        quantize_h(keys, values, codes[:], plane(2, "h_planes_first"))
+        pick(1)
         sums(0, 2 * CHUNK, CHUNK, low, widest_first)
-        scaled = gains(0, sigmoids(0, CHUNK, low, "wh_raw11", pool=late)[0], room("room02"))
+        ahead = laid.tile([P, PACK, CHUNK], F32, name="sig_ahead", align_bytes=64, offset=4096)
+        third = new_grouped(((0, 2), (1, 2)), "wa_raw1", late)
+        scale_on_gpsimd(0, 2, sigmoids(0, CHUNK, low, ahead)[0])
         sums(1, 0, HALF, high, as_loaded)
         sums(1, HALF, HALF, low, last_first)
-        scale_on_scalar(1, 0, sigmoids(1, CHUNK, high, "sig10")[0], room("room10"))
+        values = new_grouped(((1, 0),), "grouped10")
+        scale_on_scalar(1, 0, sigmoids(1, CHUNK, high, buffer(CHUNK, "sig10"))[0], room("room10"))
         pick(2)
-        quantize_h(0)
+        quantize_h(((1, 0),), values, words(1, "h_codes10"), shared_planes[:, :CHUNK])
         pick(3)
-        scale_on_scalar(1, 1, sigmoids(1, CHUNK, high, "sig11", CHUNK)[0], room("room11"))
+        values = new_grouped(((1, 1),), "grouped11")
+        scale_on_scalar(1, 1, sigmoids(1, CHUNK, high, buffer(CHUNK, "sig11"), CHUNK)[0], room("room11"))
         for u in range(TILES):
             factors(u, 0, part(early, u), high + u)
         for u in range(TILES):
             if u == 2:
-                quantize_h(1)
+                quantize_h(((1, 1),), values, words(1, "h_codes11"), shared_planes[:, N : N + CHUNK])
             rescale(u, 0, part(early, u))
         sums(0, 3 * CHUNK, CHUNK, high, widest_first)
-        grouped.append(held([P, PASSES * PACK * CHUNK], BF16, "h_codes0")[:])
-        grouped.append(held([P, PASSES * PACK * CHUNK], BF16, "grouped3")[:])
-        interleave(0, 2, scaled)
-        sig = sigmoids(1, HALF, low, "room02")
-        last = sigmoids(0, CHUNK, high, "sig02")[0]
+        fourth = new_grouped(((0, 3), (1, 3)), "grouped3")
+        sig = sigmoids(1, HALF, low, buffer(HALF, "h_codes10"))
+        last = sigmoids(0, CHUNK, high, buffer(CHUNK, "sig10"))[0]
         for u in range(2):
             update(u, 1, part(early, TILES + u), low + u)
         staged = room("room12")
         scale_on_scalar(1, 2, sig[0], staged)
-        quantize_h(2)
+        quantize_h(((0, 2), (1, 2)), third, words(2, "h_codes2"), plane(2, "h_planes2"))
         for u in range(2, TILES):
             update(u, 1, part(staged, u - 2), low + u)
         staged = room("room03")
@@ -360,7 +378,7 @@ def tile_list_pitch_control_rescale_kernel(
         update(0, 2, part(staged, 0), high)
         staged = room("room13")
         scale_on_scalar(1, 3, sig[1], staged)
-        quantize_h(3)
+        quantize_h(((0, 3), (1, 3)), fourth, words(2, "h_codes3"), plane(2, "h_planes3"))
         update(1, 2, part(staged, 0), high + 1)
         update(0, 3, part(tail, 1), high + 2)
         update(1, 3, part(tail, 2), high + 3)

@@ -88,20 +88,6 @@ def tile_list_pitch_control_rescale_kernel(
                 src.rearrange("p (g m t) -> p g t m", t=PACK, m=P),
             )
 
-        wa_raw = {}
-        wa_codes = {}
-
-        def load_wa_words(b, pool):
-            wa_raw[b] = held([P, PASSES * 2 * PASS], U8, f"wa_raw{b}", pool)
-            nc.sync.dma_start(
-                wa_raw[b][:].bitcast(I32).rearrange("p (a w) -> p a w", a=PASSES),
-                wa_words[:, :, 2 * PASS * b : 2 * PASS * (b + 1)].bitcast(I32).rearrange("a p w -> p a w"),
-            )
-
-        def reorder_wa_words(b):
-            wa_codes[b] = held([P, PASSES * 2 * PASS], U8, f"wa_codes{b}")
-            reorder_columns(wa_codes[b][:].bitcast(U16), wa_raw[b][:].bitcast(U16))
-
         def reorder_wa_planes():
             ordered = held([P, PASSES * H], U8, "wa_planes")
             reorder_columns(ordered[:], wa_planes_raw[:])
@@ -117,7 +103,11 @@ def tile_list_pitch_control_rescale_kernel(
                     tab_rows[r:P:QUADRANT, :].bitcast(I32), tab_scales[0, r:PLANE_ROWS:PACK, :].bitcast(I32)
                 )
             nc.sync.dma_start(tab_rows[PACK : PACK + PLANE_ROWS, :].bitcast(I32), tab_scales[1].bitcast(I32))
-            load_wa_words(0, keep)
+            wa_raw = held([P, PASSES * 2 * H], U8, "wa_raw")
+            nc.sync.dma_start(
+                wa_raw[:].bitcast(I32).rearrange("p (a w) -> p a w", a=PASSES),
+                wa_words.bitcast(I32).rearrange("a p w -> p a w"),
+            )
             load_tab(0, keep)
             load_planes(wa_planes_raw, wa_scales)
             lead_sb = held([P, PASSES, PACK], F32, "lead_sb")
@@ -138,7 +128,6 @@ def tile_list_pitch_control_rescale_kernel(
         load_tab(1, late)
         load_wh(1, 0, late)
         nc.sync.dma_start(gain_sb[:], gain.rearrange("(b p t) -> p b t", b=PASSES, t=PACK))
-        load_wa_words(1, late)
         load_map(0, late, "map_sb0")
         load_wh(1, 1, laid)
         for u in range(1, TILES - 1):
@@ -161,9 +150,12 @@ def tile_list_pitch_control_rescale_kernel(
             grouped = {}
             src = wh_raw[b, a][:].rearrange("p j (m t) -> p m j t", t=PACK)
             for t in range(0, PACK, 2):
-                grouped[t] = ring.tile([P, 2 * PASS], BF16, name=f"wh_grouped{t}", align_bytes=64)
+                if (b, a, t) == (1, 0, 2):
+                    grouped[t] = held([P, 2 * PASS], BF16, "handed_on")
+                else:
+                    grouped[t] = ring.tile([P, 2 * PASS], BF16, name=f"wh_grouped{t}", align_bytes=64)
                 dst = grouped[t][:].rearrange("p (t m j) -> p m j t", t=2, j=PACK)
-                if (b, a) == (0, 0) or (a, t) == (1, 2):
+                if (b, a) == (0, 0) or (b, a, t) == (0, 1, 2):
                     nc.scalar.activation(dst, src[:, :, :, t : t + 2], ACT.Copy, scale=-1.0)
                 else:
                     nc.vector.tensor_scalar_mul(dst, src[:, :, :, t : t + 2], -1.0)
@@ -182,7 +174,8 @@ def tile_list_pitch_control_rescale_kernel(
         def pick(u):
             nc.vector.tensor_copy(picked[u][:], map_sb[u][:].indirect(offsets[:]))
 
-        reorder_wa_words(0)
+        wa_codes = held([P, PASSES * 2 * H], U8, "wa_codes")
+        reorder_columns(wa_codes[:].bitcast(U16), wa_raw[:].bitcast(U16))
         gather_words(0, 0, S)
         wa_planes = reorder_wa_planes()
         quantize_wh(0, 0)
@@ -190,7 +183,6 @@ def tile_list_pitch_control_rescale_kernel(
         gather_words(1, 0, HALF)
         gather_words(1, HALF, HALF)
         quantize_wh(1, 0)
-        reorder_wa_words(1)
         pick(0)
         quantize_wh(1, 1)
 
@@ -223,12 +215,12 @@ def tile_list_pitch_control_rescale_kernel(
                     )
 
                 def away(a):
-                    col = a * PASS + t * P
+                    col = a * H + b * PASS + t * P
                     for n0 in range(0, width, step):
                         nc.tensor.matmul_mx(
                             d[:, n0 : n0 + step],
-                            lhsT=wa_codes[b][:, 2 * col : 2 * (col + P)].bitcast(FP4X4),
-                            lhsT_scale=wa_planes[:, a * H + b * PASS + t * P : a * H + b * PASS + (t + 1) * P],
+                            lhsT=wa_codes[:, 2 * col : 2 * (col + P)].bitcast(FP4X4),
+                            lhsT_scale=wa_planes[:, col : col + P],
                             rhs=v_codes[a, first + n0][:, :step].bitcast(FP8X4),
                             rhs_scale=v_plane[a][:, first + n0 : first + n0 + step],
                             start=(("away", a) == order[0]),
@@ -318,6 +310,7 @@ def tile_list_pitch_control_rescale_kernel(
         tail = held([P, 2 * TILES * CHUNK], F32, "tail_factors")[:]
         low, high = 0, PACK
         as_loaded = (("away", 0), ("home", 0), ("away", 1), ("home", 1))
+        away_first = (("away", 0), ("away", 1), ("home", 0), ("home", 1))
         widest_first = (("home", 0), ("away", 0), ("away", 1), ("home", 1))
         last_first = as_loaded[::-1]
 
@@ -335,19 +328,18 @@ def tile_list_pitch_control_rescale_kernel(
             return held([P, count * CHUNK], U8, name)[:]
 
         sums(0, 0, HALF, low, as_loaded)
-        sig = sigmoids(0, HALF, low, buffer(HALF, "sig00"))
         keys = ((0, 0), (0, 1))
-        values = new_grouped(keys, "wa_raw1", late)
-        scale_on_scalar(0, 0, sig[0], room("room00"))
-        scale_on_gpsimd(0, 1, sig[1])
+        values = new_grouped(keys, "handed_on")
+        scale_on_gpsimd(0, 1, sigmoids(0, CHUNK, low, buffer(CHUNK, "sig01"), CHUNK)[0])
+        scale_on_scalar(0, 0, sigmoids(0, CHUNK, low, buffer(CHUNK, "sig00"))[0], room("room00"))
         codes = laid.tile([P, 2 * CHUNK], U32, name="h_codes_first", align_bytes=64, offset=0)
         quantize_h(keys, values, codes[:], plane(2, "h_planes_first"))
         pick(1)
         sums(0, 2 * CHUNK, CHUNK, low, widest_first)
-        ahead = laid.tile([P, PACK, CHUNK], F32, name="sig_ahead", align_bytes=64, offset=4096)
-        third = new_grouped(((0, 2), (1, 2)), "wa_raw1", late)
+        ahead = buffer(CHUNK, "sig00")
+        third = new_grouped(((0, 2), (1, 2)), "handed_on")
         scale_on_gpsimd(0, 2, sigmoids(0, CHUNK, low, ahead)[0])
-        sums(1, 0, HALF, high, as_loaded)
+        sums(1, 0, HALF, high, away_first)
         sums(1, HALF, HALF, low, last_first)
         values = new_grouped(((1, 0),), "grouped10")
         scale_on_scalar(1, 0, sigmoids(1, CHUNK, high, buffer(CHUNK, "sig10"))[0], room("room10"))
@@ -355,7 +347,7 @@ def tile_list_pitch_control_rescale_kernel(
         quantize_h(((1, 0),), values, words(1, "h_codes10"), shared_planes[:, :CHUNK])
         pick(3)
         values = new_grouped(((1, 1),), "grouped11")
-        scale_on_scalar(1, 1, sigmoids(1, CHUNK, high, buffer(CHUNK, "sig11"), CHUNK)[0], room("room11"))
+        scale_on_scalar(1, 1, sigmoids(1, CHUNK, high, buffer(CHUNK, "sig10"), CHUNK)[0], room("room11"))
         for u in range(TILES):
             factors(u, 0, part(early, u), high + u)
         for u in range(TILES):

@@ -28,6 +28,7 @@ CHUNK = 256
 CHUNKS = S // CHUNK
 TILES = N // P
 FP4_NARROW = 128
+SHARE = 192
 BANKS = 8
 
 
@@ -255,28 +256,20 @@ def tile_list_pitch_control_rescale_kernel(
             spread(h_planes, planes, keys)
             nc.vector.quantize_mx(codes.bitcast(FP8X4), planes, values)
 
-        def gains(b, sig, room):
-            scaled = room.bitcast(BF16)[:, : PACK * CHUNK].rearrange("p (t e) -> p t e", t=PACK)
+        def scale_on_scalar(b, c, sig, room, first=0):
+            scaled = room.bitcast(BF16)[:, : PACK * (CHUNK - first)].rearrange("p (t e) -> p t e", t=PACK)
             for t in range(PACK):
-                nc.scalar.activation(
-                    scaled[:, t, :], sig[:, t, :], ACT.Copy, scale=gain_sb[:, b, t : t + 1]
-                )
-            return scaled
-
-        def interleave(b, c, scaled):
+                nc.scalar.activation(scaled[:, t, :], sig[:, t, first:], ACT.Copy, scale=gain_sb[:, b, t : t + 1])
             nc.scalar.copy(
-                grouped[b, c].rearrange("p (e i t) -> p e t i", i=4, t=PACK),
+                grouped[b, c][:, PACK * first :].rearrange("p (e i t) -> p e t i", i=4, t=PACK),
                 scaled.rearrange("p t (e i) -> p e t i", i=4),
             )
 
-        def scale_on_scalar(b, c, sig, room):
-            interleave(b, c, gains(b, sig, room))
-
-        def scale_on_gpsimd(b, c, sig):
+        def scale_on_gpsimd(b, c, sig, count=CHUNK):
             nc.gpsimd.tensor_tensor(
-                grouped[b, c].rearrange("p (e t) -> p e t", t=PACK),
-                sig.rearrange("p t e -> p e t"),
-                gain_sb[:, b, :].unsqueeze(1).to_broadcast([P, CHUNK, PACK]),
+                grouped[b, c][:, : PACK * count].rearrange("p (e t) -> p e t", t=PACK),
+                sig[:, :, :count].rearrange("p t e -> p e t"),
+                gain_sb[:, b, :].unsqueeze(1).to_broadcast([P, count, PACK]),
                 MULT,
             )
 
@@ -346,8 +339,10 @@ def tile_list_pitch_control_rescale_kernel(
         pick(2)
         quantize_h(((1, 0),), values, words(1, "h_codes10"), shared_planes[:, :CHUNK])
         pick(3)
-        values = new_grouped(((1, 1),), "grouped11")
-        scale_on_scalar(1, 1, sigmoids(1, CHUNK, high, buffer(CHUNK, "sig10"), CHUNK)[0], room("room11"))
+        values = new_grouped(((1, 1),), "grouped10")
+        second = sigmoids(1, CHUNK, high, buffer(CHUNK, "sig10"), CHUNK)[0]
+        scale_on_gpsimd(1, 1, second, SHARE)
+        scale_on_scalar(1, 1, second, room("room11"), SHARE)
         for u in range(TILES):
             factors(u, 0, part(early, u), high + u)
         for u in range(TILES):

@@ -236,7 +236,7 @@ def tile_list_pitch_control_rescale_kernel(
                 nc.scalar.activation(
                     sig[:, t, :], banks[bank0 + t][:, first : first + width], ACT.Sigmoid, bias=lead_sb[:, b, t : t + 1]
                 )
-            return [sig[:, :, e : e + CHUNK] for e in range(0, width, CHUNK)]
+            return sig[:]
 
         grouped = {}
         h_codes = {}
@@ -256,20 +256,20 @@ def tile_list_pitch_control_rescale_kernel(
             spread(h_planes, planes, keys)
             nc.vector.quantize_mx(codes.bitcast(FP8X4), planes, values)
 
-        def scale_on_scalar(b, c, sig, room, first=0):
-            scaled = room.bitcast(BF16)[:, : PACK * (CHUNK - first)].rearrange("p (t e) -> p t e", t=PACK)
+        def scale_on_scalar(b, sig, room, values):
+            scaled = room.bitcast(BF16)[:, : values.shape[1]].rearrange("p (t e) -> p t e", t=PACK)
             for t in range(PACK):
-                nc.scalar.activation(scaled[:, t, :], sig[:, t, first:], ACT.Copy, scale=gain_sb[:, b, t : t + 1])
+                nc.scalar.activation(scaled[:, t, :], sig[:, t, :], ACT.Copy, scale=gain_sb[:, b, t : t + 1])
             nc.scalar.copy(
-                grouped[b, c][:, PACK * first :].rearrange("p (e i t) -> p e t i", i=4, t=PACK),
+                values.rearrange("p (e i t) -> p e t i", i=4, t=PACK),
                 scaled.rearrange("p t (e i) -> p e t i", i=4),
             )
 
-        def scale_on_gpsimd(b, c, sig, count=CHUNK):
+        def scale_on_gpsimd(b, sig, values):
             nc.gpsimd.tensor_tensor(
-                grouped[b, c][:, : PACK * count].rearrange("p (e t) -> p e t", t=PACK),
-                sig[:, :, :count].rearrange("p t e -> p e t"),
-                gain_sb[:, b, :].unsqueeze(1).to_broadcast([P, count, PACK]),
+                values.rearrange("p (e t) -> p e t", t=PACK),
+                sig.rearrange("p t e -> p e t"),
+                gain_sb[:, b, :].unsqueeze(1).to_broadcast([P, sig.shape[2], PACK]),
                 MULT,
             )
 
@@ -323,26 +323,28 @@ def tile_list_pitch_control_rescale_kernel(
         sums(0, 0, HALF, low, as_loaded)
         keys = ((0, 0), (0, 1))
         values = new_grouped(keys, "handed_on")
-        scale_on_gpsimd(0, 1, sigmoids(0, CHUNK, low, buffer(CHUNK, "sig01"), CHUNK)[0])
-        scale_on_scalar(0, 0, sigmoids(0, CHUNK, low, buffer(CHUNK, "sig00"))[0], room("room00"))
+        rest = HALF - SHARE
+        scale_on_gpsimd(0, sigmoids(0, SHARE, low, buffer(SHARE, "sig01"), rest), values[:, PACK * rest :])
+        staged = held([P, 2 * rest], F32, "room00")[:]
+        scale_on_scalar(0, sigmoids(0, rest, low, buffer(rest, "sig00")), staged, values[:, : PACK * rest])
         codes = laid.tile([P, 2 * CHUNK], U32, name="h_codes_first", align_bytes=64, offset=0)
         quantize_h(keys, values, codes[:], plane(2, "h_planes_first"))
         pick(1)
         sums(0, 2 * CHUNK, CHUNK, low, widest_first)
         ahead = buffer(CHUNK, "sig00")
         third = new_grouped(((0, 2), (1, 2)), "handed_on")
-        scale_on_gpsimd(0, 2, sigmoids(0, CHUNK, low, ahead)[0])
+        scale_on_gpsimd(0, sigmoids(0, CHUNK, low, ahead), grouped[0, 2])
         sums(1, 0, HALF, high, away_first)
         sums(1, HALF, HALF, low, last_first)
         values = new_grouped(((1, 0),), "grouped10")
-        scale_on_scalar(1, 0, sigmoids(1, CHUNK, high, buffer(CHUNK, "sig10"))[0], room("room10"))
+        scale_on_scalar(1, sigmoids(1, CHUNK, high, buffer(CHUNK, "sig10")), room("room10"), values)
         pick(2)
         quantize_h(((1, 0),), values, words(1, "h_codes10"), shared_planes[:, :CHUNK])
         pick(3)
         values = new_grouped(((1, 1),), "grouped10")
-        second = sigmoids(1, CHUNK, high, buffer(CHUNK, "sig10"), CHUNK)[0]
-        scale_on_gpsimd(1, 1, second, SHARE)
-        scale_on_scalar(1, 1, second, room("room11"), SHARE)
+        second = sigmoids(1, CHUNK, high, buffer(CHUNK, "sig10"), CHUNK)
+        scale_on_gpsimd(1, second[:, :, :SHARE], values[:, : PACK * SHARE])
+        scale_on_scalar(1, second[:, :, SHARE:], room("room11"), values[:, PACK * SHARE :])
         for u in range(TILES):
             factors(u, 0, part(early, u), high + u)
         for u in range(TILES):
@@ -352,19 +354,19 @@ def tile_list_pitch_control_rescale_kernel(
         sums(0, 3 * CHUNK, CHUNK, high, widest_first)
         fourth = new_grouped(((0, 3), (1, 3)), "grouped3")
         sig = sigmoids(1, HALF, low, buffer(HALF, "h_codes10"))
-        last = sigmoids(0, CHUNK, high, buffer(CHUNK, "sig10"))[0]
+        last = sigmoids(0, CHUNK, high, buffer(CHUNK, "sig10"))
         for u in range(2):
             update(u, 1, part(early, TILES + u), low + u)
         staged = room("room12")
-        scale_on_scalar(1, 2, sig[0], staged)
+        scale_on_scalar(1, sig[:, :, :CHUNK], staged, grouped[1, 2])
         quantize_h(((0, 2), (1, 2)), third, words(2, "h_codes2"), plane(2, "h_planes2"))
         for u in range(2, TILES):
             update(u, 1, part(staged, u - 2), low + u)
         staged = room("room03")
-        scale_on_scalar(0, 3, last, staged)
+        scale_on_scalar(0, last, staged, grouped[0, 3])
         update(0, 2, part(staged, 0), high)
         staged = room("room13")
-        scale_on_scalar(1, 3, sig[1], staged)
+        scale_on_scalar(1, sig[:, :, CHUNK:], staged, grouped[1, 3])
         quantize_h(((0, 3), (1, 3)), fourth, words(2, "h_codes3"), plane(2, "h_planes3"))
         update(1, 2, part(staged, 0), high + 1)
         update(0, 3, part(tail, 1), high + 2)

@@ -29,6 +29,7 @@ CHUNKS = S // CHUNK
 TILES = N // P
 FP4_NARROW = 128
 SHARE = 192
+LAST_SHARE = 128
 BANKS = 8
 
 
@@ -83,6 +84,11 @@ def tile_list_pitch_control_rescale_kernel(
             map_sb[u] = held([P, T], F32, name, pool)
             nc.sync.dma_start(map_sb[u][:], gT[u * P : (u + 1) * P, :])
 
+        def load_vector(vector, b, name, pool):
+            values = held([P, PACK], F32, name, pool)
+            nc.sync.dma_start(values[:], vector[b * PASS : (b + 1) * PASS].rearrange("(p t) -> p t", t=PACK))
+            return values
+
         def reorder_columns(dst, src):
             nc.vector.tensor_copy(
                 dst.rearrange("p (g t m) -> p g t m", t=PACK, m=P),
@@ -111,8 +117,7 @@ def tile_list_pitch_control_rescale_kernel(
             )
             load_tab(0, keep)
             load_planes(wa_planes_raw, wa_scales)
-            lead_sb = held([P, PASSES, PACK], F32, "lead_sb")
-            nc.sync.dma_start(lead_sb[:], lead.rearrange("(b p t) -> p b t", b=PASSES, t=PACK))
+            lead_sb = [load_vector(lead, 0, "lead0", keep)]
             load_wh(0, 0, keep)
             load_wh(0, 1, keep)
             nc.vector.tensor_copy(v_plane[0][:], tab_rows[:].indirect(offsets[:]))
@@ -124,13 +129,14 @@ def tile_list_pitch_control_rescale_kernel(
 
         late = ctx.enter_context(tc.tile_pool(name="late", bufs=1))
         laid = ctx.enter_context(tc.tile_pool(name="laid", bufs=1))
-        gain_sb = held([P, PASSES, PACK], F32, "gain_sb", late)
         bo_sb = held([P, TILES], F32, "bo_sb", late)
         load_tab(1, late)
         load_wh(1, 0, late)
-        nc.sync.dma_start(gain_sb[:], gain.rearrange("(b p t) -> p b t", b=PASSES, t=PACK))
         load_map(0, late, "map_sb0")
+        gain_sb = [load_vector(gain, 0, "gain0", late)]
         load_wh(1, 1, laid)
+        lead_sb.append(load_vector(lead, 1, "lead1", late))
+        gain_sb.append(load_vector(gain, 1, "gain1", late))
         for u in range(1, TILES - 1):
             load_map(u, late, f"map_sb{u}")
         with nc.allow_non_contiguous_dma("one bias value for each partition"):
@@ -234,7 +240,7 @@ def tile_list_pitch_control_rescale_kernel(
         def sigmoids(b, width, bank0, sig, first=0):
             for t in range(PACK):
                 nc.scalar.activation(
-                    sig[:, t, :], banks[bank0 + t][:, first : first + width], ACT.Sigmoid, bias=lead_sb[:, b, t : t + 1]
+                    sig[:, t, :], banks[bank0 + t][:, first : first + width], ACT.Sigmoid, bias=lead_sb[b][:, t : t + 1]
                 )
             return sig[:]
 
@@ -259,7 +265,7 @@ def tile_list_pitch_control_rescale_kernel(
         def scale_on_scalar(b, sig, room, values):
             scaled = room.bitcast(BF16)[:, : values.shape[1]].rearrange("p (t e) -> p t e", t=PACK)
             for t in range(PACK):
-                nc.scalar.activation(scaled[:, t, :], sig[:, t, :], ACT.Copy, scale=gain_sb[:, b, t : t + 1])
+                nc.scalar.activation(scaled[:, t, :], sig[:, t, :], ACT.Copy, scale=gain_sb[b][:, t : t + 1])
             nc.scalar.copy(
                 values.rearrange("p (e i t) -> p e t i", i=4, t=PACK),
                 scaled.rearrange("p t (e i) -> p e t i", i=4),
@@ -269,7 +275,7 @@ def tile_list_pitch_control_rescale_kernel(
             nc.gpsimd.tensor_tensor(
                 values.rearrange("p (e t) -> p e t", t=PACK),
                 sig.rearrange("p t e -> p e t"),
-                gain_sb[:, b, :].unsqueeze(1).to_broadcast([P, sig.shape[2], PACK]),
+                gain_sb[b][:].unsqueeze(1).to_broadcast([P, sig.shape[2], PACK]),
                 MULT,
             )
 
@@ -343,8 +349,8 @@ def tile_list_pitch_control_rescale_kernel(
         pick(3)
         values = new_grouped(((1, 1),), "grouped10")
         second = sigmoids(1, CHUNK, high, buffer(CHUNK, "sig10"), CHUNK)
-        scale_on_gpsimd(1, second[:, :, :SHARE], values[:, : PACK * SHARE])
-        scale_on_scalar(1, second[:, :, SHARE:], room("room11"), values[:, PACK * SHARE :])
+        scale_on_gpsimd(1, second[:, :, :LAST_SHARE], values[:, : PACK * LAST_SHARE])
+        scale_on_scalar(1, second[:, :, LAST_SHARE:], room("room11"), values[:, PACK * LAST_SHARE :])
         for u in range(TILES):
             factors(u, 0, part(early, u), high + u)
         for u in range(TILES):

@@ -132,8 +132,8 @@ def tile_list_pitch_control_rescale_kernel(
         bo_sb = held([P, TILES], F32, "bo_sb", late)
         load_tab(1, late)
         load_wh(1, 0, late)
-        load_map(0, late, "map_sb0")
         gain_sb = [load_vector(gain, 0, "gain0", late)]
+        load_map(0, late, "map_sb0")
         load_wh(1, 1, laid)
         lead_sb.append(load_vector(lead, 1, "lead1", late))
         gain_sb.append(load_vector(gain, 1, "gain1", late))

@@ -21,15 +21,15 @@ PACK = 4
 PASS = P * PACK
 PASSES = K // PASS
 QUADRANT = 32
+SPREAD = 8
+LANDING = 4
 PLANE_ROWS = PASS // 32
 PER_COLUMN = 16
 HALF = 512
 CHUNK = 256
-CHUNKS = S // CHUNK
 TILES = N // P
-FP4_NARROW = 128
-SHARE = 192
-LAST_SHARE = 128
+FIRST_SHARE = 192
+SECOND_SHARE = 288
 BANKS = 8
 
 
@@ -53,16 +53,9 @@ def tile_list_pitch_control_rescale_kernel(
             return offsets[:, first // PER_COLUMN : (first + count) // PER_COLUMN]
 
         def zeroed(engine, width, name, pool=keep):
-            planes = held([P, width], U8, name, pool)
-            engine.memset(planes[:].bitcast(I32), 0)
-            return planes
-
-        def load_planes(planes, scales, row0=0):
-            for r in range(PACK):
-                nc.sync.dma_start(
-                    planes[row0 + r : P : QUADRANT, :].bitcast(I32).rearrange("q (a w) -> q a w", a=PASSES),
-                    scales[:, r:PLANE_ROWS:PACK, :].bitcast(I32).rearrange("a q w -> q a w"),
-                )
+            rows = held([P, width], U8, name, pool)
+            engine.memset(rows[:].bitcast(I32), 0)
+            return rows
 
         tab_sb = {}
         wh_raw = {}
@@ -84,70 +77,62 @@ def tile_list_pitch_control_rescale_kernel(
             map_sb[u] = held([P, T], F32, name, pool)
             nc.sync.dma_start(map_sb[u][:], gT[u * P : (u + 1) * P, :])
 
-        def load_vector(vector, b, name, pool):
-            values = held([P, PACK], F32, name, pool)
-            nc.sync.dma_start(values[:], vector[b * PASS : (b + 1) * PASS].rearrange("(p t) -> p t", t=PACK))
+        def load_vector(vector, name, pool):
+            values = held([P, PASSES, PACK], F32, name, pool)
+            nc.sync.dma_start(values[:], vector.rearrange("(b p t) -> p b t", b=PASSES, t=PACK))
             return values
 
-        def reorder_columns(dst, src):
-            nc.vector.tensor_copy(
-                dst.rearrange("p (g t m) -> p g t m", t=PACK, m=P),
-                src.rearrange("p (g m t) -> p g t m", t=PACK, m=P),
-            )
+        def reordered(ap):
+            return ap.rearrange("p (g t m) -> p g t m", t=PACK, m=P)
 
-        def reorder_wa_planes():
-            ordered = held([P, PASSES * H], U8, "wa_planes")
-            reorder_columns(ordered[:], wa_planes_raw[:])
-            return ordered
+        def as_given(ap):
+            return ap.rearrange("p (g m t) -> p g t m", t=PACK, m=P)
 
-        v_plane = [held([P, S], U8, "v_plane0")]
+        planes = held([P, PASSES * (S + H)], U8, "planes")
         with tc.tile_pool(name="early", bufs=1) as early:
-            tab_rows = zeroed(nc.gpsimd, T, "tab_rows", early)
-            wa_planes_raw = zeroed(nc.vector, PASSES * H, "wa_planes_raw")
-            v_plane.append(zeroed(nc.gpsimd, S, "v_plane1"))
-            for r in range(PACK):
-                nc.sync.dma_start(
-                    tab_rows[r:P:QUADRANT, :].bitcast(I32), tab_scales[0, r:PLANE_ROWS:PACK, :].bitcast(I32)
-                )
-            nc.sync.dma_start(tab_rows[PACK : PACK + PLANE_ROWS, :].bitcast(I32), tab_scales[1].bitcast(I32))
+            tab_rows = [zeroed(nc.gpsimd, T, "tab_rows0", early), zeroed(nc.vector, T, "tab_rows1", early)]
+            wa_rows = zeroed(nc.gpsimd, PASSES * H, "wa_rows", early)
             wa_raw = held([P, PASSES * 2 * H], U8, "wa_raw")
             nc.sync.dma_start(
                 wa_raw[:].bitcast(I32).rearrange("p (a w) -> p a w", a=PASSES),
                 wa_words.bitcast(I32).rearrange("a p w -> p a w"),
             )
+            nc.sync.dma_start(tab_rows[0][LANDING:P:SPREAD, :].bitcast(I32), tab_scales[0].bitcast(I32))
+            nc.sync.dma_start(tab_rows[1][LANDING:P:SPREAD, :].bitcast(I32), tab_scales[1].bitcast(I32))
+            nc.sync.dma_start(
+                wa_rows[LANDING:P:SPREAD, :].bitcast(I32).rearrange("q (a w) -> q a w", a=PASSES),
+                wa_scales.bitcast(I32).rearrange("a q w -> q a w"),
+            )
+            lead_sb = load_vector(lead, "lead", keep)
+            gain_sb = load_vector(gain, "gain", keep)
             load_tab(0, keep)
-            load_planes(wa_planes_raw, wa_scales)
-            lead_sb = [load_vector(lead, 0, "lead0", keep)]
             load_wh(0, 0, keep)
             load_wh(0, 1, keep)
-            nc.vector.tensor_copy(v_plane[0][:], tab_rows[:].indirect(offsets[:]))
-        for q in range(P // QUADRANT):
+            nc.gpsimd.tensor_copy(reordered(planes[:, PASSES * S :]), as_given(wa_rows[:]))
+            listed_rows = held([P, PASSES * S], U8, "listed_rows", early)
+            for a in range(PASSES):
+                nc.vector.tensor_copy(listed_rows[:, a * S : (a + 1) * S], tab_rows[a][:].indirect(offsets[:]))
+            nc.vector.tensor_copy(planes[:, : PASSES * S].bitcast(I32), listed_rows[:].bitcast(I32))
+        for r in range(PACK):
             nc.sync.dma_start(
-                v_plane[1][q * QUADRANT : q * QUADRANT + PACK, :].bitcast(I32),
-                v_plane[0][PACK * (q + 1) : PACK * (q + 2), :].bitcast(I32),
+                planes[r:P:QUADRANT, :].bitcast(I32), planes[SPREAD * r + LANDING : P : QUADRANT, :].bitcast(I32)
             )
 
         late = ctx.enter_context(tc.tile_pool(name="late", bufs=1))
         laid = ctx.enter_context(tc.tile_pool(name="laid", bufs=1))
-        bo_sb = held([P, TILES], F32, "bo_sb", late)
         load_tab(1, late)
         load_wh(1, 0, late)
-        gain_sb = [load_vector(gain, 0, "gain0", late)]
         load_map(0, late, "map_sb0")
         load_wh(1, 1, laid)
-        lead_sb.append(load_vector(lead, 1, "lead1", late))
-        gain_sb.append(load_vector(gain, 1, "gain1", late))
         for u in range(1, TILES - 1):
             load_map(u, late, f"map_sb{u}")
-        with nc.allow_non_contiguous_dma("one bias value for each partition"):
-            nc.sync.dma_start(bo_sb[:], bo.rearrange("(u p) -> p u", p=P))
 
         v_codes = {}
 
         def gather_words(a, first, count):
             words = held([P, count], U32, f"v_codes{a}{first}")
             nc.vector.tensor_copy(words[:], tab_sb[a][:].indirect(entries(first, count)))
-            for e in range(0, count, FP4_NARROW):
+            for e in range(0, count, CHUNK):
                 v_codes[a, first + e] = words[:, e:]
 
         wh_codes = {}
@@ -182,9 +167,8 @@ def tile_list_pitch_control_rescale_kernel(
             nc.vector.tensor_copy(picked[u][:], map_sb[u][:].indirect(offsets[:]))
 
         wa_codes = held([P, PASSES * 2 * H], U8, "wa_codes")
-        reorder_columns(wa_codes[:].bitcast(U16), wa_raw[:].bitcast(U16))
+        nc.scalar.copy(reordered(wa_codes[:].bitcast(U16)), as_given(wa_raw[:].bitcast(U16)))
         gather_words(0, 0, S)
-        wa_planes = reorder_wa_planes()
         quantize_wh(0, 0)
         quantize_wh(0, 1)
         gather_words(1, 0, HALF)
@@ -193,79 +177,71 @@ def tile_list_pitch_control_rescale_kernel(
         pick(0)
         quantize_wh(1, 1)
 
-        shared_planes = wa_planes_raw[:, : PASSES * N]
-        load_planes(shared_planes, wo_scales, PACK)
-        wo_planes = shared_planes[PACK:P, :]
         load_map(TILES - 1, keep, "wh_raw00")
+        wo_rows = zeroed(nc.gpsimd, PASSES * N, "wo_rows", late)
+        for r in range(PACK):
+            nc.sync.dma_start(
+                wo_rows[r:P:QUADRANT, :].bitcast(I32).rearrange("q (a w) -> q a w", a=PASSES),
+                wo_scales[:, r:PLANE_ROWS:PACK, :].bitcast(I32).rearrange("a q w -> q a w"),
+            )
         wo_sb = held([P, PASSES * N], U32, "wh_raw01")
         nc.sync.dma_start(
             wo_sb[:].bitcast(I32).rearrange("p (b c) -> p b c", b=PASSES),
             wo_words.rearrange("b p c i -> p b (c i)").bitcast(I32),
         )
+        bo_sb = held([P, TILES], F32, "bo_sb", late)
+        with nc.allow_non_contiguous_dma("one bias value for each partition"):
+            nc.sync.dma_start(bo_sb[:], bo.rearrange("(u p) -> p u", p=P))
 
         def sums(b, first, width, bank0, order):
-            step = width if width == HALF else FP4_NARROW
-            span = slice(first, first + width)
             for t in range(PACK):
-                d = banks[bank0 + t][:, :width]
-                cols = slice(t * P, (t + 1) * P)
-
-                def home(a):
+                for i, (side, a) in enumerate(order):
+                    if side == "home":
+                        cols = slice(t * P, (t + 1) * P)
+                        weights = wh_codes[b, a][:, cols].bitcast(FP8X4)
+                        weight_plane = wh_planes[b, a][:, cols]
+                    else:
+                        col = a * H + b * PASS + t * P
+                        weights = wa_codes[:, 2 * col : 2 * (col + P)].bitcast(FP4X4)
+                        weight_plane = planes[:, PASSES * S + col : PASSES * S + col + P]
                     nc.tensor.matmul_mx(
-                        d,
-                        lhsT=wh_codes[b, a][:, cols].bitcast(FP8X4),
-                        lhsT_scale=wh_planes[b, a][:, cols],
+                        banks[bank0 + t][:, :width],
+                        lhsT=weights,
+                        lhsT_scale=weight_plane,
                         rhs=v_codes[a, first][:, :width].bitcast(FP8X4),
-                        rhs_scale=v_plane[a][:, span],
-                        start=(("home", a) == order[0]),
-                        stop=(("home", a) == order[-1]),
+                        rhs_scale=planes[:, a * S + first : a * S + first + width],
+                        start=(i == 0),
+                        stop=(i == len(order) - 1),
                     )
-
-                def away(a):
-                    col = a * H + b * PASS + t * P
-                    for n0 in range(0, width, step):
-                        nc.tensor.matmul_mx(
-                            d[:, n0 : n0 + step],
-                            lhsT=wa_codes[:, 2 * col : 2 * (col + P)].bitcast(FP4X4),
-                            lhsT_scale=wa_planes[:, col : col + P],
-                            rhs=v_codes[a, first + n0][:, :step].bitcast(FP8X4),
-                            rhs_scale=v_plane[a][:, first + n0 : first + n0 + step],
-                            start=(("away", a) == order[0]),
-                            stop=(("away", a) == order[-1] and n0 + step == width),
-                        )
-
-                for side, a in order:
-                    (home if side == "home" else away)(a)
 
         def sigmoids(b, width, bank0, sig, first=0):
             for t in range(PACK):
                 nc.scalar.activation(
-                    sig[:, t, :], banks[bank0 + t][:, first : first + width], ACT.Sigmoid, bias=lead_sb[b][:, t : t + 1]
+                    sig[:, t, :],
+                    banks[bank0 + t][:, first : first + width],
+                    ACT.Sigmoid,
+                    bias=lead_sb[:, b, t : t + 1],
                 )
             return sig[:]
 
-        grouped = {}
         h_codes = {}
         h_planes = {}
 
-        def spread(table, whole, keys):
-            width = whole.shape[1] // len(keys)
+        def quantize_h(keys, values, codes, scales):
+            width = codes.shape[1] // len(keys)
             for i, key in enumerate(keys):
-                table[key] = whole[:, i * width : (i + 1) * width]
-            return whole
+                h_codes[key] = codes[:, i * width : (i + 1) * width]
+                h_planes[key] = scales[:, i * width : (i + 1) * width]
+            nc.vector.quantize_mx(codes.bitcast(FP8X4), scales, values)
 
-        def new_grouped(keys, name, pool=keep):
-            return spread(grouped, held([P, len(keys) * PACK * CHUNK], BF16, name, pool)[:], keys)
+        def by_slice(room, width):
+            return room.bitcast(BF16)[:, : PACK * width].rearrange("p (t e) -> p t e", t=PACK)
 
-        def quantize_h(keys, values, codes, planes):
-            spread(h_codes, codes, keys)
-            spread(h_planes, planes, keys)
-            nc.vector.quantize_mx(codes.bitcast(FP8X4), planes, values)
-
-        def scale_on_scalar(b, sig, room, values):
-            scaled = room.bitcast(BF16)[:, : values.shape[1]].rearrange("p (t e) -> p t e", t=PACK)
+        def gains(b, sig, scaled):
             for t in range(PACK):
-                nc.scalar.activation(scaled[:, t, :], sig[:, t, :], ACT.Copy, scale=gain_sb[b][:, t : t + 1])
+                nc.scalar.activation(scaled[:, t, :], sig[:, t, :], ACT.Copy, scale=gain_sb[:, b, t : t + 1])
+
+        def interleave(scaled, values):
             nc.scalar.copy(
                 values.rearrange("p (e i t) -> p e t i", i=4, t=PACK),
                 scaled.rearrange("p t (e i) -> p e t i", i=4),
@@ -275,112 +251,120 @@ def tile_list_pitch_control_rescale_kernel(
             nc.gpsimd.tensor_tensor(
                 values.rearrange("p (e t) -> p e t", t=PACK),
                 sig.rearrange("p t e -> p e t"),
-                gain_sb[b][:].unsqueeze(1).to_broadcast([P, sig.shape[2], PACK]),
+                gain_sb[:, b, :].unsqueeze(1).to_broadcast([P, sig.shape[2], PACK]),
                 MULT,
             )
 
-        def factors(u, c, factor, bank):
-            y = banks[bank][:, :CHUNK]
+        def product(u, part, y):
             for b in range(PASSES):
                 cols = slice(b * N + u * P, b * N + (u + 1) * P)
                 nc.tensor.matmul_mx(
                     y,
                     lhsT=wo_sb[:, cols].bitcast(FP8X4),
-                    lhsT_scale=wo_planes[:, cols],
-                    rhs=h_codes[b, c].bitcast(FP8X4),
-                    rhs_scale=h_planes[b, c],
+                    lhsT_scale=wo_rows[:, cols],
+                    rhs=h_codes[b, part].bitcast(FP8X4),
+                    rhs_scale=h_planes[b, part],
                     start=(b == 0),
                     stop=(b == PASSES - 1),
                 )
+
+        def add_bias(u, y, factor):
             nc.scalar.activation(factor, y, ACT.Identity, bias=bo_sb[:, u : u + 1])
 
-        def rescale(u, c, factor):
+        def rescale(u, first, factor):
             count = factor.shape[1]
-            window = map_sb[u][:].indirect(entries(c * CHUNK, count))
-            nc.vector.tensor_tensor(window, picked[u][:, c * CHUNK : c * CHUNK + count], factor, MULT)
+            window = map_sb[u][:].indirect(entries(first, count))
+            nc.vector.tensor_tensor(window, picked[u][:, first : first + count], factor, MULT)
 
-        def part(room, i, count=1):
-            return room[:, i * CHUNK : (i + count) * CHUNK]
-
-        def room(name):
-            return held([P, 2 * CHUNK], F32, name)[:]
-
-        early = held([P, (TILES + 2) * CHUNK], F32, "early_factors")[:]
-        tail = held([P, 2 * TILES * CHUNK], F32, "tail_factors")[:]
-        low, high = 0, PACK
-        as_loaded = (("away", 0), ("home", 0), ("away", 1), ("home", 1))
-        away_first = (("away", 0), ("away", 1), ("home", 0), ("home", 1))
-        widest_first = (("home", 0), ("away", 0), ("away", 1), ("home", 1))
-        last_first = as_loaded[::-1]
-
-        def update(u, c, factor, bank):
-            factors(u, c, factor, bank)
-            rescale(u, c, factor)
+        def room(width, name):
+            return held([P, width], F32, name)[:]
 
         def buffer(width, name):
             return held([P, PACK, width], F32, name)
 
-        def words(count, name):
-            return held([P, count * CHUNK], U32, name)[:]
+        def words(width, name):
+            return held([P, width], U32, name)[:]
 
-        def plane(count, name):
-            return held([P, count * CHUNK], U8, name)[:]
+        def plane(width, name):
+            return held([P, width], U8, name)[:]
+
+        def shared_half(b, bank0, share, values, names):
+            rest = HALF - share
+            scale_on_gpsimd(b, sigmoids(b, share, bank0, buffer(share, names[0]), rest), values[:, PACK * rest :])
+            sig = sigmoids(b, rest, bank0, buffer(rest, names[1]))
+            scaled = by_slice(room(2 * rest, names[2]), rest)
+            gains(b, sig, scaled)
+            interleave(scaled, values[:, : PACK * rest])
+
+        low, high = 0, PACK
+        as_loaded = (("away", 0), ("home", 0), ("away", 1), ("home", 1))
+        away_first = (("away", 1), ("away", 0), ("home", 0), ("home", 1))
+        last_first = as_loaded[::-1]
+        third, fourth = HALF, HALF + CHUNK
 
         sums(0, 0, HALF, low, as_loaded)
-        keys = ((0, 0), (0, 1))
-        values = new_grouped(keys, "handed_on")
-        rest = HALF - SHARE
-        scale_on_gpsimd(0, sigmoids(0, SHARE, low, buffer(SHARE, "sig01"), rest), values[:, PACK * rest :])
-        staged = held([P, 2 * rest], F32, "room00")[:]
-        scale_on_scalar(0, sigmoids(0, rest, low, buffer(rest, "sig00")), staged, values[:, : PACK * rest])
-        codes = laid.tile([P, 2 * CHUNK], U32, name="h_codes_first", align_bytes=64, offset=0)
-        quantize_h(keys, values, codes[:], plane(2, "h_planes_first"))
-        pick(1)
-        sums(0, 2 * CHUNK, CHUNK, low, widest_first)
-        ahead = buffer(CHUNK, "sig00")
-        third = new_grouped(((0, 2), (1, 2)), "handed_on")
-        scale_on_gpsimd(0, sigmoids(0, CHUNK, low, ahead), grouped[0, 2])
         sums(1, 0, HALF, high, away_first)
+        values = held([P, PACK * HALF], BF16, "handed_on")[:]
+        shared_half(0, low, FIRST_SHARE, values, ("sig_a", "sig_b", "room_a"))
+        codes = laid.tile([P, HALF], U32, name="h_codes_first", align_bytes=64, offset=0)
+        quantize_h(((0, 0),), values, codes[:], plane(HALF, "h_planes00"))
+        pick(1)
+        values = held([P, PACK * HALF], BF16, "values10")[:]
+        shared_half(1, high, SECOND_SHARE, values, ("sig_c", "sig_b", "room_a"))
+        sums(0, third, CHUNK, high, as_loaded)
         sums(1, HALF, HALF, low, last_first)
-        values = new_grouped(((1, 0),), "grouped10")
-        scale_on_scalar(1, sigmoids(1, CHUNK, high, buffer(CHUNK, "sig10")), room("room10"), values)
         pick(2)
-        quantize_h(((1, 0),), values, words(1, "h_codes10"), shared_planes[:, :CHUNK])
+        quantize_h(((1, 0),), values, words(HALF, "h_codes10"), plane(HALF, "h_planes10"))
         pick(3)
-        values = new_grouped(((1, 1),), "grouped10")
-        second = sigmoids(1, CHUNK, high, buffer(CHUNK, "sig10"), CHUNK)
-        scale_on_gpsimd(1, second[:, :, :LAST_SHARE], values[:, : PACK * LAST_SHARE])
-        scale_on_scalar(1, second[:, :, LAST_SHARE:], room("room11"), values[:, PACK * LAST_SHARE :])
+        ahead = sigmoids(0, CHUNK, high, buffer(CHUNK, "sig_b"))
+        values_third = held([P, 2 * PACK * CHUNK], BF16, "values10")[:]
+        scale_on_gpsimd(0, ahead, values_third[:, : PACK * CHUNK])
         for u in range(TILES):
-            factors(u, 0, part(early, u), high + u)
-        for u in range(TILES):
-            if u == 2:
-                quantize_h(((1, 1),), values, words(1, "h_codes11"), shared_planes[:, N : N + CHUNK])
-            rescale(u, 0, part(early, u))
-        sums(0, 3 * CHUNK, CHUNK, high, widest_first)
-        fourth = new_grouped(((0, 3), (1, 3)), "grouped3")
+            product(u, 0, banks[high + u][:])
+        factors = room((TILES - 1) * HALF, "factors")
+        for u in range(TILES - 1):
+            add_bias(u, banks[high + u][:], factors[:, u * HALF : (u + 1) * HALF])
+            rescale(u, 0, factors[:, u * HALF : (u + 1) * HALF])
         sig = sigmoids(1, HALF, low, buffer(HALF, "h_codes10"))
-        last = sigmoids(0, CHUNK, high, buffer(CHUNK, "sig10"))
+        staged = room(6 * CHUNK, "room_b")
+        scaled = staged.bitcast(BF16).rearrange("p (c t e) -> p t c e", c=3, t=PACK)
+        for t in range(PACK):
+            nc.scalar.activation(
+                scaled[:, t, :2, :],
+                sig[:, t, :].rearrange("p (c e) -> p c e", c=2),
+                ACT.Copy,
+                scale=gain_sb[:, 1, t : t + 1],
+            )
+        interleave(scaled[:, :, 0, :], values_third[:, PACK * CHUNK :])
+        quantize_h(((0, third), (1, third)), values_third, words(HALF, "h_codes2"), plane(HALF, "h_planes2"))
+        add_bias(TILES - 1, banks[high + TILES - 1][:], staged[:, :HALF])
+        rescale(TILES - 1, 0, staged[:, :HALF])
+        sums(0, fourth, CHUNK, high, as_loaded)
+        for u in range(TILES):
+            product(u, third, banks[low + u][:, :CHUNK])
+        last = sigmoids(0, CHUNK, high, buffer(CHUNK, "sig_c"))
+        narrow = room(5 * CHUNK, "narrow")
         for u in range(2):
-            update(u, 1, part(early, TILES + u), low + u)
-        staged = room("room12")
-        scale_on_scalar(1, sig[:, :, :CHUNK], staged, grouped[1, 2])
-        quantize_h(((0, 2), (1, 2)), third, words(2, "h_codes2"), plane(2, "h_planes2"))
-        for u in range(2, TILES):
-            update(u, 1, part(staged, u - 2), low + u)
-        staged = room("room03")
-        scale_on_scalar(0, last, staged, grouped[0, 3])
-        update(0, 2, part(staged, 0), high)
-        staged = room("room13")
-        scale_on_scalar(1, sig[:, :, CHUNK:], staged, grouped[1, 3])
-        quantize_h(((0, 3), (1, 3)), fourth, words(2, "h_codes3"), plane(2, "h_planes3"))
-        update(1, 2, part(staged, 0), high + 1)
-        update(0, 3, part(tail, 1), high + 2)
-        update(1, 3, part(tail, 2), high + 3)
-        for u in range(2, TILES):
-            for c in range(2, CHUNKS):
-                factors(u, c, part(tail, 2 * u + c - 2), high + c)
-            rescale(u, 2, part(tail, 2 * u, 2))
+            add_bias(u, banks[low + u][:, :CHUNK], narrow[:, u * CHUNK : (u + 1) * CHUNK])
+            rescale(u, third, narrow[:, u * CHUNK : (u + 1) * CHUNK])
+        gains(0, last, scaled[:, :, 2, :])
+        values = held([P, PACK * HALF], BF16, "handed_on")[:]
+        nc.scalar.copy(
+            values.rearrange("p (c e i t) -> p c e t i", c=2, i=4, t=PACK),
+            scaled[:, :, 1:, :].rearrange("p t c (e i) -> p c e t i", i=4),
+        )
+        quantize_h(((1, fourth), (0, fourth)), values, words(HALF, "h_codes3"), plane(HALF, "h_planes3"))
+        add_bias(2, banks[low + 2][:, :CHUNK], staged[:, 2 * HALF : 2 * HALF + CHUNK])
+        rescale(2, third, staged[:, 2 * HALF : 2 * HALF + CHUNK])
+        for u in range(TILES - 1):
+            product(u, fourth, banks[high + u][:, :CHUNK])
+            factor = narrow[:, (u + 2) * CHUNK : (u + 3) * CHUNK]
+            add_bias(u, banks[high + u][:, :CHUNK], factor)
+            rescale(u, fourth, factor)
+        wide = room(HALF, "wide")
+        product(TILES - 1, fourth, banks[low + TILES - 1][:, CHUNK:])
+        add_bias(TILES - 1, banks[low + TILES - 1][:], wide)
+        rescale(TILES - 1, third, wide)
 
         for u in range(TILES):
             nc.sync.dma_start(out[u * P : (u + 1) * P, :], map_sb[u][:])

@@ -21,15 +21,13 @@ PACK = 4
 PASS = P * PACK
 PASSES = K // PASS
 QUADRANT = 32
-SPREAD = 8
-LANDING = 4
 PLANE_ROWS = PASS // 32
 PER_COLUMN = 16
 HALF = 512
 CHUNK = 256
 TILES = N // P
 FIRST_SHARE = 192
-SECOND_SHARE = 288
+SECOND_SHARE = 192
 BANKS = 8
 
 
@@ -77,10 +75,17 @@ def tile_list_pitch_control_rescale_kernel(
             map_sb[u] = held([P, T], F32, name, pool)
             nc.sync.dma_start(map_sb[u][:], gT[u * P : (u + 1) * P, :])
 
-        def load_vector(vector, name, pool):
-            values = held([P, PASSES, PACK], F32, name, pool)
-            nc.sync.dma_start(values[:], vector.rearrange("(b p t) -> p b t", b=PASSES, t=PACK))
+        def load_vector(vector, b, name, pool):
+            values = held([P, PACK], F32, name, pool)
+            nc.sync.dma_start(values[:], vector[b * PASS : (b + 1) * PASS].rearrange("(p t) -> p t", t=PACK))
             return values
+
+        def load_planes(rows, scales, row0=0):
+            for r in range(PACK):
+                nc.sync.dma_start(
+                    rows[row0 + r : P : QUADRANT, :].bitcast(I32).rearrange("q (a w) -> q a w", a=PASSES),
+                    scales[:, r:PLANE_ROWS:PACK, :].bitcast(I32).rearrange("a q w -> q a w"),
+                )
 
         def reordered(ap):
             return ap.rearrange("p (g t m) -> p g t m", t=PACK, m=P)
@@ -88,42 +93,42 @@ def tile_list_pitch_control_rescale_kernel(
         def as_given(ap):
             return ap.rearrange("p (g m t) -> p g t m", t=PACK, m=P)
 
-        planes = held([P, PASSES * (S + H)], U8, "planes")
+        v_plane = [held([P, S], U8, "v_plane0")]
         with tc.tile_pool(name="early", bufs=1) as early:
-            tab_rows = [zeroed(nc.gpsimd, T, "tab_rows0", early), zeroed(nc.vector, T, "tab_rows1", early)]
-            wa_rows = zeroed(nc.gpsimd, PASSES * H, "wa_rows", early)
+            tab_rows = zeroed(nc.gpsimd, T, "tab_rows", early)
+            wa_rows = zeroed(nc.vector, PASSES * H, "wa_rows")
+            v_plane.append(zeroed(nc.gpsimd, S, "v_plane1"))
+            for r in range(PACK):
+                nc.sync.dma_start(
+                    tab_rows[r:P:QUADRANT, :].bitcast(I32), tab_scales[0, r:PLANE_ROWS:PACK, :].bitcast(I32)
+                )
+            nc.sync.dma_start(tab_rows[PACK : PACK + PLANE_ROWS, :].bitcast(I32), tab_scales[1].bitcast(I32))
             wa_raw = held([P, PASSES * 2 * H], U8, "wa_raw")
             nc.sync.dma_start(
                 wa_raw[:].bitcast(I32).rearrange("p (a w) -> p a w", a=PASSES),
                 wa_words.bitcast(I32).rearrange("a p w -> p a w"),
             )
-            nc.sync.dma_start(tab_rows[0][LANDING:P:SPREAD, :].bitcast(I32), tab_scales[0].bitcast(I32))
-            nc.sync.dma_start(tab_rows[1][LANDING:P:SPREAD, :].bitcast(I32), tab_scales[1].bitcast(I32))
-            nc.sync.dma_start(
-                wa_rows[LANDING:P:SPREAD, :].bitcast(I32).rearrange("q (a w) -> q a w", a=PASSES),
-                wa_scales.bitcast(I32).rearrange("a q w -> q a w"),
-            )
-            lead_sb = load_vector(lead, "lead", keep)
-            gain_sb = load_vector(gain, "gain", keep)
             load_tab(0, keep)
+            load_planes(wa_rows, wa_scales)
+            lead_sb = [load_vector(lead, 0, "lead0", keep)]
             load_wh(0, 0, keep)
             load_wh(0, 1, keep)
-            nc.gpsimd.tensor_copy(reordered(planes[:, PASSES * S :]), as_given(wa_rows[:]))
-            listed_rows = held([P, PASSES * S], U8, "listed_rows", early)
-            for a in range(PASSES):
-                nc.vector.tensor_copy(listed_rows[:, a * S : (a + 1) * S], tab_rows[a][:].indirect(offsets[:]))
-            nc.vector.tensor_copy(planes[:, : PASSES * S].bitcast(I32), listed_rows[:].bitcast(I32))
-        for r in range(PACK):
+            nc.vector.tensor_copy(v_plane[0][:], tab_rows[:].indirect(offsets[:]))
+        for q in range(P // QUADRANT):
             nc.sync.dma_start(
-                planes[r:P:QUADRANT, :].bitcast(I32), planes[SPREAD * r + LANDING : P : QUADRANT, :].bitcast(I32)
+                v_plane[1][q * QUADRANT : q * QUADRANT + PACK, :].bitcast(I32),
+                v_plane[0][PACK * (q + 1) : PACK * (q + 2), :].bitcast(I32),
             )
 
         late = ctx.enter_context(tc.tile_pool(name="late", bufs=1))
         laid = ctx.enter_context(tc.tile_pool(name="laid", bufs=1))
         load_tab(1, late)
         load_wh(1, 0, late)
+        gain_sb = [load_vector(gain, 0, "gain0", late)]
         load_map(0, late, "map_sb0")
         load_wh(1, 1, laid)
+        lead_sb.append(load_vector(lead, 1, "lead1", late))
+        gain_sb.append(load_vector(gain, 1, "gain1", late))
         for u in range(1, TILES - 1):
             load_map(u, late, f"map_sb{u}")
 
@@ -169,6 +174,8 @@ def tile_list_pitch_control_rescale_kernel(
         wa_codes = held([P, PASSES * 2 * H], U8, "wa_codes")
         nc.scalar.copy(reordered(wa_codes[:].bitcast(U16)), as_given(wa_raw[:].bitcast(U16)))
         gather_words(0, 0, S)
+        wa_planes = held([P, PASSES * H], U8, "wa_planes")
+        nc.vector.tensor_copy(reordered(wa_planes[:]), as_given(wa_rows[:]))
         quantize_wh(0, 0)
         quantize_wh(0, 1)
         gather_words(1, 0, HALF)
@@ -178,12 +185,8 @@ def tile_list_pitch_control_rescale_kernel(
         quantize_wh(1, 1)
 
         load_map(TILES - 1, keep, "wh_raw00")
-        wo_rows = zeroed(nc.gpsimd, PASSES * N, "wo_rows", late)
-        for r in range(PACK):
-            nc.sync.dma_start(
-                wo_rows[r:P:QUADRANT, :].bitcast(I32).rearrange("q (a w) -> q a w", a=PASSES),
-                wo_scales[:, r:PLANE_ROWS:PACK, :].bitcast(I32).rearrange("a q w -> q a w"),
-            )
+        load_planes(wa_rows[:, : PASSES * N], wo_scales, PACK)
+        wo_rows = wa_rows[PACK:P, : PASSES * N]
         wo_sb = held([P, PASSES * N], U32, "wh_raw01")
         nc.sync.dma_start(
             wo_sb[:].bitcast(I32).rearrange("p (b c) -> p b c", b=PASSES),
@@ -203,13 +206,13 @@ def tile_list_pitch_control_rescale_kernel(
                     else:
                         col = a * H + b * PASS + t * P
                         weights = wa_codes[:, 2 * col : 2 * (col + P)].bitcast(FP4X4)
-                        weight_plane = planes[:, PASSES * S + col : PASSES * S + col + P]
+                        weight_plane = wa_planes[:, col : col + P]
                     nc.tensor.matmul_mx(
                         banks[bank0 + t][:, :width],
                         lhsT=weights,
                         lhsT_scale=weight_plane,
                         rhs=v_codes[a, first][:, :width].bitcast(FP8X4),
-                        rhs_scale=planes[:, a * S + first : a * S + first + width],
+                        rhs_scale=v_plane[a][:, first : first + width],
                         start=(i == 0),
                         stop=(i == len(order) - 1),
                     )
@@ -220,7 +223,7 @@ def tile_list_pitch_control_rescale_kernel(
                     sig[:, t, :],
                     banks[bank0 + t][:, first : first + width],
                     ACT.Sigmoid,
-                    bias=lead_sb[:, b, t : t + 1],
+                    bias=lead_sb[b][:, t : t + 1],
                 )
             return sig[:]
 
@@ -239,7 +242,7 @@ def tile_list_pitch_control_rescale_kernel(
 
         def gains(b, sig, scaled):
             for t in range(PACK):
-                nc.scalar.activation(scaled[:, t, :], sig[:, t, :], ACT.Copy, scale=gain_sb[:, b, t : t + 1])
+                nc.scalar.activation(scaled[:, t, :], sig[:, t, :], ACT.Copy, scale=gain_sb[b][:, t : t + 1])
 
         def interleave(scaled, values):
             nc.scalar.copy(
@@ -251,7 +254,7 @@ def tile_list_pitch_control_rescale_kernel(
             nc.gpsimd.tensor_tensor(
                 values.rearrange("p (e t) -> p e t", t=PACK),
                 sig.rearrange("p t e -> p e t"),
-                gain_sb[:, b, :].unsqueeze(1).to_broadcast([P, sig.shape[2], PACK]),
+                gain_sb[b][:].unsqueeze(1).to_broadcast([P, sig.shape[2], PACK]),
                 MULT,
             )
 
@@ -298,27 +301,26 @@ def tile_list_pitch_control_rescale_kernel(
 
         low, high = 0, PACK
         as_loaded = (("away", 0), ("home", 0), ("away", 1), ("home", 1))
-        away_first = (("away", 1), ("away", 0), ("home", 0), ("home", 1))
+        away_first = (("away", 0), ("away", 1), ("home", 0), ("home", 1))
         last_first = as_loaded[::-1]
         third, fourth = HALF, HALF + CHUNK
 
         sums(0, 0, HALF, low, as_loaded)
-        sums(1, 0, HALF, high, away_first)
         values = held([P, PACK * HALF], BF16, "handed_on")[:]
         shared_half(0, low, FIRST_SHARE, values, ("sig_a", "sig_b", "room_a"))
         codes = laid.tile([P, HALF], U32, name="h_codes_first", align_bytes=64, offset=0)
         quantize_h(((0, 0),), values, codes[:], plane(HALF, "h_planes00"))
         pick(1)
-        values = held([P, PACK * HALF], BF16, "values10")[:]
-        shared_half(1, high, SECOND_SHARE, values, ("sig_c", "sig_b", "room_a"))
-        sums(0, third, CHUNK, high, as_loaded)
+        sums(0, third, CHUNK, low, as_loaded)
+        values_third = held([P, 2 * PACK * CHUNK], BF16, "handed_on")[:]
+        scale_on_gpsimd(0, sigmoids(0, CHUNK, low, buffer(CHUNK, "sig_b")), values_third[:, : PACK * CHUNK])
+        sums(1, 0, HALF, high, away_first)
         sums(1, HALF, HALF, low, last_first)
+        values = held([P, PACK * HALF], BF16, "values10")[:]
+        shared_half(1, high, SECOND_SHARE, values, ("sig_a", "sig_c", "room_a"))
         pick(2)
         quantize_h(((1, 0),), values, words(HALF, "h_codes10"), plane(HALF, "h_planes10"))
         pick(3)
-        ahead = sigmoids(0, CHUNK, high, buffer(CHUNK, "sig_b"))
-        values_third = held([P, 2 * PACK * CHUNK], BF16, "values10")[:]
-        scale_on_gpsimd(0, ahead, values_third[:, : PACK * CHUNK])
         for u in range(TILES):
             product(u, 0, banks[high + u][:])
         factors = room((TILES - 1) * HALF, "factors")
@@ -333,7 +335,7 @@ def tile_list_pitch_control_rescale_kernel(
                 scaled[:, t, :2, :],
                 sig[:, t, :].rearrange("p (c e) -> p c e", c=2),
                 ACT.Copy,
-                scale=gain_sb[:, 1, t : t + 1],
+                scale=gain_sb[1][:, t : t + 1],
             )
         interleave(scaled[:, :, 0, :], values_third[:, PACK * CHUNK :])
         quantize_h(((0, third), (1, third)), values_third, words(HALF, "h_codes2"), plane(HALF, "h_planes2"))
@@ -348,7 +350,7 @@ def tile_list_pitch_control_rescale_kernel(
             add_bias(u, banks[low + u][:, :CHUNK], narrow[:, u * CHUNK : (u + 1) * CHUNK])
             rescale(u, third, narrow[:, u * CHUNK : (u + 1) * CHUNK])
         gains(0, last, scaled[:, :, 2, :])
-        values = held([P, PACK * HALF], BF16, "handed_on")[:]
+        values = held([P, PACK * HALF], BF16, "values10")[:]
         nc.scalar.copy(
             values.rearrange("p (c e i t) -> p c e t i", c=2, i=4, t=PACK),
             scaled[:, :, 1:, :].rearrange("p t c (e i) -> p c e t i", i=4),

@@ -27,7 +27,8 @@ HALF = 512
 CHUNK = 256
 TILES = N // P
 FIRST_SHARE = 192
-SECOND_SHARE = 192
+SECOND_SHARE = 256
+THIRD_SHARE = 192
 BANKS = 8
 
 
@@ -312,15 +313,16 @@ def tile_list_pitch_control_rescale_kernel(
         quantize_h(((0, 0),), values, codes[:], plane(HALF, "h_planes00"))
         pick(1)
         sums(0, third, CHUNK, low, as_loaded)
-        values_third = held([P, 2 * PACK * CHUNK], BF16, "handed_on")[:]
-        scale_on_gpsimd(0, sigmoids(0, CHUNK, low, buffer(CHUNK, "sig_b")), values_third[:, : PACK * CHUNK])
+        ahead = sigmoids(0, CHUNK, low, buffer(CHUNK, "sig_b"))
         sums(1, 0, HALF, high, away_first)
         sums(1, HALF, HALF, low, last_first)
-        values = held([P, PACK * HALF], BF16, "values10")[:]
-        shared_half(1, high, SECOND_SHARE, values, ("sig_a", "sig_c", "room_a"))
+        values = held([P, PACK * HALF], BF16, "handed_on")[:]
+        shared_half(1, high, SECOND_SHARE, values, ("sig_c", "sig_a", "room_a"))
         pick(2)
         quantize_h(((1, 0),), values, words(HALF, "h_codes10"), plane(HALF, "h_planes10"))
         pick(3)
+        values_third = held([P, 2 * PACK * CHUNK], BF16, "handed_on")[:]
+        scale_on_gpsimd(0, ahead[:, :, :THIRD_SHARE], values_third[:, : PACK * THIRD_SHARE])
         for u in range(TILES):
             product(u, 0, banks[high + u][:])
         factors = room((TILES - 1) * HALF, "factors")
@@ -328,16 +330,21 @@ def tile_list_pitch_control_rescale_kernel(
             add_bias(u, banks[high + u][:], factors[:, u * HALF : (u + 1) * HALF])
             rescale(u, 0, factors[:, u * HALF : (u + 1) * HALF])
         sig = sigmoids(1, HALF, low, buffer(HALF, "h_codes10"))
-        staged = room(6 * CHUNK, "room_b")
-        scaled = staged.bitcast(BF16).rearrange("p (c t e) -> p t c e", c=3, t=PACK)
+        left = CHUNK - THIRD_SHARE
+        staged = room(PACK * HALF, "room_b")
+        both = staged.bitcast(BF16).rearrange("p (c t e) -> p c t e", c=2, t=PACK)
+        scaled_third = both[:, 0, :, THIRD_SHARE:]
+        scaled = both[:, 1]
+        quarters = staged.bitcast(BF16).rearrange("p (n e) -> p n e", e=CHUNK)
+        gains(0, ahead[:, :, THIRD_SHARE:], scaled_third[:, :, :left])
         for t in range(PACK):
             nc.scalar.activation(
-                scaled[:, t, :2, :],
+                quarters[:, 2 * t + 1 : 2 * t + 2 * PACK + 1 : 2 * PACK - 1, :],
                 sig[:, t, :].rearrange("p (c e) -> p c e", c=2),
                 ACT.Copy,
                 scale=gain_sb[1][:, t : t + 1],
             )
-        interleave(scaled[:, :, 0, :], values_third[:, PACK * CHUNK :])
+        interleave(scaled_third, values_third[:, PACK * THIRD_SHARE :])
         quantize_h(((0, third), (1, third)), values_third, words(HALF, "h_codes2"), plane(HALF, "h_planes2"))
         add_bias(TILES - 1, banks[high + TILES - 1][:], staged[:, :HALF])
         rescale(TILES - 1, 0, staged[:, :HALF])
@@ -349,12 +356,9 @@ def tile_list_pitch_control_rescale_kernel(
         for u in range(2):
             add_bias(u, banks[low + u][:, :CHUNK], narrow[:, u * CHUNK : (u + 1) * CHUNK])
             rescale(u, third, narrow[:, u * CHUNK : (u + 1) * CHUNK])
-        gains(0, last, scaled[:, :, 2, :])
+        gains(0, last, scaled[:, :, CHUNK:])
         values = held([P, PACK * HALF], BF16, "values10")[:]
-        nc.scalar.copy(
-            values.rearrange("p (c e i t) -> p c e t i", c=2, i=4, t=PACK),
-            scaled[:, :, 1:, :].rearrange("p t c (e i) -> p c e t i", i=4),
-        )
+        interleave(scaled, values)
         quantize_h(((1, fourth), (0, fourth)), values, words(HALF, "h_codes3"), plane(HALF, "h_planes3"))
         add_bias(2, banks[low + 2][:, :CHUNK], staged[:, 2 * HALF : 2 * HALF + CHUNK])
         rescale(2, third, staged[:, 2 * HALF : 2 * HALF + CHUNK])

@@ -323,15 +323,22 @@ def tile_list_pitch_control_rescale_kernel(
         pick(3)
         values_third = held([P, 2 * PACK * CHUNK], BF16, "handed_on")[:]
         scale_on_gpsimd(0, ahead[:, :, :THIRD_SHARE], values_third[:, : PACK * THIRD_SHARE])
-        for u in range(TILES):
-            product(u, 0, banks[high + u][:])
+        first_banks = banks[high : high + TILES - 1] + [banks[low]]
+        for u in range(TILES - 1):
+            product(u, 0, first_banks[u][:])
         factors = room((TILES - 1) * HALF, "factors")
         for u in range(TILES - 1):
-            add_bias(u, banks[high + u][:], factors[:, u * HALF : (u + 1) * HALF])
+            add_bias(u, first_banks[u][:], factors[:, u * HALF : (u + 1) * HALF])
             rescale(u, 0, factors[:, u * HALF : (u + 1) * HALF])
-        sig = sigmoids(1, HALF, low, buffer(HALF, "h_codes10"))
+        early_sig = held([P, PACK - 1, HALF], F32, "early_sig")
+        sig = [early_sig[:, t, :] for t in range(PACK - 1)]
+        for t in range(PACK):
+            if t == PACK - 1:
+                product(TILES - 1, 0, first_banks[-1][:])
+                sig.append(room(HALF, "h_codes10"))
+            nc.scalar.activation(sig[t], banks[low + t][:], ACT.Sigmoid, bias=lead_sb[1][:, t : t + 1])
         left = CHUNK - THIRD_SHARE
-        staged = room(PACK * HALF, "room_b")
+        staged = room(PACK * HALF, "h_planes10")
         both = staged.bitcast(BF16).rearrange("p (c t e) -> p c t e", c=2, t=PACK)
         scaled_third = both[:, 0, :, THIRD_SHARE:]
         scaled = both[:, 1]
@@ -340,37 +347,38 @@ def tile_list_pitch_control_rescale_kernel(
         for t in range(PACK):
             nc.scalar.activation(
                 quarters[:, 2 * t + 1 : 2 * t + 2 * PACK + 1 : 2 * PACK - 1, :],
-                sig[:, t, :].rearrange("p (c e) -> p c e", c=2),
+                sig[t].rearrange("p (c e) -> p c e", c=2),
                 ACT.Copy,
                 scale=gain_sb[1][:, t : t + 1],
             )
         interleave(scaled_third, values_third[:, PACK * THIRD_SHARE :])
         quantize_h(((0, third), (1, third)), values_third, words(HALF, "h_codes2"), plane(HALF, "h_planes2"))
-        add_bias(TILES - 1, banks[high + TILES - 1][:], staged[:, :HALF])
+        add_bias(TILES - 1, first_banks[-1][:], staged[:, :HALF])
         rescale(TILES - 1, 0, staged[:, :HALF])
         sums(0, fourth, CHUNK, high, as_loaded)
         for u in range(TILES):
             product(u, third, banks[low + u][:, :CHUNK])
         last = sigmoids(0, CHUNK, high, buffer(CHUNK, "sig_c"))
-        narrow = room(5 * CHUNK, "narrow")
-        for u in range(2):
-            add_bias(u, banks[low + u][:, :CHUNK], narrow[:, u * CHUNK : (u + 1) * CHUNK])
-            rescale(u, third, narrow[:, u * CHUNK : (u + 1) * CHUNK])
         gains(0, last, scaled[:, :, CHUNK:])
+        narrow = room(3 * CHUNK, "narrow")
+        add_bias(0, banks[low][:, :CHUNK], narrow[:, :CHUNK])
+        rescale(0, third, narrow[:, :CHUNK])
         values = held([P, PACK * HALF], BF16, "values10")[:]
         interleave(scaled, values)
         quantize_h(((1, fourth), (0, fourth)), values, words(HALF, "h_codes3"), plane(HALF, "h_planes3"))
-        add_bias(2, banks[low + 2][:, :CHUNK], staged[:, 2 * HALF : 2 * HALF + CHUNK])
-        rescale(2, third, staged[:, 2 * HALF : 2 * HALF + CHUNK])
-        for u in range(TILES - 1):
+        add_bias(1, banks[low + 1][:, :CHUNK], staged[:, 2 * HALF : 2 * HALF + CHUNK])
+        rescale(1, third, staged[:, 2 * HALF : 2 * HALF + CHUNK])
+        for u in range(2):
             product(u, fourth, banks[high + u][:, :CHUNK])
-            factor = narrow[:, (u + 2) * CHUNK : (u + 3) * CHUNK]
+            factor = narrow[:, (u + 1) * CHUNK : (u + 2) * CHUNK]
             add_bias(u, banks[high + u][:, :CHUNK], factor)
             rescale(u, fourth, factor)
-        wide = room(HALF, "wide")
-        product(TILES - 1, fourth, banks[low + TILES - 1][:, CHUNK:])
-        add_bias(TILES - 1, banks[low + TILES - 1][:], wide)
-        rescale(TILES - 1, third, wide)
+        wide = room(2 * HALF, "wide")
+        for u in range(2, TILES):
+            product(u, fourth, banks[low + u][:, CHUNK:])
+            factor = wide[:, (u - 2) * HALF : (u - 1) * HALF]
+            add_bias(u, banks[low + u][:], factor)
+            rescale(u, third, factor)
 
         for u in range(TILES):
             nc.sync.dma_start(out[u * P : (u + 1) * P, :], map_sb[u][:])

@@ -28,7 +28,7 @@ CHUNK = 256
 TILES = N // P
 FIRST_SHARE = 192
 SECOND_SHARE = 256
-THIRD_SHARE = 192
+THIRD_SHARE = 128
 BANKS = 8
 
 
@@ -45,6 +45,11 @@ def tile_list_pitch_control_rescale_kernel(
         def held(shape, dtype, name, pool=keep):
             return pool.tile(shape, dtype, name=name, align_bytes=64)
 
+        wa_raw = held([P, PASSES * 2 * H], U8, "wa_raw")
+        nc.sync.dma_start(
+            wa_raw[:].bitcast(I32).rearrange("p (a w) -> p a w", a=PASSES),
+            wa_words.bitcast(I32).rearrange("a p w -> p a w"),
+        )
         offsets = keep.tile([P, S // PER_COLUMN], U16, name="offsets")
         nc.sync.dma_start(offsets[:], offs)
 
@@ -104,11 +109,6 @@ def tile_list_pitch_control_rescale_kernel(
                     tab_rows[r:P:QUADRANT, :].bitcast(I32), tab_scales[0, r:PLANE_ROWS:PACK, :].bitcast(I32)
                 )
             nc.sync.dma_start(tab_rows[PACK : PACK + PLANE_ROWS, :].bitcast(I32), tab_scales[1].bitcast(I32))
-            wa_raw = held([P, PASSES * 2 * H], U8, "wa_raw")
-            nc.sync.dma_start(
-                wa_raw[:].bitcast(I32).rearrange("p (a w) -> p a w", a=PASSES),
-                wa_words.bitcast(I32).rearrange("a p w -> p a w"),
-            )
             load_tab(0, keep)
             load_planes(wa_rows, wa_scales)
             lead_sb = [load_vector(lead, 0, "lead0", keep)]
@@ -226,7 +226,7 @@ def tile_list_pitch_control_rescale_kernel(
                     ACT.Sigmoid,
                     bias=lead_sb[b][:, t : t + 1],
                 )
-            return sig[:]
+            return sig
 
         h_codes = {}
         h_planes = {}
@@ -284,7 +284,7 @@ def tile_list_pitch_control_rescale_kernel(
             return held([P, width], F32, name)[:]
 
         def buffer(width, name):
-            return held([P, PACK, width], F32, name)
+            return held([P, PACK, width], F32, name)[:]
 
         def words(width, name):
             return held([P, width], U32, name)[:]
@@ -330,8 +330,8 @@ def tile_list_pitch_control_rescale_kernel(
         for u in range(TILES - 1):
             add_bias(u, first_banks[u][:], factors[:, u * HALF : (u + 1) * HALF])
             rescale(u, 0, factors[:, u * HALF : (u + 1) * HALF])
-        early_sig = held([P, PACK - 1, HALF], F32, "early_sig")
-        sig = [early_sig[:, t, :] for t in range(PACK - 1)]
+        early_sig = room((PACK + 1) * HALF, "room_a")
+        sig = [early_sig[:, t * HALF : (t + 1) * HALF] for t in range(PACK - 1)]
         for t in range(PACK):
             if t == PACK - 1:
                 product(TILES - 1, 0, first_banks[-1][:])
@@ -358,19 +358,19 @@ def tile_list_pitch_control_rescale_kernel(
         sums(0, fourth, CHUNK, high, as_loaded)
         for u in range(TILES):
             product(u, third, banks[low + u][:, :CHUNK])
-        last = sigmoids(0, CHUNK, high, buffer(CHUNK, "sig_c"))
+        last = sigmoids(0, CHUNK, high, early_sig[:, (PACK - 1) * HALF :].rearrange("p (t e) -> p t e", t=PACK))
         gains(0, last, scaled[:, :, CHUNK:])
-        narrow = room(3 * CHUNK, "narrow")
-        add_bias(0, banks[low][:, :CHUNK], narrow[:, :CHUNK])
-        rescale(0, third, narrow[:, :CHUNK])
         values = held([P, PACK * HALF], BF16, "values10")[:]
         interleave(scaled, values)
         quantize_h(((1, fourth), (0, fourth)), values, words(HALF, "h_codes3"), plane(HALF, "h_planes3"))
-        add_bias(1, banks[low + 1][:, :CHUNK], staged[:, 2 * HALF : 2 * HALF + CHUNK])
-        rescale(1, third, staged[:, 2 * HALF : 2 * HALF + CHUNK])
+        for u in range(2):
+            factor = staged[:, 2 * HALF + u * CHUNK : 2 * HALF + (u + 1) * CHUNK]
+            add_bias(u, banks[low + u][:, :CHUNK], factor)
+            rescale(u, third, factor)
+        narrow = room(2 * CHUNK, "narrow")
         for u in range(2):
             product(u, fourth, banks[high + u][:, :CHUNK])
-            factor = narrow[:, (u + 1) * CHUNK : (u + 2) * CHUNK]
+            factor = narrow[:, u * CHUNK : (u + 1) * CHUNK]
             add_bias(u, banks[high + u][:, :CHUNK], factor)
             rescale(u, fourth, factor)
         wide = room(2 * HALF, "wide")

@@ -26,8 +26,8 @@ PER_COLUMN = 16
 HALF = 512
 CHUNK = 256
 TILES = N // P
-FIRST_SHARE = 192
-SECOND_SHARE = 256
+FIRST_SHARE = 176
+SECOND_SHARE = 272
 THIRD_SHARE = 128
 BANKS = 8
 

@@ -26,8 +26,7 @@ PER_COLUMN = 16
 HALF = 512
 CHUNK = 256
 TILES = N // P
-FIRST_SHARE = 176
-SECOND_SHARE = 272
+SECOND_SHARE = 256
 THIRD_SHARE = 128
 BANKS = 8
 
@@ -126,18 +125,20 @@ def tile_list_pitch_control_rescale_kernel(
         load_tab(1, late)
         load_wh(1, 0, late)
         gain_sb = [load_vector(gain, 0, "gain0", late)]
-        load_map(0, late, "map_sb0")
         load_wh(1, 1, laid)
         lead_sb.append(load_vector(lead, 1, "lead1", late))
+        load_map(0, late, "map_sb0")
         gain_sb.append(load_vector(gain, 1, "gain1", late))
         for u in range(1, TILES - 1):
             load_map(u, late, f"map_sb{u}")
 
         v_codes = {}
 
-        def gather_words(a, first, count):
+        def gather_words(a, first, count, piece=None):
             words = held([P, count], U32, f"v_codes{a}{first}")
-            nc.vector.tensor_copy(words[:], tab_sb[a][:].indirect(entries(first, count)))
+            piece = piece or count
+            for e in range(0, count, piece):
+                nc.vector.tensor_copy(words[:, e : e + piece], tab_sb[a][:].indirect(entries(first + e, piece)))
             for e in range(0, count, CHUNK):
                 v_codes[a, first + e] = words[:, e:]
 
@@ -148,10 +149,7 @@ def tile_list_pitch_control_rescale_kernel(
             grouped = {}
             src = wh_raw[b, a][:].rearrange("p j (m t) -> p m j t", t=PACK)
             for t in range(0, PACK, 2):
-                if (b, a, t) == (1, 0, 2):
-                    grouped[t] = held([P, 2 * PASS], BF16, "handed_on")
-                else:
-                    grouped[t] = ring.tile([P, 2 * PASS], BF16, name=f"wh_grouped{t}", align_bytes=64)
+                grouped[t] = ring.tile([P, 2 * PASS], BF16, name=f"wh_grouped{t}", align_bytes=64)
                 dst = grouped[t][:].rearrange("p (t m j) -> p m j t", t=2, j=PACK)
                 if (b, a) == (0, 0) or (b, a, t) == (0, 1, 2):
                     nc.scalar.activation(dst, src[:, :, :, t : t + 2], ACT.Copy, scale=-1.0)
@@ -179,14 +177,13 @@ def tile_list_pitch_control_rescale_kernel(
         nc.vector.tensor_copy(reordered(wa_planes[:]), as_given(wa_rows[:]))
         quantize_wh(0, 0)
         quantize_wh(0, 1)
-        gather_words(1, 0, HALF)
+        gather_words(1, 0, HALF, CHUNK)
         gather_words(1, HALF, HALF)
         quantize_wh(1, 0)
-        pick(0)
         quantize_wh(1, 1)
 
-        load_map(TILES - 1, keep, "wh_raw00")
         load_planes(wa_rows[:, : PASSES * N], wo_scales, PACK)
+        load_map(TILES - 1, keep, "wh_raw00")
         wo_rows = wa_rows[PACK:P, : PASSES * N]
         wo_sb = held([P, PASSES * N], U32, "wh_raw01")
         nc.sync.dma_start(
@@ -197,7 +194,7 @@ def tile_list_pitch_control_rescale_kernel(
         with nc.allow_non_contiguous_dma("one bias value for each partition"):
             nc.sync.dma_start(bo_sb[:], bo.rearrange("(u p) -> p u", p=P))
 
-        def sums(b, first, width, bank0, order):
+        def sums(b, first, width, bank0, order, column=0):
             for t in range(PACK):
                 for i, (side, a) in enumerate(order):
                     if side == "home":
@@ -209,7 +206,7 @@ def tile_list_pitch_control_rescale_kernel(
                         weights = wa_codes[:, 2 * col : 2 * (col + P)].bitcast(FP4X4)
                         weight_plane = wa_planes[:, col : col + P]
                     nc.tensor.matmul_mx(
-                        banks[bank0 + t][:, :width],
+                        banks[bank0 + t][:, column : column + width],
                         lhsT=weights,
                         lhsT_scale=weight_plane,
                         rhs=v_codes[a, first][:, :width].bitcast(FP8X4),
@@ -260,16 +257,19 @@ def tile_list_pitch_control_rescale_kernel(
             )
 
         def product(u, part, y):
-            for b in range(PASSES):
-                cols = slice(b * N + u * P, b * N + (u + 1) * P)
+            pieces = [(key, column) for key, column in (((1, part), 0), ((0, part), 0))]
+            if part == 0:
+                pieces.append(((0, CHUNK), CHUNK))
+            for i, (key, column) in enumerate(pieces):
+                cols = slice(key[0] * N + u * P, key[0] * N + (u + 1) * P)
                 nc.tensor.matmul_mx(
-                    y,
+                    y[:, column : column + h_codes[key].shape[1]],
                     lhsT=wo_sb[:, cols].bitcast(FP8X4),
                     lhsT_scale=wo_rows[:, cols],
-                    rhs=h_codes[b, part].bitcast(FP8X4),
-                    rhs_scale=h_planes[b, part],
-                    start=(b == 0),
-                    stop=(b == PASSES - 1),
+                    rhs=h_codes[key].bitcast(FP8X4),
+                    rhs_scale=h_planes[key],
+                    start=(i == 0),
+                    stop=(i == len(pieces) - 1),
                 )
 
         def add_bias(u, y, factor):
@@ -306,22 +306,35 @@ def tile_list_pitch_control_rescale_kernel(
         last_first = as_loaded[::-1]
         third, fourth = HALF, HALF + CHUNK
 
-        sums(0, 0, HALF, low, as_loaded)
-        values = held([P, PACK * HALF], BF16, "handed_on")[:]
-        shared_half(0, low, FIRST_SHARE, values, ("sig_a", "sig_b", "room_a"))
-        codes = laid.tile([P, HALF], U32, name="h_codes_first", align_bytes=64, offset=0)
-        quantize_h(((0, 0),), values, codes[:], plane(HALF, "h_planes00"))
+        sums(0, 0, CHUNK, low, as_loaded)
+        values = held([P, PACK * CHUNK], BF16, "handed_on")[:]
+        scaled = by_slice(room(HALF, "room_first"), CHUNK)
+        sig = sigmoids(0, CHUNK, low, buffer(CHUNK, "sig_b"))
+        sums(0, CHUNK, CHUNK, low, as_loaded, CHUNK)
+        gains(0, sig, scaled)
+        interleave(scaled, values)
+        codes = laid.tile([P, CHUNK], U32, name="h_codes_first", align_bytes=64, offset=0)
+        quantize_h(((0, 0),), values, codes[:], plane(CHUNK, "h_planes00"))
+        pick(0)
         pick(1)
-        sums(0, third, CHUNK, low, as_loaded)
-        ahead = sigmoids(0, CHUNK, low, buffer(CHUNK, "sig_b"))
+        values_next = held([P, PACK * CHUNK], BF16, "handed_on")[:]
+        scale_on_gpsimd(0, sigmoids(0, CHUNK, low, buffer(CHUNK, "sig_b"), CHUNK), values_next)
         sums(1, 0, HALF, high, away_first)
+        values = held([P, PACK * HALF], BF16, "values_second")[:]
+        rest = HALF - SECOND_SHARE
+        scale_on_gpsimd(1, sigmoids(1, SECOND_SHARE, high, buffer(SECOND_SHARE, "sig_c"), rest), values[:, PACK * rest :])
+        sig = sigmoids(1, rest, high, buffer(rest, "sig_a"))
+        scaled = by_slice(laid.tile([P, 2 * rest], F32, name="room_second", align_bytes=64, offset=8192 + 10240 - 1024)[:], rest)
+        gains(1, sig, scaled)
+        interleave(scaled, values[:, : PACK * rest])
+        sums(0, third, CHUNK, high, as_loaded)
         sums(1, HALF, HALF, low, last_first)
-        values = held([P, PACK * HALF], BF16, "handed_on")[:]
-        shared_half(1, high, SECOND_SHARE, values, ("sig_c", "sig_a", "room_a"))
+        ahead = sigmoids(0, CHUNK, high, laid.tile([P, PACK, CHUNK], F32, name="ahead", align_bytes=64, offset=8192 + 10240)[:])
         pick(2)
-        quantize_h(((1, 0),), values, words(HALF, "h_codes10"), plane(HALF, "h_planes10"))
+        quantize_h(((0, CHUNK),), values_next, words(CHUNK, "h_codes01"), wa_rows[:, :CHUNK])
+        quantize_h(((1, 0),), values, words(HALF, "h_codes10"), wa_rows[:, N : N + HALF])
         pick(3)
-        values_third = held([P, 2 * PACK * CHUNK], BF16, "handed_on")[:]
+        values_third = held([P, 2 * PACK * CHUNK], BF16, "values_second")[:]
         scale_on_gpsimd(0, ahead[:, :, :THIRD_SHARE], values_third[:, : PACK * THIRD_SHARE])
         first_banks = banks[high : high + TILES - 1] + [banks[low]]
         for u in range(TILES - 1):
@@ -330,7 +343,7 @@ def tile_list_pitch_control_rescale_kernel(
         for u in range(TILES - 1):
             add_bias(u, first_banks[u][:], factors[:, u * HALF : (u + 1) * HALF])
             rescale(u, 0, factors[:, u * HALF : (u + 1) * HALF])
-        early_sig = room((PACK + 1) * HALF, "room_a")
+        early_sig = laid.tile([P, (PACK + 1) * HALF], F32, name="early_sig", align_bytes=64, offset=8192)[:]
         sig = [early_sig[:, t * HALF : (t + 1) * HALF] for t in range(PACK - 1)]
         for t in range(PACK):
             if t == PACK - 1:
@@ -338,7 +351,7 @@ def tile_list_pitch_control_rescale_kernel(
                 sig.append(room(HALF, "h_codes10"))
             nc.scalar.activation(sig[t], banks[low + t][:], ACT.Sigmoid, bias=lead_sb[1][:, t : t + 1])
         left = CHUNK - THIRD_SHARE
-        staged = room(PACK * HALF, "h_planes10")
+        staged = room(PACK * HALF, "h_codes01")
         both = staged.bitcast(BF16).rearrange("p (c t e) -> p c t e", c=2, t=PACK)
         scaled_third = both[:, 0, :, THIRD_SHARE:]
         scaled = both[:, 1]

@@ -24,11 +24,15 @@ QUADRANT = 32
 PLANE_ROWS = PASS // 32
 PER_COLUMN = 16
 HALF = 512
-CHUNK = 256
+QUARTER = 256
+SECOND, THIRD, FOURTH = QUARTER, 2 * QUARTER, 3 * QUARTER
 TILES = N // P
-SECOND_SHARE = 256
-THIRD_SHARE = 128
 BANKS = 8
+HALF_SHARE = 256
+LAST_SHARE = 128
+LATE_SIGMOIDS = PACK * PASS * 4
+THIRD_SIGMOIDS = LATE_SIGMOIDS + (PACK + 1) * HALF * 4
+STAGED_HALF = THIRD_SIGMOIDS - 1024
 
 
 def tile_list_pitch_control_rescale_kernel(
@@ -68,13 +72,13 @@ def tile_list_pitch_control_rescale_kernel(
             tab_sb[a] = held([P, T], U32, f"tab_sb{a}", pool)
             nc.sync.dma_start(tab_sb[a][:].bitcast(I32), tab_words[a].rearrange("p t i -> p (t i)").bitcast(I32))
 
-        def load_wh(b, a, pool):
-            if (b, a) == (1, 1):
-                wh_raw[b, a] = pool.tile([P, PACK, PASS], F32, name="wh_last", align_bytes=64, offset=0)
-            else:
-                wh_raw[b, a] = held([P, PACK, PASS], F32, f"wh_raw{b}{a}", pool)
+        def load_wh(b, a, raw):
+            wh_raw[b, a] = raw
             rows = wh[a * PASS : (a + 1) * PASS, b * PASS : (b + 1) * PASS]
-            nc.sync.dma_start(wh_raw[b, a][:], rows.rearrange("(p j) c -> p j c", j=PACK))
+            nc.sync.dma_start(raw[:], rows.rearrange("(p j) c -> p j c", j=PACK))
+
+        def wh_buffer(name, pool):
+            return held([P, PACK, PASS], F32, name, pool)
 
         def load_map(u, pool, name):
             map_sb[u] = held([P, T], F32, name, pool)
@@ -92,11 +96,11 @@ def tile_list_pitch_control_rescale_kernel(
                     scales[:, r:PLANE_ROWS:PACK, :].bitcast(I32).rearrange("a q w -> q a w"),
                 )
 
-        def reordered(ap):
-            return ap.rearrange("p (g t m) -> p g t m", t=PACK, m=P)
-
-        def as_given(ap):
-            return ap.rearrange("p (g m t) -> p g t m", t=PACK, m=P)
+        def reorder_columns(copy, dst, src):
+            copy(
+                dst.rearrange("p (g t m) -> p g t m", t=PACK, m=P),
+                src.rearrange("p (g m t) -> p g t m", t=PACK, m=P),
+            )
 
         v_plane = [held([P, S], U8, "v_plane0")]
         with tc.tile_pool(name="early", bufs=1) as early:
@@ -111,8 +115,8 @@ def tile_list_pitch_control_rescale_kernel(
             load_tab(0, keep)
             load_planes(wa_rows, wa_scales)
             lead_sb = [load_vector(lead, 0, "lead0", keep)]
-            load_wh(0, 0, keep)
-            load_wh(0, 1, keep)
+            load_wh(0, 0, wh_buffer("wh_raw00", keep))
+            load_wh(0, 1, wh_buffer("wh_raw01", keep))
             nc.vector.tensor_copy(v_plane[0][:], tab_rows[:].indirect(offsets[:]))
         for q in range(P // QUADRANT):
             nc.sync.dma_start(
@@ -122,36 +126,39 @@ def tile_list_pitch_control_rescale_kernel(
 
         late = ctx.enter_context(tc.tile_pool(name="late", bufs=1))
         laid = ctx.enter_context(tc.tile_pool(name="laid", bufs=1))
+
+        def placed(shape, dtype, name, offset):
+            return laid.tile(shape, dtype, name=name, align_bytes=64, offset=offset)
+
         load_tab(1, late)
-        load_wh(1, 0, late)
+        load_wh(1, 0, wh_buffer("wh_raw10", late))
         gain_sb = [load_vector(gain, 0, "gain0", late)]
-        load_wh(1, 1, laid)
-        lead_sb.append(load_vector(lead, 1, "lead1", late))
+        load_wh(1, 1, placed([P, PACK, PASS], F32, "wh_last", 0))
         load_map(0, late, "map_sb0")
+        lead_sb.append(load_vector(lead, 1, "lead1", late))
         gain_sb.append(load_vector(gain, 1, "gain1", late))
         for u in range(1, TILES - 1):
             load_map(u, late, f"map_sb{u}")
 
         v_codes = {}
 
-        def gather_words(a, first, count, piece=None):
+        def gather_words(a, first, count, piece):
             words = held([P, count], U32, f"v_codes{a}{first}")
-            piece = piece or count
             for e in range(0, count, piece):
                 nc.vector.tensor_copy(words[:, e : e + piece], tab_sb[a][:].indirect(entries(first + e, piece)))
-            for e in range(0, count, CHUNK):
+            for e in range(0, count, QUARTER):
                 v_codes[a, first + e] = words[:, e:]
 
         wh_codes = {}
         wh_planes = {}
 
-        def quantize_wh(b, a):
+        def quantize_wh(b, a, on_scalar):
             grouped = {}
             src = wh_raw[b, a][:].rearrange("p j (m t) -> p m j t", t=PACK)
             for t in range(0, PACK, 2):
                 grouped[t] = ring.tile([P, 2 * PASS], BF16, name=f"wh_grouped{t}", align_bytes=64)
                 dst = grouped[t][:].rearrange("p (t m j) -> p m j t", t=2, j=PACK)
-                if (b, a) == (0, 0) or (b, a, t) == (0, 1, 2):
+                if t in on_scalar:
                     nc.scalar.activation(dst, src[:, :, :, t : t + 2], ACT.Copy, scale=-1.0)
                 else:
                     nc.vector.tensor_scalar_mul(dst, src[:, :, :, t : t + 2], -1.0)
@@ -171,20 +178,20 @@ def tile_list_pitch_control_rescale_kernel(
             nc.vector.tensor_copy(picked[u][:], map_sb[u][:].indirect(offsets[:]))
 
         wa_codes = held([P, PASSES * 2 * H], U8, "wa_codes")
-        nc.scalar.copy(reordered(wa_codes[:].bitcast(U16)), as_given(wa_raw[:].bitcast(U16)))
-        gather_words(0, 0, S)
+        reorder_columns(nc.scalar.copy, wa_codes[:].bitcast(U16), wa_raw[:].bitcast(U16))
+        gather_words(0, 0, S, S)
         wa_planes = held([P, PASSES * H], U8, "wa_planes")
-        nc.vector.tensor_copy(reordered(wa_planes[:]), as_given(wa_rows[:]))
-        quantize_wh(0, 0)
-        quantize_wh(0, 1)
-        gather_words(1, 0, HALF, CHUNK)
-        gather_words(1, HALF, HALF)
-        quantize_wh(1, 0)
-        quantize_wh(1, 1)
+        reorder_columns(nc.vector.tensor_copy, wa_planes[:], wa_rows[:])
+        quantize_wh(0, 0, (0, 2))
+        quantize_wh(0, 1, (2,))
+        gather_words(1, 0, HALF, QUARTER)
+        gather_words(1, HALF, HALF, HALF)
+        quantize_wh(1, 0, ())
+        quantize_wh(1, 1, ())
 
         load_planes(wa_rows[:, : PASSES * N], wo_scales, PACK)
         load_map(TILES - 1, keep, "wh_raw00")
-        wo_rows = wa_rows[PACK:P, : PASSES * N]
+        wo_planes = wa_rows[PACK:P, : PASSES * N]
         wo_sb = held([P, PASSES * N], U32, "wh_raw01")
         nc.sync.dma_start(
             wo_sb[:].bitcast(I32).rearrange("p (b c) -> p b c", b=PASSES),
@@ -215,28 +222,15 @@ def tile_list_pitch_control_rescale_kernel(
                         stop=(i == len(order) - 1),
                     )
 
-        def sigmoids(b, width, bank0, sig, first=0):
+        def sigmoids(b, bank0, column, sig):
             for t in range(PACK):
                 nc.scalar.activation(
                     sig[:, t, :],
-                    banks[bank0 + t][:, first : first + width],
+                    banks[bank0 + t][:, column : column + sig.shape[2]],
                     ACT.Sigmoid,
                     bias=lead_sb[b][:, t : t + 1],
                 )
             return sig
-
-        h_codes = {}
-        h_planes = {}
-
-        def quantize_h(keys, values, codes, scales):
-            width = codes.shape[1] // len(keys)
-            for i, key in enumerate(keys):
-                h_codes[key] = codes[:, i * width : (i + 1) * width]
-                h_planes[key] = scales[:, i * width : (i + 1) * width]
-            nc.vector.quantize_mx(codes.bitcast(FP8X4), scales, values)
-
-        def by_slice(room, width):
-            return room.bitcast(BF16)[:, : PACK * width].rearrange("p (t e) -> p t e", t=PACK)
 
         def gains(b, sig, scaled):
             for t in range(PACK):
@@ -256,35 +250,47 @@ def tile_list_pitch_control_rescale_kernel(
                 MULT,
             )
 
-        def product(u, part, y):
-            pieces = [(key, column) for key, column in (((1, part), 0), ((0, part), 0))]
-            if part == 0:
-                pieces.append(((0, CHUNK), CHUNK))
-            for i, (key, column) in enumerate(pieces):
-                cols = slice(key[0] * N + u * P, key[0] * N + (u + 1) * P)
+        h_codes = {}
+        h_planes = {}
+
+        def quantize_h(keys, values, codes, scales):
+            width = codes.shape[1] // len(keys)
+            for i, key in enumerate(keys):
+                h_codes[key] = codes[:, i * width : (i + 1) * width]
+                h_planes[key] = scales[:, i * width : (i + 1) * width]
+            nc.vector.quantize_mx(codes.bitcast(FP8X4), scales, values)
+
+        def product(u, keys, y):
+            for i, (b, first) in enumerate(keys):
+                cols = slice(b * N + u * P, b * N + (u + 1) * P)
+                column = first - keys[0][1]
                 nc.tensor.matmul_mx(
-                    y[:, column : column + h_codes[key].shape[1]],
+                    y[:, column : column + h_codes[b, first].shape[1]],
                     lhsT=wo_sb[:, cols].bitcast(FP8X4),
-                    lhsT_scale=wo_rows[:, cols],
-                    rhs=h_codes[key].bitcast(FP8X4),
-                    rhs_scale=h_planes[key],
+                    lhsT_scale=wo_planes[:, cols],
+                    rhs=h_codes[b, first].bitcast(FP8X4),
+                    rhs_scale=h_planes[b, first],
                     start=(i == 0),
-                    stop=(i == len(pieces) - 1),
+                    stop=(i == len(keys) - 1),
                 )
 
-        def add_bias(u, y, factor):
-            nc.scalar.activation(factor, y, ACT.Identity, bias=bo_sb[:, u : u + 1])
-
-        def rescale(u, first, factor):
+        def update(u, first, y, factor):
             count = factor.shape[1]
+            nc.scalar.activation(factor, y, ACT.Identity, bias=bo_sb[:, u : u + 1])
             window = map_sb[u][:].indirect(entries(first, count))
             nc.vector.tensor_tensor(window, picked[u][:, first : first + count], factor, MULT)
 
-        def room(width, name):
+        def floats(width, name):
             return held([P, width], F32, name)[:]
 
-        def buffer(width, name):
+        def by_slice(ap):
+            return ap.rearrange("p (t e) -> p t e", t=PACK)
+
+        def sigmoid_buffer(width, name):
             return held([P, PACK, width], F32, name)[:]
+
+        def h_values(width, name):
+            return held([P, PACK * width], BF16, name)[:]
 
         def words(width, name):
             return held([P, width], U32, name)[:]
@@ -292,106 +298,99 @@ def tile_list_pitch_control_rescale_kernel(
         def plane(width, name):
             return held([P, width], U8, name)[:]
 
-        def shared_half(b, bank0, share, values, names):
-            rest = HALF - share
-            scale_on_gpsimd(b, sigmoids(b, share, bank0, buffer(share, names[0]), rest), values[:, PACK * rest :])
-            sig = sigmoids(b, rest, bank0, buffer(rest, names[1]))
-            scaled = by_slice(room(2 * rest, names[2]), rest)
-            gains(b, sig, scaled)
-            interleave(scaled, values[:, : PACK * rest])
-
         low, high = 0, PACK
         as_loaded = (("away", 0), ("home", 0), ("away", 1), ("home", 1))
         away_first = (("away", 0), ("away", 1), ("home", 0), ("home", 1))
         last_first = as_loaded[::-1]
-        third, fourth = HALF, HALF + CHUNK
+        first_half = ((1, 0), (0, 0), (0, SECOND))
+        last_tile = TILES - 1
 
-        sums(0, 0, CHUNK, low, as_loaded)
-        values = held([P, PACK * CHUNK], BF16, "handed_on")[:]
-        scaled = by_slice(room(HALF, "room_first"), CHUNK)
-        sig = sigmoids(0, CHUNK, low, buffer(CHUNK, "sig_b"))
-        sums(0, CHUNK, CHUNK, low, as_loaded, CHUNK)
+        sums(0, 0, QUARTER, low, as_loaded)
+        values = h_values(QUARTER, "values_quarter")
+        scaled = by_slice(floats(HALF, "staged_first").bitcast(BF16))
+        sig = sigmoids(0, low, 0, sigmoid_buffer(QUARTER, "sig_quarter"))
+        sums(0, SECOND, QUARTER, low, as_loaded, SECOND)
         gains(0, sig, scaled)
         interleave(scaled, values)
-        codes = laid.tile([P, CHUNK], U32, name="h_codes_first", align_bytes=64, offset=0)
-        quantize_h(((0, 0),), values, codes[:], plane(CHUNK, "h_planes00"))
+        quantize_h(((0, 0),), values, placed([P, QUARTER], U32, "h_codes00", 0)[:], plane(QUARTER, "h_planes00"))
         pick(0)
         pick(1)
-        values_next = held([P, PACK * CHUNK], BF16, "handed_on")[:]
-        scale_on_gpsimd(0, sigmoids(0, CHUNK, low, buffer(CHUNK, "sig_b"), CHUNK), values_next)
+
+        values_second = h_values(QUARTER, "values_quarter")
+        scale_on_gpsimd(0, sigmoids(0, low, SECOND, sigmoid_buffer(QUARTER, "sig_quarter")), values_second)
+
         sums(1, 0, HALF, high, away_first)
-        values = held([P, PACK * HALF], BF16, "values_second")[:]
-        rest = HALF - SECOND_SHARE
-        scale_on_gpsimd(1, sigmoids(1, SECOND_SHARE, high, buffer(SECOND_SHARE, "sig_c"), rest), values[:, PACK * rest :])
-        sig = sigmoids(1, rest, high, buffer(rest, "sig_a"))
-        scaled = by_slice(laid.tile([P, 2 * rest], F32, name="room_second", align_bytes=64, offset=8192 + 10240 - 1024)[:], rest)
+        values = h_values(HALF, "values_half")
+        rest = HALF - HALF_SHARE
+        scale_on_gpsimd(1, sigmoids(1, high, rest, sigmoid_buffer(HALF_SHARE, "sig_share")), values[:, PACK * rest :])
+        sig = sigmoids(1, high, 0, sigmoid_buffer(rest, "sig_rest"))
+        scaled = by_slice(placed([P, 2 * rest], F32, "staged_half", STAGED_HALF)[:].bitcast(BF16))
         gains(1, sig, scaled)
         interleave(scaled, values[:, : PACK * rest])
-        sums(0, third, CHUNK, high, as_loaded)
+        sums(0, THIRD, QUARTER, high, as_loaded)
         sums(1, HALF, HALF, low, last_first)
-        ahead = sigmoids(0, CHUNK, high, laid.tile([P, PACK, CHUNK], F32, name="ahead", align_bytes=64, offset=8192 + 10240)[:])
+        sig_third = sigmoids(0, high, 0, placed([P, PACK, QUARTER], F32, "sig_third", THIRD_SIGMOIDS)[:])
         pick(2)
-        quantize_h(((0, CHUNK),), values_next, words(CHUNK, "h_codes01"), wa_rows[:, :CHUNK])
+        quantize_h(((0, SECOND),), values_second, words(QUARTER, "h_codes01"), wa_rows[:, :QUARTER])
         quantize_h(((1, 0),), values, words(HALF, "h_codes10"), wa_rows[:, N : N + HALF])
-        pick(3)
-        values_third = held([P, 2 * PACK * CHUNK], BF16, "values_second")[:]
-        scale_on_gpsimd(0, ahead[:, :, :THIRD_SHARE], values_third[:, : PACK * THIRD_SHARE])
-        first_banks = banks[high : high + TILES - 1] + [banks[low]]
-        for u in range(TILES - 1):
-            product(u, 0, first_banks[u][:])
-        factors = room((TILES - 1) * HALF, "factors")
-        for u in range(TILES - 1):
-            add_bias(u, first_banks[u][:], factors[:, u * HALF : (u + 1) * HALF])
-            rescale(u, 0, factors[:, u * HALF : (u + 1) * HALF])
-        early_sig = laid.tile([P, (PACK + 1) * HALF], F32, name="early_sig", align_bytes=64, offset=8192)[:]
-        sig = [early_sig[:, t * HALF : (t + 1) * HALF] for t in range(PACK - 1)]
-        for t in range(PACK):
-            if t == PACK - 1:
-                product(TILES - 1, 0, first_banks[-1][:])
-                sig.append(room(HALF, "h_codes10"))
-            nc.scalar.activation(sig[t], banks[low + t][:], ACT.Sigmoid, bias=lead_sb[1][:, t : t + 1])
-        left = CHUNK - THIRD_SHARE
-        staged = room(PACK * HALF, "h_codes01")
-        both = staged.bitcast(BF16).rearrange("p (c t e) -> p c t e", c=2, t=PACK)
-        scaled_third = both[:, 0, :, THIRD_SHARE:]
-        scaled = both[:, 1]
-        quarters = staged.bitcast(BF16).rearrange("p (n e) -> p n e", e=CHUNK)
-        gains(0, ahead[:, :, THIRD_SHARE:], scaled_third[:, :, :left])
+        pick(last_tile)
+        values_third = h_values(HALF, "values_half")
+        scale_on_gpsimd(0, sig_third[:, :, :LAST_SHARE], values_third[:, : PACK * LAST_SHARE])
+
+        for u in range(last_tile):
+            product(u, first_half, banks[high + u][:])
+        factors = floats(last_tile * HALF, "factors")
+        for u in range(last_tile):
+            update(u, 0, banks[high + u][:], factors[:, u * HALF : (u + 1) * HALF])
+
+        late_sigmoids = placed([P, (PACK + 1) * HALF], F32, "late_sigmoids", LATE_SIGMOIDS)[:]
+
+        def wide_sigmoid(t, sig_t):
+            nc.scalar.activation(sig_t, banks[low + t][:], ACT.Sigmoid, bias=lead_sb[1][:, t : t + 1])
+            return sig_t
+
+        sig_wide = [wide_sigmoid(t, late_sigmoids[:, t * HALF : (t + 1) * HALF]) for t in range(PACK - 1)]
+        product(last_tile, first_half, banks[low][:])
+        sig_wide.append(wide_sigmoid(PACK - 1, floats(HALF, "h_codes10")))
+
+        staged = floats(PACK * HALF, "h_codes01")
+        by_quarter = staged.bitcast(BF16).rearrange("p (c t e) -> p c t e", c=2, t=PACK)
+        scaled_third = by_quarter[:, 0, :, LAST_SHARE:]
+        scaled_fourth = by_quarter[:, 1]
+        runs = staged.bitcast(BF16).rearrange("p (n e) -> p n e", e=QUARTER)
+        gains(0, sig_third[:, :, LAST_SHARE:], scaled_third[:, :, : QUARTER - LAST_SHARE])
         for t in range(PACK):
             nc.scalar.activation(
-                quarters[:, 2 * t + 1 : 2 * t + 2 * PACK + 1 : 2 * PACK - 1, :],
-                sig[t].rearrange("p (c e) -> p c e", c=2),
+                runs[:, 2 * t + 1 : 2 * t + 2 * PACK + 1 : 2 * PACK - 1, :],
+                sig_wide[t].rearrange("p (c e) -> p c e", c=2),
                 ACT.Copy,
                 scale=gain_sb[1][:, t : t + 1],
             )
-        interleave(scaled_third, values_third[:, PACK * THIRD_SHARE :])
-        quantize_h(((0, third), (1, third)), values_third, words(HALF, "h_codes2"), plane(HALF, "h_planes2"))
-        add_bias(TILES - 1, first_banks[-1][:], staged[:, :HALF])
-        rescale(TILES - 1, 0, staged[:, :HALF])
-        sums(0, fourth, CHUNK, high, as_loaded)
+        interleave(scaled_third, values_third[:, PACK * LAST_SHARE :])
+        quantize_h(((0, THIRD), (1, THIRD)), values_third, words(HALF, "h_codes2"), plane(HALF, "h_planes2"))
+        update(last_tile, 0, banks[low][:], staged[:, :HALF])
+
+        sums(0, FOURTH, QUARTER, high, as_loaded)
         for u in range(TILES):
-            product(u, third, banks[low + u][:, :CHUNK])
-        last = sigmoids(0, CHUNK, high, early_sig[:, (PACK - 1) * HALF :].rearrange("p (t e) -> p t e", t=PACK))
-        gains(0, last, scaled[:, :, CHUNK:])
-        values = held([P, PACK * HALF], BF16, "values10")[:]
-        interleave(scaled, values)
-        quantize_h(((1, fourth), (0, fourth)), values, words(HALF, "h_codes3"), plane(HALF, "h_planes3"))
+            product(u, ((1, THIRD), (0, THIRD)), banks[low + u][:, :QUARTER])
+        sig = sigmoids(0, high, 0, by_slice(late_sigmoids[:, (PACK - 1) * HALF :]))
+        gains(0, sig, scaled_fourth[:, :, QUARTER:])
+        values = h_values(HALF, "values_fourth")
+        interleave(scaled_fourth, values)
+        quantize_h(((1, FOURTH), (0, FOURTH)), values, words(HALF, "h_codes3"), plane(HALF, "h_planes3"))
+
+        fourth = ((1, FOURTH), (0, FOURTH))
         for u in range(2):
-            factor = staged[:, 2 * HALF + u * CHUNK : 2 * HALF + (u + 1) * CHUNK]
-            add_bias(u, banks[low + u][:, :CHUNK], factor)
-            rescale(u, third, factor)
-        narrow = room(2 * CHUNK, "narrow")
+            at = 2 * HALF + u * QUARTER
+            update(u, THIRD, banks[low + u][:, :QUARTER], staged[:, at : at + QUARTER])
+        narrow = floats(2 * QUARTER, "narrow_factors")
         for u in range(2):
-            product(u, fourth, banks[high + u][:, :CHUNK])
-            factor = narrow[:, u * CHUNK : (u + 1) * CHUNK]
-            add_bias(u, banks[high + u][:, :CHUNK], factor)
-            rescale(u, fourth, factor)
-        wide = room(2 * HALF, "wide")
+            product(u, fourth, banks[high + u][:, :QUARTER])
+            update(u, FOURTH, banks[high + u][:, :QUARTER], narrow[:, u * QUARTER : (u + 1) * QUARTER])
+        wide = floats(2 * HALF, "wide_factors")
         for u in range(2, TILES):
-            product(u, fourth, banks[low + u][:, CHUNK:])
-            factor = wide[:, (u - 2) * HALF : (u - 1) * HALF]
-            add_bias(u, banks[low + u][:], factor)
-            rescale(u, third, factor)
+            product(u, fourth, banks[low + u][:, QUARTER:])
+            update(u, THIRD, banks[low + u][:], wide[:, (u - 2) * HALF : (u - 1) * HALF])
 
         for u in range(TILES):
             nc.sync.dma_start(out[u * P : (u + 1) * P, :], map_sb[u][:])

@@ -1,6 +1,7 @@
 from contextlib import ExitStack
 
 import concourse.mybir as mybir
+from concourse.masks import make_identity
 
 K, H, N, T, S = 1024, 1024, 512, 2048, 1024
 FLOPS = 2 * S * (2 * K * H + H * N)
@@ -28,6 +29,7 @@ QUARTER = 256
 SECOND, THIRD, FOURTH = QUARTER, 2 * QUARTER, 3 * QUARTER
 TILES = N // P
 BANKS = 8
+VECTOR_ROW = 20
 HALF_SHARE = 256
 LAST_SHARE = 128
 LATE_SIGMOIDS = PACK * PASS * 4
@@ -84,10 +86,8 @@ def tile_list_pitch_control_rescale_kernel(
             map_sb[u] = held([P, T], F32, name, pool)
             nc.sync.dma_start(map_sb[u][:], gT[u * P : (u + 1) * P, :])
 
-        def load_vector(vector, b, name, pool):
-            values = held([P, PACK], F32, name, pool)
-            nc.sync.dma_start(values[:], vector[b * PASS : (b + 1) * PASS].rearrange("(p t) -> p t", t=PACK))
-            return values
+        def load_vector(vector, row):
+            nc.sync.dma_start(vector_rows[row : P : 2 * QUADRANT, :], vector.rearrange("(b r) -> b r", b=PASSES))
 
         def load_planes(rows, scales, row0=0):
             for r in range(PACK):
@@ -114,7 +114,10 @@ def tile_list_pitch_control_rescale_kernel(
             nc.sync.dma_start(tab_rows[PACK : PACK + PLANE_ROWS, :].bitcast(I32), tab_scales[1].bitcast(I32))
             load_tab(0, keep)
             load_planes(wa_rows, wa_scales)
-            lead_sb = [load_vector(lead, 0, "lead0", keep)]
+            vector_rows = held([P, PASS], F32, "vector_rows")
+            nc.vector.memset(vector_rows[:], 0.0)
+            load_vector(lead, VECTOR_ROW)
+            load_vector(gain, VECTOR_ROW + 1)
             load_wh(0, 0, wh_buffer("wh_raw00", keep))
             load_wh(0, 1, wh_buffer("wh_raw01", keep))
             nc.vector.tensor_copy(v_plane[0][:], tab_rows[:].indirect(offsets[:]))
@@ -132,13 +135,20 @@ def tile_list_pitch_control_rescale_kernel(
 
         load_tab(1, late)
         load_wh(1, 0, wh_buffer("wh_raw10", late))
-        gain_sb = [load_vector(gain, 0, "gain0", late)]
         load_wh(1, 1, placed([P, PACK, PASS], F32, "wh_last", 0))
         load_map(0, late, "map_sb0")
-        lead_sb.append(load_vector(lead, 1, "lead1", late))
-        gain_sb.append(load_vector(gain, 1, "gain1", late))
         for u in range(1, TILES - 1):
             load_map(u, late, f"map_sb{u}")
+
+        identity = held([P, P], F32, "identity")
+        make_identity(nc, identity[:])
+        for t in range(PACK):
+            nc.tensor.transpose(banks[BANKS - 1][:, t * P : (t + 1) * P], vector_rows[:, t:PASS:PACK], identity[:])
+        vectors = held([P, 2, PASSES, PACK], F32, "vectors")
+        turned = banks[BANKS - 1][:].rearrange("p (t b row) -> p row b t", t=PACK, b=PASSES)
+        nc.scalar.copy(vectors[:], turned[:, VECTOR_ROW : VECTOR_ROW + 2, :, :])
+        lead_sb = [vectors[:, 0, b, :] for b in range(PASSES)]
+        gain_sb = [vectors[:, 1, b, :] for b in range(PASSES)]
 
         v_codes = {}
 
@@ -246,7 +256,7 @@ def tile_list_pitch_control_rescale_kernel(
             nc.gpsimd.tensor_tensor(
                 values.rearrange("p (e t) -> p e t", t=PACK),
                 sig.rearrange("p t e -> p e t"),
-                gain_sb[b][:].unsqueeze(1).to_broadcast([P, sig.shape[2], PACK]),
+                gain_sb[b].unsqueeze(1).to_broadcast([P, sig.shape[2], PACK]),
                 MULT,
             )
 

@@ -29,6 +29,7 @@ QUARTER = 256
 SECOND, THIRD, FOURTH = QUARTER, 2 * QUARTER, 3 * QUARTER
 TILES = N // P
 BANKS = 8
+LINE = 16
 VECTOR_ROW = 20
 HALF_SHARE = 256
 LAST_SHARE = 128
@@ -96,10 +97,10 @@ def tile_list_pitch_control_rescale_kernel(
                     scales[:, r:PLANE_ROWS:PACK, :].bitcast(I32).rearrange("a q w -> q a w"),
                 )
 
-        def reorder_columns(copy, dst, src):
+        def reorder_columns(copy, dst, src, run):
             copy(
-                dst.rearrange("p (g t m) -> p g t m", t=PACK, m=P),
-                src.rearrange("p (g m t) -> p g t m", t=PACK, m=P),
+                dst.rearrange("p (g t n m) -> p g n t m", t=PACK, n=P // run, m=run),
+                src.rearrange("p (g n m t) -> p g n t m", t=PACK, n=P // run, m=run),
             )
 
         v_plane = [held([P, S], U8, "v_plane0")]
@@ -188,10 +189,10 @@ def tile_list_pitch_control_rescale_kernel(
             nc.vector.tensor_copy(picked[u][:], map_sb[u][:].indirect(offsets[:]))
 
         wa_codes = held([P, PASSES * 2 * H], U8, "wa_codes")
-        reorder_columns(nc.scalar.copy, wa_codes[:].bitcast(U16), wa_raw[:].bitcast(U16))
+        reorder_columns(nc.scalar.copy, wa_codes[:].bitcast(U16), wa_raw[:].bitcast(U16), LINE // 2)
         gather_words(0, 0, S, S)
         wa_planes = held([P, PASSES * H], U8, "wa_planes")
-        reorder_columns(nc.vector.tensor_copy, wa_planes[:], wa_rows[:])
+        reorder_columns(nc.vector.tensor_copy, wa_planes[:], wa_rows[:], LINE)
         quantize_wh(0, 0, (0, 2))
         quantize_wh(0, 1, (2,))
         gather_words(1, 0, HALF, QUARTER)

@@ -30,6 +30,7 @@ SECOND, THIRD, FOURTH = QUARTER, 2 * QUARTER, 3 * QUARTER
 TILES = N // P
 BANKS = 8
 LINE = 16
+ALIGN = 256
 VECTOR_ROW = 20
 HALF_SHARE = 256
 LAST_SHARE = 128
@@ -49,7 +50,7 @@ def tile_list_pitch_control_rescale_kernel(
         banks = [psum.tile([P, HALF], F32, name=f"bank{i}") for i in range(BANKS)]
 
         def held(shape, dtype, name, pool=keep):
-            return pool.tile(shape, dtype, name=name, align_bytes=64)
+            return pool.tile(shape, dtype, name=name, align_bytes=ALIGN)
 
         wa_raw = held([P, PASSES * 2 * H], U8, "wa_raw")
         nc.sync.dma_start(
@@ -132,7 +133,7 @@ def tile_list_pitch_control_rescale_kernel(
         laid = ctx.enter_context(tc.tile_pool(name="laid", bufs=1))
 
         def placed(shape, dtype, name, offset):
-            return laid.tile(shape, dtype, name=name, align_bytes=64, offset=offset)
+            return laid.tile(shape, dtype, name=name, align_bytes=ALIGN, offset=offset)
 
         load_tab(1, late)
         load_wh(1, 0, wh_buffer("wh_raw10", late))
@@ -167,7 +168,7 @@ def tile_list_pitch_control_rescale_kernel(
             grouped = {}
             src = wh_raw[b, a][:].rearrange("p j (m t) -> p m j t", t=PACK)
             for t in range(0, PACK, 2):
-                grouped[t] = ring.tile([P, 2 * PASS], BF16, name=f"wh_grouped{t}", align_bytes=64)
+                grouped[t] = ring.tile([P, 2 * PASS], BF16, name=f"wh_grouped{t}", align_bytes=ALIGN)
                 dst = grouped[t][:].rearrange("p (t m j) -> p m j t", t=2, j=PACK)
                 if t in on_scalar:
                     nc.scalar.activation(dst, src[:, :, :, t : t + 2], ACT.Copy, scale=-1.0)

@@ -32,7 +32,7 @@ BANKS = 8
 LINE = 16
 ALIGN = 256
 VECTOR_ROW = 20
-HALF_SHARE = 256
+HALF_SHARE = 208
 LAST_SHARE = 128
 LATE_SIGMOIDS = PACK * PASS * 4
 THIRD_SIGMOIDS = LATE_SIGMOIDS + (PACK + 1) * HALF * 4

from contextlib import ExitStack

import concourse.mybir as mybir
from concourse.masks import make_identity

K, H, N, T, S = 1024, 1024, 512, 2048, 1024
FLOPS = 2 * S * (2 * K * H + H * N)

F32 = mybir.dt.float32
BF16 = mybir.dt.bfloat16
I32 = mybir.dt.int32
U32 = mybir.dt.uint32
U16 = mybir.dt.uint16
U8 = mybir.dt.uint8
FP8X4 = mybir.dt.float8_e4m3fn_x4
FP4X4 = mybir.dt.float4_e2m1fn_x4
ACT = mybir.ActivationFunctionType
MULT = mybir.AluOpType.mult

P = 128
PACK = 4
PASS = P * PACK
PASSES = K // PASS
QUADRANT = 32
PLANE_ROWS = PASS // 32
PER_COLUMN = 16
HALF = 512
QUARTER = 256
SECOND, THIRD, FOURTH = QUARTER, 2 * QUARTER, 3 * QUARTER
TILES = N // P
BANKS = 8
LINE = 16
ALIGN = 256
VECTOR_ROW = 20
HALF_SHARE = 208
LAST_SHARE = 128
LATE_SIGMOIDS = PACK * PASS * 4
THIRD_SIGMOIDS = LATE_SIGMOIDS + (PACK + 1) * HALF * 4
STAGED_HALF = THIRD_SIGMOIDS - 1024


def tile_list_pitch_control_rescale_kernel(
    tc, tab_words, tab_scales, offs, gT, wh, wa_words, wa_scales, lead, gain, wo_words, wo_scales, bo, out
):
    nc = tc.nc
    with ExitStack() as ctx:
        keep = ctx.enter_context(tc.tile_pool(name="keep", bufs=1))
        ring = ctx.enter_context(tc.tile_pool(name="ring", bufs=2))
        psum = ctx.enter_context(tc.psum_pool(name="psum", bufs=1))
        banks = [psum.tile([P, HALF], F32, name=f"bank{i}") for i in range(BANKS)]

        def held(shape, dtype, name, pool=keep):
            return pool.tile(shape, dtype, name=name, align_bytes=ALIGN)

        wa_raw = held([P, PASSES * 2 * H], U8, "wa_raw")
        nc.sync.dma_start(
            wa_raw[:].bitcast(I32).rearrange("p (a w) -> p a w", a=PASSES),
            wa_words.bitcast(I32).rearrange("a p w -> p a w"),
        )
        offsets = keep.tile([P, S // PER_COLUMN], U16, name="offsets")
        nc.sync.dma_start(offsets[:], offs)

        def entries(first, count):
            return offsets[:, first // PER_COLUMN : (first + count) // PER_COLUMN]

        def zeroed(engine, width, name, pool=keep):
            rows = held([P, width], U8, name, pool)
            engine.memset(rows[:].bitcast(I32), 0)
            return rows

        tab_sb = {}
        wh_raw = {}
        map_sb = {}

        def load_tab(a, pool):
            tab_sb[a] = held([P, T], U32, f"tab_sb{a}", pool)
            nc.sync.dma_start(tab_sb[a][:].bitcast(I32), tab_words[a].rearrange("p t i -> p (t i)").bitcast(I32))

        def load_wh(b, a, raw):
            wh_raw[b, a] = raw
            rows = wh[a * PASS : (a + 1) * PASS, b * PASS : (b + 1) * PASS]
            nc.sync.dma_start(raw[:], rows.rearrange("(p j) c -> p j c", j=PACK))

        def wh_buffer(name, pool):
            return held([P, PACK, PASS], F32, name, pool)

        def load_map(u, pool, name):
            map_sb[u] = held([P, T], F32, name, pool)
            nc.sync.dma_start(map_sb[u][:], gT[u * P : (u + 1) * P, :])

        def load_vector(vector, row):
            nc.sync.dma_start(vector_rows[row : P : 2 * QUADRANT, :], vector.rearrange("(b r) -> b r", b=PASSES))

        def load_planes(rows, scales, row0=0):
            for r in range(PACK):
                nc.sync.dma_start(
                    rows[row0 + r : P : QUADRANT, :].bitcast(I32).rearrange("q (a w) -> q a w", a=PASSES),
                    scales[:, r:PLANE_ROWS:PACK, :].bitcast(I32).rearrange("a q w -> q a w"),
                )

        def reorder_columns(copy, dst, src, run):
            copy(
                dst.rearrange("p (g t n m) -> p g n t m", t=PACK, n=P // run, m=run),
                src.rearrange("p (g n m t) -> p g n t m", t=PACK, n=P // run, m=run),
            )

        v_plane = [held([P, S], U8, "v_plane0")]
        with tc.tile_pool(name="early", bufs=1) as early:
            tab_rows = zeroed(nc.gpsimd, T, "tab_rows", early)
            wa_rows = zeroed(nc.vector, PASSES * H, "wa_rows")
            v_plane.append(zeroed(nc.gpsimd, S, "v_plane1"))
            for r in range(PACK):
                nc.sync.dma_start(
                    tab_rows[r:P:QUADRANT, :].bitcast(I32), tab_scales[0, r:PLANE_ROWS:PACK, :].bitcast(I32)
                )
            nc.sync.dma_start(tab_rows[PACK : PACK + PLANE_ROWS, :].bitcast(I32), tab_scales[1].bitcast(I32))
            load_tab(0, keep)
            load_planes(wa_rows, wa_scales)
            vector_rows = held([P, PASS], F32, "vector_rows")
            nc.vector.memset(vector_rows[:], 0.0)
            load_vector(lead, VECTOR_ROW)
            load_vector(gain, VECTOR_ROW + 1)
            load_wh(0, 0, wh_buffer("wh_raw00", keep))
            load_wh(0, 1, wh_buffer("wh_raw01", keep))
            nc.vector.tensor_copy(v_plane[0][:], tab_rows[:].indirect(offsets[:]))
        for q in range(P // QUADRANT):
            nc.sync.dma_start(
                v_plane[1][q * QUADRANT : q * QUADRANT + PACK, :].bitcast(I32),
                v_plane[0][PACK * (q + 1) : PACK * (q + 2), :].bitcast(I32),
            )

        late = ctx.enter_context(tc.tile_pool(name="late", bufs=1))
        laid = ctx.enter_context(tc.tile_pool(name="laid", bufs=1))

        def placed(shape, dtype, name, offset):
            return laid.tile(shape, dtype, name=name, align_bytes=ALIGN, offset=offset)

        load_tab(1, late)
        load_wh(1, 0, wh_buffer("wh_raw10", late))
        load_wh(1, 1, placed([P, PACK, PASS], F32, "wh_last", 0))
        load_map(0, late, "map_sb0")
        for u in range(1, TILES - 1):
            load_map(u, late, f"map_sb{u}")

        identity = held([P, P], F32, "identity")
        make_identity(nc, identity[:])
        for t in range(PACK):
            nc.tensor.transpose(banks[BANKS - 1][:, t * P : (t + 1) * P], vector_rows[:, t:PASS:PACK], identity[:])
        vectors = held([P, 2, PASSES, PACK], F32, "vectors")
        turned = banks[BANKS - 1][:].rearrange("p (t b row) -> p row b t", t=PACK, b=PASSES)
        nc.scalar.copy(vectors[:], turned[:, VECTOR_ROW : VECTOR_ROW + 2, :, :])
        lead_sb = [vectors[:, 0, b, :] for b in range(PASSES)]
        gain_sb = [vectors[:, 1, b, :] for b in range(PASSES)]

        v_codes = {}

        def gather_words(a, first, count, piece):
            words = held([P, count], U32, f"v_codes{a}{first}")
            for e in range(0, count, piece):
                nc.vector.tensor_copy(words[:, e : e + piece], tab_sb[a][:].indirect(entries(first + e, piece)))
            for e in range(0, count, QUARTER):
                v_codes[a, first + e] = words[:, e:]

        wh_codes = {}
        wh_planes = {}

        def quantize_wh(b, a, on_scalar):
            grouped = {}
            src = wh_raw[b, a][:].rearrange("p j (m t) -> p m j t", t=PACK)
            for t in range(0, PACK, 2):
                grouped[t] = ring.tile([P, 2 * PASS], BF16, name=f"wh_grouped{t}", align_bytes=ALIGN)
                dst = grouped[t][:].rearrange("p (t m j) -> p m j t", t=2, j=PACK)
                if t in on_scalar:
                    nc.scalar.activation(dst, src[:, :, :, t : t + 2], ACT.Copy, scale=-1.0)
                else:
                    nc.vector.tensor_scalar_mul(dst, src[:, :, :, t : t + 2], -1.0)
            wh_codes[b, a] = held([P, PASS], U32, f"wh_codes{b}{a}")
            wh_planes[b, a] = held([P, PASS], U8, f"wh_planes{b}{a}")
            for t in range(0, PACK, 2):
                cols = slice(t * P, (t + 2) * P)
                nc.vector.quantize_mx(
                    wh_codes[b, a][:, cols].bitcast(FP8X4),
                    wh_planes[b, a][:, cols],
                    grouped[t][:],
                )

        picked = [held([P, S], F32, f"picked{u}") for u in range(TILES)]

        def pick(u):
            nc.vector.tensor_copy(picked[u][:], map_sb[u][:].indirect(offsets[:]))

        wa_codes = held([P, PASSES * 2 * H], U8, "wa_codes")
        reorder_columns(nc.scalar.copy, wa_codes[:].bitcast(U16), wa_raw[:].bitcast(U16), LINE // 2)
        gather_words(0, 0, S, S)
        wa_planes = held([P, PASSES * H], U8, "wa_planes")
        reorder_columns(nc.vector.tensor_copy, wa_planes[:], wa_rows[:], LINE)
        quantize_wh(0, 0, (0, 2))
        quantize_wh(0, 1, (2,))
        gather_words(1, 0, HALF, QUARTER)
        gather_words(1, HALF, HALF, HALF)
        quantize_wh(1, 0, ())
        quantize_wh(1, 1, ())

        load_planes(wa_rows[:, : PASSES * N], wo_scales, PACK)
        load_map(TILES - 1, keep, "wh_raw00")
        wo_planes = wa_rows[PACK:P, : PASSES * N]
        wo_sb = held([P, PASSES * N], U32, "wh_raw01")
        nc.sync.dma_start(
            wo_sb[:].bitcast(I32).rearrange("p (b c) -> p b c", b=PASSES),
            wo_words.rearrange("b p c i -> p b (c i)").bitcast(I32),
        )
        bo_sb = held([P, TILES], F32, "bo_sb", late)
        with nc.allow_non_contiguous_dma("one bias value for each partition"):
            nc.sync.dma_start(bo_sb[:], bo.rearrange("(u p) -> p u", p=P))

        def sums(b, first, width, bank0, order, column=0):
            for t in range(PACK):
                for i, (side, a) in enumerate(order):
                    if side == "home":
                        cols = slice(t * P, (t + 1) * P)
                        weights = wh_codes[b, a][:, cols].bitcast(FP8X4)
                        weight_plane = wh_planes[b, a][:, cols]
                    else:
                        col = a * H + b * PASS + t * P
                        weights = wa_codes[:, 2 * col : 2 * (col + P)].bitcast(FP4X4)
                        weight_plane = wa_planes[:, col : col + P]
                    nc.tensor.matmul_mx(
                        banks[bank0 + t][:, column : column + width],
                        lhsT=weights,
                        lhsT_scale=weight_plane,
                        rhs=v_codes[a, first][:, :width].bitcast(FP8X4),
                        rhs_scale=v_plane[a][:, first : first + width],
                        start=(i == 0),
                        stop=(i == len(order) - 1),
                    )

        def sigmoids(b, bank0, column, sig):
            for t in range(PACK):
                nc.scalar.activation(
                    sig[:, t, :],
                    banks[bank0 + t][:, column : column + sig.shape[2]],
                    ACT.Sigmoid,
                    bias=lead_sb[b][:, t : t + 1],
                )
            return sig

        def gains(b, sig, scaled):
            for t in range(PACK):
                nc.scalar.activation(scaled[:, t, :], sig[:, t, :], ACT.Copy, scale=gain_sb[b][:, t : t + 1])

        def interleave(scaled, values):
            nc.scalar.copy(
                values.rearrange("p (e i t) -> p e t i", i=4, t=PACK),
                scaled.rearrange("p t (e i) -> p e t i", i=4),
            )

        def scale_on_gpsimd(b, sig, values):
            nc.gpsimd.tensor_tensor(
                values.rearrange("p (e t) -> p e t", t=PACK),
                sig.rearrange("p t e -> p e t"),
                gain_sb[b].unsqueeze(1).to_broadcast([P, sig.shape[2], PACK]),
                MULT,
            )

        h_codes = {}
        h_planes = {}

        def quantize_h(keys, values, codes, scales):
            width = codes.shape[1] // len(keys)
            for i, key in enumerate(keys):
                h_codes[key] = codes[:, i * width : (i + 1) * width]
                h_planes[key] = scales[:, i * width : (i + 1) * width]
            nc.vector.quantize_mx(codes.bitcast(FP8X4), scales, values)

        def product(u, keys, y):
            for i, (b, first) in enumerate(keys):
                cols = slice(b * N + u * P, b * N + (u + 1) * P)
                column = first - keys[0][1]
                nc.tensor.matmul_mx(
                    y[:, column : column + h_codes[b, first].shape[1]],
                    lhsT=wo_sb[:, cols].bitcast(FP8X4),
                    lhsT_scale=wo_planes[:, cols],
                    rhs=h_codes[b, first].bitcast(FP8X4),
                    rhs_scale=h_planes[b, first],
                    start=(i == 0),
                    stop=(i == len(keys) - 1),
                )

        def update(u, first, y, factor):
            count = factor.shape[1]
            nc.scalar.activation(factor, y, ACT.Identity, bias=bo_sb[:, u : u + 1])
            window = map_sb[u][:].indirect(entries(first, count))
            nc.vector.tensor_tensor(window, picked[u][:, first : first + count], factor, MULT)

        def floats(width, name):
            return held([P, width], F32, name)[:]

        def by_slice(ap):
            return ap.rearrange("p (t e) -> p t e", t=PACK)

        def sigmoid_buffer(width, name):
            return held([P, PACK, width], F32, name)[:]

        def h_values(width, name):
            return held([P, PACK * width], BF16, name)[:]

        def words(width, name):
            return held([P, width], U32, name)[:]

        def plane(width, name):
            return held([P, width], U8, name)[:]

        low, high = 0, PACK
        as_loaded = (("away", 0), ("home", 0), ("away", 1), ("home", 1))
        away_first = (("away", 0), ("away", 1), ("home", 0), ("home", 1))
        last_first = as_loaded[::-1]
        first_half = ((1, 0), (0, 0), (0, SECOND))
        last_tile = TILES - 1

        sums(0, 0, QUARTER, low, as_loaded)
        values = h_values(QUARTER, "values_quarter")
        scaled = by_slice(floats(HALF, "staged_first").bitcast(BF16))
        sig = sigmoids(0, low, 0, sigmoid_buffer(QUARTER, "sig_quarter"))
        sums(0, SECOND, QUARTER, low, as_loaded, SECOND)
        gains(0, sig, scaled)
        interleave(scaled, values)
        quantize_h(((0, 0),), values, placed([P, QUARTER], U32, "h_codes00", 0)[:], plane(QUARTER, "h_planes00"))
        pick(0)
        pick(1)

        values_second = h_values(QUARTER, "values_quarter")
        scale_on_gpsimd(0, sigmoids(0, low, SECOND, sigmoid_buffer(QUARTER, "sig_quarter")), values_second)

        sums(1, 0, HALF, high, away_first)
        values = h_values(HALF, "values_half")
        rest = HALF - HALF_SHARE
        scale_on_gpsimd(1, sigmoids(1, high, rest, sigmoid_buffer(HALF_SHARE, "sig_share")), values[:, PACK * rest :])
        sig = sigmoids(1, high, 0, sigmoid_buffer(rest, "sig_rest"))
        scaled = by_slice(placed([P, 2 * rest], F32, "staged_half", STAGED_HALF)[:].bitcast(BF16))
        gains(1, sig, scaled)
        interleave(scaled, values[:, : PACK * rest])
        sums(0, THIRD, QUARTER, high, as_loaded)
        sums(1, HALF, HALF, low, last_first)
        sig_third = sigmoids(0, high, 0, placed([P, PACK, QUARTER], F32, "sig_third", THIRD_SIGMOIDS)[:])
        pick(2)
        quantize_h(((0, SECOND),), values_second, words(QUARTER, "h_codes01"), wa_rows[:, :QUARTER])
        quantize_h(((1, 0),), values, words(HALF, "h_codes10"), wa_rows[:, N : N + HALF])
        pick(last_tile)
        values_third = h_values(HALF, "values_half")
        scale_on_gpsimd(0, sig_third[:, :, :LAST_SHARE], values_third[:, : PACK * LAST_SHARE])

        for u in range(last_tile):
            product(u, first_half, banks[high + u][:])
        factors = floats(last_tile * HALF, "factors")
        for u in range(last_tile):
            update(u, 0, banks[high + u][:], factors[:, u * HALF : (u + 1) * HALF])

        late_sigmoids = placed([P, (PACK + 1) * HALF], F32, "late_sigmoids", LATE_SIGMOIDS)[:]

        def wide_sigmoid(t, sig_t):
            nc.scalar.activation(sig_t, banks[low + t][:], ACT.Sigmoid, bias=lead_sb[1][:, t : t + 1])
            return sig_t

        sig_wide = [wide_sigmoid(t, late_sigmoids[:, t * HALF : (t + 1) * HALF]) for t in range(PACK - 1)]
        product(last_tile, first_half, banks[low][:])
        sig_wide.append(wide_sigmoid(PACK - 1, floats(HALF, "h_codes10")))

        staged = floats(PACK * HALF, "h_codes01")
        by_quarter = staged.bitcast(BF16).rearrange("p (c t e) -> p c t e", c=2, t=PACK)
        scaled_third = by_quarter[:, 0, :, LAST_SHARE:]
        scaled_fourth = by_quarter[:, 1]
        runs = staged.bitcast(BF16).rearrange("p (n e) -> p n e", e=QUARTER)
        gains(0, sig_third[:, :, LAST_SHARE:], scaled_third[:, :, : QUARTER - LAST_SHARE])
        for t in range(PACK):
            nc.scalar.activation(
                runs[:, 2 * t + 1 : 2 * t + 2 * PACK + 1 : 2 * PACK - 1, :],
                sig_wide[t].rearrange("p (c e) -> p c e", c=2),
                ACT.Copy,
                scale=gain_sb[1][:, t : t + 1],
            )
        interleave(scaled_third, values_third[:, PACK * LAST_SHARE :])
        quantize_h(((0, THIRD), (1, THIRD)), values_third, words(HALF, "h_codes2"), plane(HALF, "h_planes2"))
        update(last_tile, 0, banks[low][:], staged[:, :HALF])

        sums(0, FOURTH, QUARTER, high, as_loaded)
        for u in range(TILES):
            product(u, ((1, THIRD), (0, THIRD)), banks[low + u][:, :QUARTER])
        sig = sigmoids(0, high, 0, by_slice(late_sigmoids[:, (PACK - 1) * HALF :]))
        gains(0, sig, scaled_fourth[:, :, QUARTER:])
        values = h_values(HALF, "values_fourth")
        interleave(scaled_fourth, values)
        quantize_h(((1, FOURTH), (0, FOURTH)), values, words(HALF, "h_codes3"), plane(HALF, "h_planes3"))

        fourth = ((1, FOURTH), (0, FOURTH))
        for u in range(2):
            at = 2 * HALF + u * QUARTER
            update(u, THIRD, banks[low + u][:, :QUARTER], staged[:, at : at + QUARTER])
        narrow = floats(2 * QUARTER, "narrow_factors")
        for u in range(2):
            product(u, fourth, banks[high + u][:, :QUARTER])
            update(u, FOURTH, banks[high + u][:, :QUARTER], narrow[:, u * QUARTER : (u + 1) * QUARTER])
        wide = floats(2 * HALF, "wide_factors")
        for u in range(2, TILES):
            product(u, fourth, banks[low + u][:, QUARTER:])
            update(u, THIRD, banks[low + u][:], wide[:, (u - 2) * HALF : (u - 1) * HALF])

        for u in range(TILES):
            nc.sync.dma_start(out[u * P : (u + 1) * P, :], map_sb[u][:])
